import numpy as np, ml_dtypes
CORES = [16,17,18,19,32,33,34,35]
N = 8
import mx_ref
BF = ml_dtypes.bfloat16
def cols(t, e):
    v = np.concatenate([t.reshape(128, -1, 4), np.zeros((128, 1, 4), BF)], axis=1)
    return np.ascontiguousarray(v[:, e]).reshape(128, -1)
def decode(q):
    o = []
    for b in range(4):
        e = np.zeros((128, 128, 4), np.float32); e[np.arange(128), np.arange(128), b] = 1
        o.append(mx_ref.matmul(mx_ref.quantize(e.reshape(128, 512).astype(BF)), q))
    return np.stack(o, axis=2).reshape(128, -1)
def f(rng, *shape):
    return mx_ref.flush((rng.standard_normal(shape, dtype=np.float32) * np.exp2(rng.integers(-2, 3, shape[:-1] + (1,)))).astype(BF))
def wide(rng, *shape, cols=0):
    v = rng.standard_normal(shape, dtype=np.float32) * np.exp2(rng.integers(-12, 13, shape)).astype(np.float32)
    if cols: v *= np.repeat(np.exp2(rng.integers(-cols, cols + 1, shape[:-2] + (1, shape[-1] // 4))) * (rng.random(shape[:-2] + (1, shape[-1] // 4)) > 0.0625), 4, axis=-1).astype(np.float32)
    return mx_ref.flush(v.astype(BF))
T, K = 512, 64
def setup_inputs(rng):
    u = np.zeros((N, 128, 512), BF); u[:, :, :4] = f(rng, N, 128, 4)
    return {"gr": f(rng, N, 128, 4 * T), "u": u}
def raised(rng, chosen):
    d = setup_inputs(rng)
    for r in range(N):
        g = d["gr"][r].astype(np.float32).reshape(128, T, 4)
        sign = np.where(d["u"][r][:, :4].astype(np.float32) < 0, -1, 1).reshape(128, 1, 4) * rng.choice([-1, 1], K).reshape(1, K, 1)
        v = g * np.float32(2.0 ** -8)
        v[:, chosen[r]] = np.abs(g[:, chosen[r]]) * sign
        d["gr"][r] = mx_ref.flush(v.reshape(128, 4 * T).astype(BF))
    return d
def setup_inputs_same(rng):
    d = raised(rng, [rng.permutation(T)[:K]] * N)
    k = rng.permutation(np.concatenate([[12, -12, -11], rng.integers(-12, 13, N - 3)]))
    d["gr"] = mx_ref.flush((d["gr"].astype(np.float32) * np.exp2(k).astype(np.float32).reshape(N, 1, 1)).astype(BF))
    return d
def setup_inputs_apart(rng):
    p = rng.permutation(T)
    return raised(rng, [p[(r * K + np.arange(K)) % T] for r in range(N)])
def setup_inputs_ties(rng):
    d = setup_inputs(rng); n = T // 11
    for r in range(N):
        p = rng.permutation(T)[:11 * n]
        e = np.full(T, -1); e[p] = np.repeat(np.arange(n), 11)
        s = rng.choice([-1, 1], (n, 11)); s[:, 0] = 1; s[:, 1] = -1
        sign = np.ones(T, np.float32); sign[p] = s.reshape(-1)
        d["gr"][r] = (cols(d["gr"][r], e).astype(np.float32).reshape(128, T, 4) * sign.reshape(1, T, 1)).reshape(128, 4 * T).astype(BF)
    return d
def setup_inputs_few(rng):
    d = setup_inputs(rng); p = rng.permutation(N)
    d["u"][p[0]] = 0
    sign = rng.choice([-1, 1], (128, 1, 4))
    d["u"][p[1]][:, :4] = (sign * rng.uniform(1, 4, (128, 1, 4)) * 2.0 ** 28).reshape(128, 4).astype(BF)
    d["gr"][p[1]] = (sign * rng.choice([-1, 1], (1, T, 1)) * rng.uniform(1, 4, (128, T, 4)) * 2.0 ** 28).reshape(128, 4 * T).astype(BF)
    for r in p[2:2 + N // 2]:
        k = rng.permutation(T)[:rng.integers(1, K)]
        e = np.full(T, -1); e[k] = k
        d["gr"][r] = cols(d["gr"][r], e)
    return d
def setup_inputs_spread(rng):
    d = setup_inputs(rng); d["gr"] = wide(rng, N, 128, 4 * T, cols=8); return d
def check_inputs(d):
    return ["u"] if (d["u"][:, :, 4:].astype(np.float32) != 0).any() else []
def reference(gr, u):
    acc = np.zeros((128, T, 4), np.float32); nb = np.zeros((N, K), np.float32); sc = np.zeros((N, 1, K), np.float32)
    er = gr.astype(np.float32).reshape(N, 128, T, 4)
    for s in range(N):
        score = np.abs(mx_ref.matmul(mx_ref.quantize(u[s]), mx_ref.quantize(gr[s]))[0]) + np.float32(0.0)
        e = np.argsort(-score, kind="stable")[:K]
        v = decode(mx_ref.quantize(cols(gr[s], e))).reshape(128, K, 4)
        acc[:, e] = acc[:, e] + v
        er[s][:, e] = er[s][:, e] - v
        nb[s] = e
        sc[s, 0] = score[e]
    return {"acc": np.stack([acc.reshape(128, 4 * T)] * N), "er": er.reshape(N, 128, 4 * T), "nb": np.stack([nb] * N), "sc": sc}

@@ -1,0 +1,341 @@
+from concourse.bass import DstId, RemoteDMATransfer
+from concourse.mybir import dt, AluOpType, AxisListType, ActivationFunctionType
+
+A = AluOpType
+F = ActivationFunctionType
+AX = AxisListType.X
+STEP = 4096.0
+DROP = 1048576.0
+
+SCRATCH = {
+    "grt": ("sbuf", [128, 2048], "bfloat16"),
+    "uc": ("sbuf", [128, 16], "bfloat16"),
+    "ut": ("sbuf", [128, 512], "bfloat16"),
+    "uq": ("sbuf", [128, 128], "float8_e4m3fn_x4"),
+    "us": ("sbuf", [128, 128], "uint8"),
+    "gq": ("sbuf", [128, 512], "float8_e4m3fn_x4"),
+    "gs": ("sbuf", [128, 512], "uint8"),
+    "ones": ("sbuf", [128, 128], "bfloat16"),
+    "ident": ("sbuf", [128, 128], "bfloat16"),
+    "et": ("sbuf", [128, 2048], "bfloat16"),
+    "eq": ("sbuf", [128, 512], "float8_e4m3fn_x4"),
+    "es": ("sbuf", [128, 512], "uint8"),
+    "pi": ("sbuf", [128, 32], "int32"),
+    "p3": ("sbuf", [128, 32], "int32"),
+    "ic": ("sbuf", [128, 4], "int32"),
+    "fc": ("sbuf", [128, 4], "float32"),
+    "uoff": ("sbuf", [128, 32], "uint16"),
+    "j0": ("sbuf", [128, 64], "float32"),
+    "jt": ("sbuf", [128, 64], "float32"),
+    "m0": ("sbuf", [128, 64], "float32"),
+    "md": ("sbuf", [128, 64], "float32"),
+    "n0": ("sbuf", [128, 512], "float32"),
+    "n1": ("sbuf", [128, 512], "float32"),
+    "stp": ("sbuf", [128, 512], "float32"),
+    "cor": ("sbuf", [128, 1], "float32"),
+    "sl0": ("sbuf", [128, 512], "float32"),
+    "slot": ("sbuf", [128, 512], "float32"),
+    "pt": ("sbuf", [128, 512], "float32"),
+    "pv": ("sbuf", [128, 512], "float32"),
+    "pts": ("sbuf", [128, 512], "float32"),
+    "pvs": ("sbuf", [128, 448], "float32"),
+    "sabs": ("sbuf", [128, 512], "float32"),
+    "scol": ("sbuf", [128, 4], "float32"),
+    "eqt": ("sbuf", [128, 512], "float32"),
+    "eqm": ("sbuf", [128, 512], "float32"),
+    "cmp": ("sbuf", [128, 2048], "float32"),
+    "cnt": ("sbuf", [128, 8], "float32"),
+    "eqc": ("sbuf", [128, 4], "float32"),
+    "ru": ("sbuf", [128, 4], "uint16"),
+    "w": ("sbuf", [128, 512], "float32"),
+    "t1": ("sbuf", [128, 64], "float32"),
+    "xp": ("sbuf", [128, 64], "float32"),
+    "yr": ("sbuf", [128, 64], "float32"),
+    "bb": ("sbuf", [128, 256], "float32"),
+    "bm": ("sbuf", [128, 256], "float32"),
+    "lf": ("sbuf", [128, 32], "float32"),
+    "lx": ("sbuf", [128, 32], "uint16"),
+    "lown": ("sbuf", [128, 4], "uint16"),
+    "ou": ("sbuf", [128, 16], "uint16"),
+    "h": ("sbuf", [128, 512], "bfloat16"),
+    "hq": ("sbuf", [128, 128], "float8_e4m3fn_x4"),
+    "hs": ("sbuf", [128, 128], "uint8"),
+    "ql": ("sbuf", [128, 192], "float8_e4m3fn_x4"),
+    "pl": ("sbuf", [128, 192], "uint8"),
+    "qr": ("sbuf", [128, 256], "float8_e4m3fn_x4"),
+    "pr": ("sbuf", [128, 256], "uint8"),
+    "e32": ("sbuf", [128, 2048], "float32"),
+    "d": ("sbuf", [128, 256], "float32"),
+    "scg": ("sbuf", [128, 64], "float32"),
+    "scp": ("sbuf", [128, 64], "float32"),
+    "x": ("sbuf", [128, 2056], "float32"),
+    "offc": ("sbuf", [128, 112], "uint16"),
+    "offf": ("sbuf", [128, 128], "uint16"),
+    "ac": ("sbuf", [128, 2048], "float32"),
+    "ps": ("psum", [128, 4096], "float32"),
+}
+SEMAPHORES = ["qv", "qs", "qt", "qp", "lu", "l0", "l1", "st", "ll", "lr", "cl", "cr", "loc"]
+
+
+def rank_program(g, core, T, topo):
+    rank = T.rank_of(core)
+    if rank is None:
+        return
+    N = len(T.cores)
+    near = [r for r in range(N) if topo.chip(T.cores[r]) == topo.chip(core)]
+    far = [r for r in range(N) if r not in near]
+    near_others = [r for r in near if r != rank]
+
+    queue = {"v": g.vector, "s": g.scalar, "t": g.tensor, "p": g, "y": g.sync}
+    count = {"v": 0, "s": 0, "t": 0, "p": 0, "st": 0}
+    seen = {}
+
+    def need(e, deps):
+        top = {}
+        for sem, val in deps:
+            top[sem] = max(val, top.get(sem, 0))
+        for sem in top:
+            if seen.get((e, sem), 0) < top[sem]:
+                queue[e].wait_ge(T.sem[sem], top[sem])
+                seen[(e, sem)] = top[sem]
+
+    def op(e, deps, call):
+        need(e, deps)
+        count[e] += 1
+        call().then_inc(T.sem["q" + e], 1)
+        return ("q" + e, count[e])
+
+    def load(e, out, in_, sem):
+        queue[e].dma_start(out, in_).then_inc(T.sem[sem], 16)
+        return (sem, 16)
+
+    def store(e, deps, out, in_):
+        need(e, deps)
+        queue[e].dma_start(out, in_).then_inc(T.sem["st"], 16)
+        count["st"] += 16
+
+    V, S = g.vector, g.scalar
+
+    def bank(b, n):
+        return T.ps[:, 512 * b:512 * b + n]
+
+    def vs(deps, out, in0, s1, op0, s2=None, op1=None):
+        if op1 is None:
+            return op("v", deps, lambda: V.tensor_scalar(out=out, in0=in0, scalar1=s1, scalar2=None, op0=op0))
+        return op("v", deps, lambda: V.tensor_scalar(out=out, in0=in0, scalar1=s1, scalar2=s2, op0=op0, op1=op1))
+
+    lu = load("y", T.uc[:, 0:16], T.u[:, 0:16], "lu")
+    l0 = load("y", T.grt[:, 0:1024], T.gr[:, 0:1024], "l0")
+    l1 = load("y", T.grt[:, 1024:2048], T.gr[:, 1024:2048], "l1")
+
+    def whole(out, pattern, base=0):
+        return op("p", [], lambda: g.iota(out, pattern, base, 0, allow_small_or_imprecise_dtypes=True))
+    k_pi = op("p", [], lambda: g.iota(T.pi[:, 0:32], [[0, 32]], 0, 1))
+    k_ones = op("v", [], lambda: V.memset(T.ones[:, :], 1.0))
+    k_id = op("p", [k_ones], lambda: g.affine_select(T.ident[:, :], T.ones[:, :], [[-1, 128]], A.is_equal, 0.0, 0, 1))
+    k_j0 = whole(T.j0[:, :], [[128, 4], [1, 16]])
+    k_m0 = whole(T.m0[:, :], [[1, 16], [0, 4]])
+    k_sl0 = whole(T.sl0[:, :], [[4, 512]], 8)
+    k_n0 = whole(T.n0[:, :], [[0, 128], [4, 4]])
+
+    k_p3 = vs([k_pi], T.p3[:, :], T.pi[:, :], 3, A.bitwise_and)
+    for i, bits in ((0, 3), (1, 12), (2, 112), (3, 15)):
+        k_ic = vs([k_pi], T.ic[:, i:i + 1], T.pi[:, 0:1], bits, A.bitwise_and)
+    k_uoff = op("v", [k_p3], lambda: V.tensor_copy(T.uoff[:, :], T.p3[:, :]))
+    k_fc = op("v", [k_ic], lambda: V.tensor_copy(T.fc[:, :], T.ic[:, :]))
+    k_et = op("v", [], lambda: V.memset(T.et[:, :], 0.0))
+    k_e = [op("s", [k_id, k_et], lambda: S.activation(T.et[:, 512 * b + b:512 * (b + 1):4], T.ident[:, :], F.Copy)) for b in range(4)]
+    k_slot = op("s", [k_sl0, k_fc], lambda: S.activation(T.slot[:, :], T.sl0[:, :], F.Identity, bias=T.fc[:, 0:1]))
+    k_pt = op("s", [k_sl0, k_fc], lambda: S.activation(T.pt[:, :], T.sl0[:, :], F.Identity, bias=T.fc[:, 0:1], scale=0.0))
+
+    k_ut = op("v", [lu, k_uoff], lambda: V.tensor_copy(T.ut[:, :], T.uc[:, 0:16].indirect(T.uoff[:, 0:32])))
+    k_uq = op("v", [k_ut], lambda: V.quantize_mx(T.uq[:, 0:128], T.us[:, 0:128], T.ut[:, 0:512]))
+
+    def pack(a, ld):
+        return op("v", [ld], lambda: V.quantize_mx(T.gq[:, a:a + 256], T.gs[:, a:a + 256], T.grt[:, 4 * a:4 * a + 1024]))
+    k_g = [pack(0, l0)]
+    k_w = op("v", [], lambda: V.memset(T.w[:, 0:64], 0.0))
+    k_xp = op("v", [], lambda: V.memset(T.xp[:, :], 0.0))
+    k_jt = vs([k_j0, k_fc], T.jt[:, :], T.j0[:, :], T.fc[:, 2:3], A.add)
+    k_md = vs([k_m0, k_fc], T.md[:, :], T.m0[:, :], T.fc[:, 3:4], A.is_equal)
+    k_g.append(pack(256, l1))
+    k_c0 = op("s", [l0], lambda: S.activation(T.e32[:, 0:512], T.grt[:, 0:512], F.Copy))
+    k_abs, k_sc = [], []
+    for i, b in ((0, 0), (1, 5)):
+        a = 256 * i
+        k = op("t", [k_uq, k_g[i]], lambda: g.tensor.matmul_mx(bank(b, 256), T.uq[:, 0:128], T.us[:, 0:128], T.gq[:, a:a + 256], T.gs[:, a:a + 256], True, True))
+        k_abs.append(op("s", [k], lambda: S.activation(T.sabs[:, a:a + 256], bank(b, 256), F.Abs)))
+        for q in (2 * i, 2 * i + 1):
+            k_sc.append(op("t", [k_uq, k_g[i]], lambda: g.tensor.matmul_mx(
+                bank(1 + q, 128), T.gq[:, 128 * q:128 * q + 128], T.gs[:, 128 * q:128 * q + 128], T.uq[:, 0:128], T.us[:, 0:128], True, True)))
+
+    k_scol, k_eq, k_cnt = [], [], {}
+
+    def column_score(q):
+        k_scol.append(op("v", [k_sc[q]], lambda: V.tensor_reduce(T.scol[:, q:q + 1], bank(1 + q, 1), AX, A.max, apply_absolute_value=True)))
+
+    def equal_scores(q):
+        k_eq.append(vs([k_abs[q // 2], k_scol[q]], T.eqt[:, 128 * q:128 * q + 128], T.sabs[:, 128 * q:128 * q + 128], T.scol[:, q:q + 1], A.is_equal))
+
+    def larger_scores(q, i):
+        lo, hi = 256 * i, 256 * i + 256
+        cut = min(max(128 * q, lo), hi)
+        for a, b, how in ((lo, cut, A.is_ge), (cut, hi, A.is_gt)):
+            if a < b:
+                k = vs([k_abs[i], k_scol[q]], T.cmp[:, 512 * q + a:512 * q + b], T.sabs[:, a:b], T.scol[:, q:q + 1], how)
+        part = T.cmp[:, 512 * q + lo:512 * q + hi]
+        k_cnt[(q, i)] = op("s", [k], lambda: S.activation(part, part, F.Copy, accum_out=T.cnt[:, 4 * i + q:4 * i + q + 1]))
+    for q in (0, 1):
+        column_score(q)
+    for q in (0, 1):
+        equal_scores(q)
+    for q in (0, 1):
+        larger_scores(q, 0)
+    for q in (2, 3):
+        column_score(q)
+    for q in (2, 3):
+        equal_scores(q)
+    k_eqm = op("p", k_eq, lambda: g.affine_select(T.eqm[:, :], T.eqt[:, :], [[0, 4], [-1, 128]], A.is_gt, 0.0, 0, 1))
+    for q, i in ((0, 1), (1, 1), (2, 0), (2, 1), (3, 0), (3, 1)):
+        larger_scores(q, i)
+
+    def eq_part(q):
+        return T.eqm[:, 128 * q:128 * q + 128]
+    k_eqc = [op("v", [k_eqm], lambda: V.tensor_reduce(T.eqc[:, q:q + 1], eq_part(q), AX, A.add)) for q in range(3)]
+    k_eqc.append(op("s", [k_eqm], lambda: S.activation(eq_part(3), eq_part(3), F.Copy, accum_out=T.eqc[:, 3:4])))
+    k_ru = [vs([k_cnt[(q, 0)], k_cnt[(q, 1)], k_eqc[q]], T.ru[:, q:q + 1], T.cnt[:, q:q + 1], T.cnt[:, 4 + q:5 + q], A.add, T.eqc[:, q:q + 1], A.add) for q in range(4)]
+
+    k_c1 = op("s", [l0, l1], lambda: S.activation(T.e32[:, 512:2048], T.grt[:, 512:2048], F.Copy))
+
+    k_w1 = op("v", [k_w, k_jt] + k_ru, lambda: V.tensor_copy(T.w[:, 0:512].indirect(T.ru[:, 0:4]), T.jt[:, 0:64]))
+    k_t1 = op("v", [k_w1], lambda: V.transpose(T.t1[:, :], T.w[:, 0:64]))
+    k_x1 = op("v", [k_t1, k_xp], lambda: V.tensor_tensor(T.xp[:, 0:64:32], T.t1[:, 0:64:32], T.t1[:, 16:64:32], A.add))
+    k_y = op("v", [k_x1], lambda: V.transpose(T.yr[:, :], T.xp[:, :]))
+    k_h0 = op("v", [], lambda: V.memset(T.h[:, 256:512], 0.0))
+    k_x0 = op("v", [], lambda: V.memset(T.x[:, 0:8], 0.0))
+    k_cor = vs([k_fc], T.cor[:, :], T.fc[:, 1:2], STEP / 4, A.mult, -3 * STEP, A.add)
+    k_bm = []
+    for a in range(4):
+        k = op("p", [k_y], lambda: g.partition_broadcast(T.bb[:, 64 * a:64 * a + 64], T.yr[32 * a:32 * a + 1, 0:64], 128))
+        k_bm.append(op("v", [k, k_md], lambda: V.tensor_tensor(T.bm[:, 64 * a:64 * a + 64], T.bb[:, 64 * a:64 * a + 64], T.md[:, :], A.mult)))
+        if a == 0:
+            k_eqz = op("v", k_e, lambda: V.quantize_mx(T.eq[:, 0:512], T.es[:, 0:512], T.et[:, 0:2048]))
+    own = 4 * rank
+    k_lf = [op("v", k_bm, lambda: V.tensor_reduce(T.lf[:, own + c:own + c + 1], T.bm[:, c:256:4], AX, A.add)) for c in range(4)]
+
+    far_e = topo.engines(core, T.cores[far[0]])
+    near_e = [e for e in topo.engines(core, T.cores[near_others[0]]) if e not in far_e]
+    far_mask = sum(1 << e for e in far_e)
+    near_mask = sum(1 << e for e in near_e)
+    left = ("loc", 3 * (len(far_e) + len(near_e)))
+
+    def ids(ranks):
+        return [DstId(rid=topo.addr(T.cores[r])[0], pnc=topo.addr(T.cores[r])[1]) for r in ranks]
+
+    def near_at(r):
+        return [q for q in near if q != r].index(rank)
+
+    def send(deps, src, near_dst, far_dst, near_sem, far_sem):
+        need("p", deps)
+        g.remote_dma_fused([
+            RemoteDMATransfer(dst_ids=ids(far), dma_engine_mask=far_mask, remote_sem=T.sem[far_sem], srcs=[src], dsts=[far_dst(r) for r in far]),
+            RemoteDMATransfer(dst_ids=ids(near_others), dma_engine_mask=near_mask, remote_sem=T.sem[near_sem], srcs=[src], dsts=[near_dst(r) for r in near_others]),
+        ], local_sem=T.sem["loc"])
+
+    send(k_lf, T.lf[:, own:own + 4], lambda r: T.lf[:, own:own + 4], lambda r: T.lf[:, own:own + 4], "ll", "lr")
+    ll = ("ll", len(near_others) * len(near_e))
+    lr = ("lr", len(far) * len(far_e))
+
+    k_ou = {t: vs(k_lf, T.ou[:, 4 * t:4 * t + 4], T.lf[:, own:own + 4], 4.0, A.mult, float(t), A.add) for t in (2, 0, 3, 1)}
+    k_h = []
+    for t in (2, 3):
+        k_h.append(op("s", [k_ou[t], l0, l1], lambda: S.activation(T.h[:, t:256:4], T.grt[:, 0:2048].indirect(T.ou[:, 4 * t:4 * t + 4]), F.Copy)))
+    for t in (0, 1):
+        k_h.append(op("v", [k_ou[t], l0, l1], lambda: V.tensor_copy(T.h[:, t:256:4], T.grt[:, 0:2048].indirect(T.ou[:, 4 * t:4 * t + 4]))))
+    k_hq = op("v", k_h + [k_h0], lambda: V.quantize_mx(T.hq[:, 0:128], T.hs[:, 0:128], T.h[:, 0:512]))
+
+    fa = 64 * near.index(rank)
+    send([k_hq], T.hq[:, 0:64].bitcast(dt.uint8),
+         lambda r: T.ql[:, 64 * near_at(r):64 * near_at(r) + 64].bitcast(dt.uint8),
+         lambda r: T.qr[:, fa:fa + 64].bitcast(dt.uint8), "cl", "cr")
+    send([k_hq], T.hs[:, 0:64],
+         lambda r: T.pl[:, 64 * near_at(r):64 * near_at(r) + 64],
+         lambda r: T.pr[:, fa:fa + 64], "cl", "cr")
+    cl = ("cl", 2 * len(near_others) * len(near_e))
+    cr = ("cr", 2 * len(far) * len(far_e))
+
+    def unpack(b, to, q, s, a, n, deps):
+        return op("t", deps + [k_eqz], lambda: g.tensor.matmul_mx(bank(to, n), T.eq[:, 128 * b:128 * b + 128], T.es[:, 128 * b:128 * b + 128], q[:, a:a + n], s[:, a:a + n], True, True))
+
+    def xs(r, b, n):
+        return T.x[:, 8 + 256 * r + b:8 + 256 * (r + n):4]
+    k_own = [unpack(b, 4 + b, T.hq, T.hs, 0, 128, [k_hq] + k_scol + k_abs) for b in range(4)]
+    k_xo = [op("s", [k_own[b]], lambda: S.activation(xs(rank, b, 1), bank(4 + b, 64), F.Copy)) for b in range(4)]
+    k_lown = op("v", k_lf, lambda: V.tensor_copy(T.lown[:, :], T.lf[:, own:own + 4]))
+    k_n1 = vs([k_n0, k_fc], T.n1[:, :], T.n0[:, :], T.fc[:, 1:2], A.is_equal, -(DROP + STEP), A.mult)
+    k_d = [op("v", [k_xo[b]] + k_h, lambda: V.tensor_tensor(T.d[:, 64 * b:64 * b + 64], T.h[:, b:256:4], xs(rank, b, 1), A.subtract)) for b in range(4)]
+    k_er = op("v", k_d + [k_c0, k_c1] + [k_ou[t] for t in range(4)], lambda: V.tensor_copy(T.e32[:, 0:2048].indirect(T.ou[:, 0:16]), T.d[:, 0:256]))
+
+    k_scg = op("s", [k_lown] + k_abs, lambda: S.activation(T.scg[:, :], T.sabs[:, 0:512].indirect(T.lown[:, 0:4]), F.Copy))
+    k_scp = [op("s", [k_scg], lambda: S.activation(T.scp[0:1, c:64:4], T.scg[0:1, 16 * c:16 * c + 16], F.Copy)) for c in range(4)]
+    store("y", k_scp, T.sc[:, :], T.scp[0:1, 0:64])
+    k_stp = op("s", [k_n1], lambda: S.activation(T.stp[:, :], T.n1[:, :], F.Identity, bias=STEP))
+
+    k_lx = {}
+    for part, arrived in ((near, ll), (far, lr)):
+        a = 4 * part[0]
+        k = op("v", [arrived] + (k_lf if part is near else []), lambda: V.tensor_copy(T.lx[:, a:a + 16], T.lf[:, a:a + 16]))
+        for r in part:
+            k_lx[r] = k
+    k_tab = k_pt
+    for s in range(N):
+        lst = T.lx[:, 4 * s:4 * s + 4]
+        if s:
+            k_tab = op("v", [k_tab, k_lx[s]], lambda: V.tensor_copy(T.pv[:, 64 * s:64 * s + 64], T.pt[:, 0:512].indirect(lst)))
+            k_pv = k_tab
+        k_tab = op("v", [k_tab, k_lx[s], k_slot], lambda: V.tensor_copy(T.pt[:, 0:512].indirect(lst), T.slot[:, 64 * s:64 * s + 64]))
+    k_pvs = op("v", [k_pv, k_stp], lambda: V.tensor_tensor_scan(T.pvs[:, 0:448], T.stp[:, 0:448], T.pv[:, 64:512], 0.0, A.add, A.max))
+    k_offc = vs([k_pvs, k_cor], T.offc[:, 0:112], T.pvs[:, 3:448:4], T.cor[:, 0:1], A.add)
+
+    def final_offsets():
+        k = op("v", [k_tab, k_stp], lambda: V.tensor_tensor_scan(T.pts[:, 0:512], T.stp[:, 0:512], T.pt[:, 0:512], 0.0, A.add, A.max))
+        return vs([k, k_cor], T.offf[:, 0:128], T.pts[:, 3:512:4], T.cor[:, 0:1], A.add)
+    for s in near + far:
+        store("y", k_lf if s == rank else [ll if s in near else lr], T.nb[s:s + 1, 0:64], T.lf[0:16, 4 * s:4 * s + 4])
+    store("y", [k_er, left], T.er[:, 0:1024], T.e32[:, 0:1024])
+    store("y", [k_er, left], T.er[:, 1024:2048], T.e32[:, 1024:2048])
+
+    k_near = [unpack(b, b, T.ql, T.pl, 0, 192, [cl] + k_abs + k_scol) for b in range(4)]
+    k_v = []
+    for b in range(4):
+        i = near.index(rank)
+        for at, first, n in ((0, near[0], i), (i, rank + 1, len(near) - 1 - i)):
+            if n:
+                k_v.append(op("s", [k_near[b]], lambda: S.activation(xs(first, b, n), T.ps[:, 512 * b + 64 * at:512 * b + 64 * (at + n)], F.Copy)))
+    k_far1 = [unpack(b, 4 + b, T.qr, T.pr, 0, 128, [cr] + k_xo) for b in range(4)]
+    k_far2 = [unpack(b, b, T.qr, T.pr, 128, 128, [cr] + k_v) for b in range(4)]
+    k_v += k_xo
+    k_ready = {r: k_v for r in near}
+    k_fv1 = [op("s", [k_far1[b]], lambda: S.activation(xs(far[0], b, 2), bank(4 + b, 128), F.Copy)) for b in (1, 3)]
+    k_fv2 = [op("s", [k_far2[b]], lambda: S.activation(xs(far[2], b, 2), bank(b, 128), F.Copy)) for b in range(4)]
+
+    k = k_x0
+    for s in range(N):
+        if s == far[0]:
+            k_offf = final_offsets()
+            k_fv1 += [op("v", [k_far1[b]], lambda: V.tensor_copy(xs(far[0], b, 2), bank(4 + b, 128))) for b in (0, 2)]
+            for r in far:
+                k_ready[r] = k_fv1 if r in far[:2] else k_fv2
+        if s:
+            a = 8 + 256 * s
+            k = op("v", [k, k_offc, k_x0] + k_ready[s] + k_ready[0] + k_d, lambda: V.tensor_tensor(
+                T.x[:, a:a + 256], T.x[:, 0:a].indirect(T.offc[:, 16 * (s - 1):16 * s]), T.x[:, a:a + 256], A.add))
+    for e, y, a, b in (("v", "y", 0, 384), ("s", "y", 384, 768), ("v", "y", 768, 1408), ("s", "s", 1408, 2048)):
+        out, src = T.ac[:, a:b], T.x[:, 0:2056].indirect(T.offf[:, a // 16:b // 16])
+        if e == "v":
+            ka = op("v", [k, k_offf], lambda: V.tensor_copy(out, src))
+        else:
+            ka = op("s", [k, k_offf], lambda: S.activation(out, src, F.Copy))
+        store(y, [ka], T.acc[:, a:b], out)
+
+    need("p", [("q" + e, count[e]) for e in "vstp"] + [("st", count["st"]), left])

@@ -17,18 +17,16 @@ SCRATCH = {
     "gs": ("sbuf", [128, 512], "uint8"),
     "ones": ("sbuf", [128, 128], "bfloat16"),
     "ident": ("sbuf", [128, 128], "bfloat16"),
-    "et": ("sbuf", [128, 2048], "bfloat16"),
+    "et": ("sbuf", [128, 520], "bfloat16"),
     "eq": ("sbuf", [128, 512], "float8_e4m3fn_x4"),
     "es": ("sbuf", [128, 512], "uint8"),
-    "pi": ("sbuf", [128, 32], "int32"),
-    "p3": ("sbuf", [128, 32], "int32"),
-    "ic": ("sbuf", [128, 4], "int32"),
-    "fc": ("sbuf", [128, 4], "float32"),
-    "uoff": ("sbuf", [128, 32], "uint16"),
+    "pi": ("sbuf", [128, 16], "int32"),
+    "p3": ("sbuf", [128, 16], "int32"),
+    "ic": ("sbuf", [128, 3], "int32"),
+    "fc": ("sbuf", [128, 3], "float32"),
+    "uoff": ("sbuf", [128, 16], "uint16"),
     "j0": ("sbuf", [128, 64], "float32"),
     "jt": ("sbuf", [128, 64], "float32"),
-    "m0": ("sbuf", [128, 64], "float32"),
-    "md": ("sbuf", [128, 64], "float32"),
     "n0": ("sbuf", [128, 512], "float32"),
     "n1": ("sbuf", [128, 512], "float32"),
     "stp": ("sbuf", [128, 512], "float32"),
@@ -41,18 +39,19 @@ SCRATCH = {
     "pvs": ("sbuf", [128, 448], "float32"),
     "sabs": ("sbuf", [128, 512], "float32"),
     "scol": ("sbuf", [128, 4], "float32"),
-    "eqt": ("sbuf", [128, 512], "float32"),
-    "eqm": ("sbuf", [128, 512], "float32"),
-    "cmp": ("sbuf", [128, 2048], "float32"),
-    "cnt": ("sbuf", [128, 8], "float32"),
-    "eqc": ("sbuf", [128, 4], "float32"),
+    "sg": ("sbuf", [128, 512], "bfloat16"),
+    "keep": ("sbuf", [128, 256], "bfloat16"),
+    "ts": ("sbuf", [128, 1024], "bfloat16"),
+    "cmp": ("sbuf", [128, 2048], "bfloat16"),
+    "junk": ("sbuf", [128, 1024], "float32"),
+    "sd": ("sbuf", [128, 4], "float32"),
+    "cnt": ("sbuf", [128, 4], "float32"),
+    "z": ("sbuf", [128, 4], "float32"),
+    "r2": ("sbuf", [128, 4], "float32"),
     "ru": ("sbuf", [128, 4], "uint16"),
     "w": ("sbuf", [128, 512], "float32"),
-    "t1": ("sbuf", [128, 64], "float32"),
-    "xp": ("sbuf", [128, 64], "float32"),
-    "yr": ("sbuf", [128, 64], "float32"),
-    "bb": ("sbuf", [128, 256], "float32"),
-    "bm": ("sbuf", [128, 256], "float32"),
+    "t1": ("sbuf", [128, 128], "float32"),
+    "y": ("sbuf", [128, 8], "float32"),
     "lf": ("sbuf", [128, 32], "float32"),
     "lx": ("sbuf", [128, 32], "uint16"),
     "lown": ("sbuf", [128, 4], "uint16"),
@@ -74,7 +73,12 @@ SCRATCH = {
     "ac": ("sbuf", [128, 2048], "float32"),
     "ps": ("psum", [128, 4096], "float32"),
 }
-SEMAPHORES = ["qv", "qs", "qt", "qp", "lu", "l0", "l1", "st", "ll", "lr", "cl", "cr", "loc"]
+ORDER = [("scores", 0), ("scores", 1), ("sizes", 0), ("col", 0, "v"), ("col", 1, "v"), ("scores", 2), ("signs", 0), ("sizes", 1),
+         ("col", 2, "s"), ("signs", 1), ("beats", 0, 1), ("beats", 1, 0), ("sizes", 2), ("col", 3, "s"), ("beats", 2, 0, 2),
+         ("beats", 1, 2, 2), ("beats", 0, 2, 2), ("signs", 2), ("signs", 3), ("beats", 3, 0, 3), ("total", 2), ("total", 1),
+         ("total", 0), ("total", 3), ("equals", 0), ("equals", 1), ("beats", 2, 3), ("running", 0), ("equals", 2), ("running", 1),
+         ("equals", 3), ("running", 2), ("running", 3)]
+SEMAPHORES = ["qv", "qs", "qt", "qp", "lu", "l0", "l1", "l2", "st", "ll", "lr", "cl", "cr", "cp", "loc"]
 
 
 def rank_program(g, core, T, topo):
@@ -124,110 +128,106 @@ def rank_program(g, core, T, topo):
             return op("v", deps, lambda: V.tensor_scalar(out=out, in0=in0, scalar1=s1, scalar2=None, op0=op0))
         return op("v", deps, lambda: V.tensor_scalar(out=out, in0=in0, scalar1=s1, scalar2=s2, op0=op0, op1=op1))
 
-    lu = load("y", T.uc[:, 0:16], T.u[:, 0:16], "lu")
-    l0 = load("y", T.grt[:, 0:1024], T.gr[:, 0:1024], "l0")
-    l1 = load("y", T.grt[:, 1024:2048], T.gr[:, 1024:2048], "l1")
+    pieces = ((0, 256), (256, 384), (384, 512))
+    lu = load("s", T.uc[:, 0:16], T.u[:, 0:16], "lu")
+    lg = [load("y", T.grt[:, 4 * a:4 * b], T.gr[:, 4 * a:4 * b], "l%d" % i) for i, (a, b) in enumerate(pieces)]
 
     def whole(out, pattern, base=0):
         return op("p", [], lambda: g.iota(out, pattern, base, 0, allow_small_or_imprecise_dtypes=True))
-    k_pi = op("p", [], lambda: g.iota(T.pi[:, 0:32], [[0, 32]], 0, 1))
+    k_pi = op("p", [], lambda: g.iota(T.pi[:, 0:16], [[0, 16]], 0, 1))
     k_ones = op("v", [], lambda: V.memset(T.ones[:, :], 1.0))
     k_id = op("p", [k_ones], lambda: g.affine_select(T.ident[:, :], T.ones[:, :], [[-1, 128]], A.is_equal, 0.0, 0, 1))
     k_j0 = whole(T.j0[:, :], [[128, 4], [1, 16]])
-    k_m0 = whole(T.m0[:, :], [[1, 16], [0, 4]])
     k_sl0 = whole(T.sl0[:, :], [[4, 512]], 8)
     k_n0 = whole(T.n0[:, :], [[0, 128], [4, 4]])
 
+    k_et = op("v", [], lambda: V.memset(T.et[:, :], 0.0))
+    k_kp = op("v", [], lambda: V.memset(T.keep[:, 0:128], 1.0))
     k_p3 = vs([k_pi], T.p3[:, :], T.pi[:, :], 3, A.bitwise_and)
-    for i, bits in ((0, 3), (1, 12), (2, 112), (3, 15)):
+    for i, bits in ((0, 3), (1, 12), (2, 112)):
         k_ic = vs([k_pi], T.ic[:, i:i + 1], T.pi[:, 0:1], bits, A.bitwise_and)
     k_uoff = op("v", [k_p3], lambda: V.tensor_copy(T.uoff[:, :], T.p3[:, :]))
     k_fc = op("v", [k_ic], lambda: V.tensor_copy(T.fc[:, :], T.ic[:, :]))
-    k_et = op("v", [], lambda: V.memset(T.et[:, :], 0.0))
-    k_e = [op("s", [k_id, k_et], lambda: S.activation(T.et[:, 512 * b + b:512 * (b + 1):4], T.ident[:, :], F.Copy)) for b in range(4)]
-    k_slot = op("s", [k_sl0, k_fc], lambda: S.activation(T.slot[:, :], T.sl0[:, :], F.Identity, bias=T.fc[:, 0:1]))
-    k_pt = op("s", [k_sl0, k_fc], lambda: S.activation(T.pt[:, :], T.sl0[:, :], F.Identity, bias=T.fc[:, 0:1], scale=0.0))
-
-    k_ut = op("v", [lu, k_uoff], lambda: V.tensor_copy(T.ut[:, :], T.uc[:, 0:16].indirect(T.uoff[:, 0:32])))
-    k_uq = op("v", [k_ut], lambda: V.quantize_mx(T.uq[:, 0:128], T.us[:, 0:128], T.ut[:, 0:512]))
-
-    def pack(a, ld):
-        return op("v", [ld], lambda: V.quantize_mx(T.gq[:, a:a + 256], T.gs[:, a:a + 256], T.grt[:, 4 * a:4 * a + 1024]))
-    k_g = [pack(0, l0)]
     k_w = op("v", [], lambda: V.memset(T.w[:, 0:64], 0.0))
-    k_xp = op("v", [], lambda: V.memset(T.xp[:, :], 0.0))
-    k_jt = vs([k_j0, k_fc], T.jt[:, :], T.j0[:, :], T.fc[:, 2:3], A.add)
-    k_md = vs([k_m0, k_fc], T.md[:, :], T.m0[:, :], T.fc[:, 3:4], A.is_equal)
-    k_g.append(pack(256, l1))
-    k_c0 = op("s", [l0], lambda: S.activation(T.e32[:, 0:512], T.grt[:, 0:512], F.Copy))
-    k_abs, k_sc = [], []
-    for i, b in ((0, 0), (1, 5)):
-        a = 256 * i
-        k = op("t", [k_uq, k_g[i]], lambda: g.tensor.matmul_mx(bank(b, 256), T.uq[:, 0:128], T.us[:, 0:128], T.gq[:, a:a + 256], T.gs[:, a:a + 256], True, True))
-        k_abs.append(op("s", [k], lambda: S.activation(T.sabs[:, a:a + 256], bank(b, 256), F.Abs)))
-        for q in (2 * i, 2 * i + 1):
-            k_sc.append(op("t", [k_uq, k_g[i]], lambda: g.tensor.matmul_mx(
-                bank(1 + q, 128), T.gq[:, 128 * q:128 * q + 128], T.gs[:, 128 * q:128 * q + 128], T.uq[:, 0:128], T.us[:, 0:128], True, True)))
-
-    k_scol, k_eq, k_cnt = [], [], {}
-
-    def column_score(q):
-        k_scol.append(op("v", [k_sc[q]], lambda: V.tensor_reduce(T.scol[:, q:q + 1], bank(1 + q, 1), AX, A.max, apply_absolute_value=True)))
-
-    def equal_scores(q):
-        k_eq.append(vs([k_abs[q // 2], k_scol[q]], T.eqt[:, 128 * q:128 * q + 128], T.sabs[:, 128 * q:128 * q + 128], T.scol[:, q:q + 1], A.is_equal))
-
-    def larger_scores(q, i):
-        lo, hi = 256 * i, 256 * i + 256
-        cut = min(max(128 * q, lo), hi)
-        for a, b, how in ((lo, cut, A.is_ge), (cut, hi, A.is_gt)):
-            if a < b:
-                k = vs([k_abs[i], k_scol[q]], T.cmp[:, 512 * q + a:512 * q + b], T.sabs[:, a:b], T.scol[:, q:q + 1], how)
-        part = T.cmp[:, 512 * q + lo:512 * q + hi]
-        k_cnt[(q, i)] = op("s", [k], lambda: S.activation(part, part, F.Copy, accum_out=T.cnt[:, 4 * i + q:4 * i + q + 1]))
-    for q in (0, 1):
-        column_score(q)
-    for q in (0, 1):
-        equal_scores(q)
-    for q in (0, 1):
-        larger_scores(q, 0)
-    for q in (2, 3):
-        column_score(q)
-    for q in (2, 3):
-        equal_scores(q)
-    k_eqm = op("p", k_eq, lambda: g.affine_select(T.eqm[:, :], T.eqt[:, :], [[0, 4], [-1, 128]], A.is_gt, 0.0, 0, 1))
-    for q, i in ((0, 1), (1, 1), (2, 0), (2, 1), (3, 0), (3, 1)):
-        larger_scores(q, i)
-
-    def eq_part(q):
-        return T.eqm[:, 128 * q:128 * q + 128]
-    k_eqc = [op("v", [k_eqm], lambda: V.tensor_reduce(T.eqc[:, q:q + 1], eq_part(q), AX, A.add)) for q in range(3)]
-    k_eqc.append(op("s", [k_eqm], lambda: S.activation(eq_part(3), eq_part(3), F.Copy, accum_out=T.eqc[:, 3:4])))
-    k_ru = [vs([k_cnt[(q, 0)], k_cnt[(q, 1)], k_eqc[q]], T.ru[:, q:q + 1], T.cnt[:, q:q + 1], T.cnt[:, 4 + q:5 + q], A.add, T.eqc[:, q:q + 1], A.add) for q in range(4)]
-
-    k_c1 = op("s", [l0, l1], lambda: S.activation(T.e32[:, 512:2048], T.grt[:, 512:2048], F.Copy))
-
-    k_w1 = op("v", [k_w, k_jt] + k_ru, lambda: V.tensor_copy(T.w[:, 0:512].indirect(T.ru[:, 0:4]), T.jt[:, 0:64]))
-    k_t1 = op("v", [k_w1], lambda: V.transpose(T.t1[:, :], T.w[:, 0:64]))
-    k_x1 = op("v", [k_t1, k_xp], lambda: V.tensor_tensor(T.xp[:, 0:64:32], T.t1[:, 0:64:32], T.t1[:, 16:64:32], A.add))
-    k_y = op("v", [k_x1], lambda: V.transpose(T.yr[:, :], T.xp[:, :]))
     k_h0 = op("v", [], lambda: V.memset(T.h[:, 256:512], 0.0))
     k_x0 = op("v", [], lambda: V.memset(T.x[:, 0:8], 0.0))
+    k = vs([k_id], T.keep[:, 128:256], T.ident[:, :], -2.0, A.mult, 1.0, A.add)
+    k_kp = op("v", [k, k_kp], lambda: V.memset(T.keep[:, 128:129], 0.0))
+    k_jt = vs([k_j0, k_fc], T.jt[:, :], T.j0[:, :], T.fc[:, 2:3], A.add)
     k_cor = vs([k_fc], T.cor[:, :], T.fc[:, 1:2], STEP / 4, A.mult, -3 * STEP, A.add)
-    k_bm = []
-    for a in range(4):
-        k = op("p", [k_y], lambda: g.partition_broadcast(T.bb[:, 64 * a:64 * a + 64], T.yr[32 * a:32 * a + 1, 0:64], 128))
-        k_bm.append(op("v", [k, k_md], lambda: V.tensor_tensor(T.bm[:, 64 * a:64 * a + 64], T.bb[:, 64 * a:64 * a + 64], T.md[:, :], A.mult)))
-        if a == 0:
-            k_eqz = op("v", k_e, lambda: V.quantize_mx(T.eq[:, 0:512], T.es[:, 0:512], T.et[:, 0:2048]))
+    k_e = op("s", [k_id, k_et], lambda: S.activation(T.et[:, 3:515:4], T.ident[:, :], F.Copy))
+
+    k_ut = [op("v", [lu, k_uoff], lambda: V.tensor_copy(T.ut[:, 0:256], T.uc[:, 0:16].indirect(T.uoff[:, 0:16]))),
+            op("s", [lu, k_uoff], lambda: S.activation(T.ut[:, 256:512], T.uc[:, 0:16].indirect(T.uoff[:, 0:16]), F.Copy))]
+    k_uq = op("v", k_ut, lambda: V.quantize_mx(T.uq[:, 0:128], T.us[:, 0:128], T.ut[:, 0:512]))
+
+    k_abs, k_scol, k_sc, k_row = {}, {}, {}, {}
+
+    def scores(i):
+        a, b = pieces[i]
+        kq = op("v", [lg[i]], lambda: V.quantize_mx(T.gq[:, a:b], T.gs[:, a:b], T.grt[:, 4 * a:4 * b]))
+        row = bank((0, 5, 6)[i], b - a)
+        k_row[i] = (op("t", [k_uq, kq], lambda: g.tensor.matmul_mx(row, T.uq[:, 0:128], T.us[:, 0:128], T.gq[:, a:b], T.gs[:, a:b], True, True)), row)
+        for q in range(a // 128, b // 128):
+            k_sc[q] = op("t", [k_uq, kq], lambda: g.tensor.matmul_mx(
+                bank(1 + q, 128), T.gq[:, 128 * q:128 * q + 128], T.gs[:, 128 * q:128 * q + 128], T.uq[:, 0:128], T.us[:, 0:128], True, True))
+
+    def sizes(i):
+        a, b = pieces[i]
+        k = op("s", [k_row[i][0]], lambda: S.activation(T.sabs[:, a:b], k_row[i][1], F.Abs))
+        for j in range(a // 128, b // 128):
+            k_abs[j] = k
+
+    def column_score(q, e):
+        if e == "v":
+            k_scol[q] = op("v", [k_sc[q]], lambda: V.tensor_reduce(T.scol[:, q:q + 1], bank(1 + q, 1), AX, A.max, apply_absolute_value=True))
+        else:
+            k_scol[q] = op("s", [k_sc[q]], lambda: S.activation(T.scol[:, q:q + 1], bank(1 + q, 1), F.Abs))
+
+    def blk(t, j, n=1):
+        return t[:, 128 * j:128 * (j + n)]
+    k_b, k_sg, k_cnt, k_ts = {q: {} for q in range(4)}, {}, {}, {}
+
+    def beats(q, j, n=1):
+        at = 4 * q + j - (j > q)
+        k = vs([k_abs[i] for i in range(j, j + n)] + [k_scol[q]], blk(T.cmp, at, n), blk(T.sabs, j, n), T.scol[:, q:q + 1], A.is_ge if j < q else A.is_gt, -512.0, A.mult)
+        for i in range(n):
+            k_b[q][at + i - 4 * q] = k
+
+    def signs(q):
+        k_sg[q] = op("s", [k_abs[q], k_scol[q]], lambda: S.activation(blk(T.sg, q), blk(T.sabs, q), F.Sign, bias=T.scol[:, q:q + 1], scale=-1.0, accum_out=T.sd[:, q:q + 1]))
+
+    def equals(q):
+        k_b[q][3] = vs([k_sg[q]], blk(T.cmp, 4 * q + 3), blk(T.sg, q), 0.0, A.is_equal, 256.0, A.mult)
+
+    def total(q):
+        k_cnt[q] = op("s", [k_b[q][0], k_b[q][1], k_sg[q]], lambda: S.activation(blk(T.junk, 2 * q, 2), blk(T.cmp, 4 * q, 2), F.Identity, bias=T.sd[:, q:q + 1], accum_out=T.cnt[:, q:q + 1]))
+
+    def running(q):
+        k_ts[q] = op("v", [k_b[q][2], k_b[q][3], k_kp], lambda: V.tensor_tensor_scan(blk(T.ts, 2 * q, 2), T.keep[:, :], blk(T.cmp, 4 * q + 2, 2), 0.0, A.mult, A.add))
+
+    steps = {"scores": scores, "sizes": sizes, "col": column_score, "beats": beats, "signs": signs, "equals": equals, "total": total, "running": running}
+    for step in ORDER:
+        steps[step[0]](*step[1:])
+    k = op("v", list(k_ts.values()), lambda: V.tensor_tensor(T.z[:, :], T.ts[:, 127:1024:256], T.ts[:, 255:1024:256], A.add))
+    k = op("v", [k] + list(k_cnt.values()), lambda: V.tensor_tensor(T.r2[:, :], T.z[:, :], T.cnt[:, :], A.add))
+    k_ru = vs([k], T.ru[:, :], T.r2[:, :], -1.0 / 512, A.mult, 64.0, A.add)
+
+    k_c1 = op("s", lg, lambda: S.activation(T.e32[:, 0:1024], T.grt[:, 0:1024], F.Copy))
+
     own = 4 * rank
-    k_lf = [op("v", k_bm, lambda: V.tensor_reduce(T.lf[:, own + c:own + c + 1], T.bm[:, c:256:4], AX, A.add)) for c in range(4)]
+    k = op("v", [k_w, k_jt, k_ru], lambda: V.tensor_copy(T.w[:, 0:512].indirect(T.ru[:, 0:4]), T.jt[:, 0:64]))
+    k = op("v", [k], lambda: V.tensor_copy(T.w[:, 64:128], T.w[:, 0:64]))
+    kt = [op("v", [k], lambda: V.transpose(T.t1[:, 32 * c:32 * c + 32], T.w[:, c:128:4])) for c in range(4)]
+    k = op("v", kt, lambda: V.tensor_tensor(T.y[:, 0:4], T.t1[:, 0:128:32], T.t1[:, 16:128:32], A.add))
+    kh = [op("v", [k], lambda: V.tensor_tensor(T.y[a:a + 64, 4:8], T.y[a:a + 64, 0:4], T.y[64 - a:128 - a, 0:4], A.add)) for a in (0, 64)]
+    k_lf = [op("v", kh, lambda: V.tensor_tensor(T.lf[a:a + 32, own:own + 4], T.y[a:a + 32, 4:8], T.y[a ^ 32:(a ^ 32) + 32, 4:8], A.add)) for a in (0, 32, 64, 96)]
 
     far_e = topo.engines(core, T.cores[far[0]])
     near_e = [e for e in topo.engines(core, T.cores[near_others[0]]) if e not in far_e]
     far_mask = sum(1 << e for e in far_e)
     near_mask = sum(1 << e for e in near_e)
-    left = ("loc", 3 * (len(far_e) + len(near_e)))
+    left = ("loc", 5 * (len(far_e) + len(near_e)))
 
     def ids(ranks):
         return [DstId(rid=topo.addr(T.cores[r])[0], pnc=topo.addr(T.cores[r])[1]) for r in ranks]
@@ -235,7 +235,7 @@ def rank_program(g, core, T, topo):
     def near_at(r):
         return [q for q in near if q != r].index(rank)
 
-    def send(deps, src, near_dst, far_dst, near_sem, far_sem):
+    def send(deps, src, near_dst, far_dst, near_sem, far_sem, far=far):
         need("p", deps)
         g.remote_dma_fused([
             RemoteDMATransfer(dst_ids=ids(far), dma_engine_mask=far_mask, remote_sem=T.sem[far_sem], srcs=[src], dsts=[far_dst(r) for r in far]),
@@ -249,23 +249,34 @@ def rank_program(g, core, T, topo):
     k_ou = {t: vs(k_lf, T.ou[:, 4 * t:4 * t + 4], T.lf[:, own:own + 4], 4.0, A.mult, float(t), A.add) for t in (2, 0, 3, 1)}
     k_h = []
     for t in (2, 3):
-        k_h.append(op("s", [k_ou[t], l0, l1], lambda: S.activation(T.h[:, t:256:4], T.grt[:, 0:2048].indirect(T.ou[:, 4 * t:4 * t + 4]), F.Copy)))
+        k_h.append(op("s", [k_ou[t]] + lg, lambda: S.activation(T.h[:, t:256:4], T.grt[:, 0:2048].indirect(T.ou[:, 4 * t:4 * t + 4]), F.Copy)))
     for t in (0, 1):
-        k_h.append(op("v", [k_ou[t], l0, l1], lambda: V.tensor_copy(T.h[:, t:256:4], T.grt[:, 0:2048].indirect(T.ou[:, 4 * t:4 * t + 4]))))
+        k_h.append(op("v", [k_ou[t]] + lg, lambda: V.tensor_copy(T.h[:, t:256:4], T.grt[:, 0:2048].indirect(T.ou[:, 4 * t:4 * t + 4]))))
     k_hq = op("v", k_h + [k_h0], lambda: V.quantize_mx(T.hq[:, 0:128], T.hs[:, 0:128], T.h[:, 0:512]))
+    k_eqz = [op("v", [k_e], lambda: V.quantize_mx(T.eq[:, 128 * b:128 * b + 128], T.es[:, 128 * b:128 * b + 128], T.et[:, 3 - b:515 - b])) for b in range(4)]
+    k_c0 = op("s", lg, lambda: S.activation(T.e32[:, 1024:2048], T.grt[:, 1024:2048], F.Copy))
+    k_slot = op("s", [k_sl0, k_fc], lambda: S.activation(T.slot[:, :], T.sl0[:, :], F.Identity, bias=T.fc[:, 0:1]))
+    k_pt = op("s", [k_sl0, k_fc], lambda: S.activation(T.pt[:, :], T.sl0[:, :], F.Identity, bias=T.fc[:, 0:1], scale=0.0))
+    k_abs, k_scol = list(k_abs.values()), list(k_scol.values())
 
     fa = 64 * near.index(rank)
+    partner = [far[near.index(rank)]]
     send([k_hq], T.hq[:, 0:64].bitcast(dt.uint8),
          lambda r: T.ql[:, 64 * near_at(r):64 * near_at(r) + 64].bitcast(dt.uint8),
-         lambda r: T.qr[:, fa:fa + 64].bitcast(dt.uint8), "cl", "cr")
+         lambda r: T.qr[:, fa:fa + 64].bitcast(dt.uint8), "cl", "cp", partner)
     send([k_hq], T.hs[:, 0:64],
          lambda r: T.pl[:, 64 * near_at(r):64 * near_at(r) + 64],
-         lambda r: T.pr[:, fa:fa + 64], "cl", "cr")
+         lambda r: T.pr[:, fa:fa + 64], "cl", "cp", partner)
     cl = ("cl", 2 * len(near_others) * len(near_e))
-    cr = ("cr", 2 * len(far) * len(far_e))
+    cp = ("cp", 2 * len(far_e))
+    need("p", [cp])
+    for piece in (T.qr[:, fa:fa + 64].bitcast(dt.uint8), T.pr[:, fa:fa + 64]):
+        g.remote_dma_fused([RemoteDMATransfer(dst_ids=ids(near_others), dma_engine_mask=far_mask + near_mask, remote_sem=T.sem["cr"],
+                                              srcs=[piece], dsts=[piece] * len(near_others))], local_sem=T.sem["loc"])
+    cr = ("cr", 2 * len(near_others) * (len(far_e) + len(near_e)))
 
     def unpack(b, to, q, s, a, n, deps):
-        return op("t", deps + [k_eqz], lambda: g.tensor.matmul_mx(bank(to, n), T.eq[:, 128 * b:128 * b + 128], T.es[:, 128 * b:128 * b + 128], q[:, a:a + n], s[:, a:a + n], True, True))
+        return op("t", deps + [k_eqz[b]], lambda: g.tensor.matmul_mx(bank(to, n), T.eq[:, 128 * b:128 * b + 128], T.es[:, 128 * b:128 * b + 128], q[:, a:a + n], s[:, a:a + n], True, True))
 
     def xs(r, b, n):
         return T.x[:, 8 + 256 * r + b:8 + 256 * (r + n):4]
@@ -312,7 +323,7 @@ def rank_program(g, core, T, topo):
         for at, first, n in ((0, near[0], i), (i, rank + 1, len(near) - 1 - i)):
             if n:
                 k_v.append(op("s", [k_near[b]], lambda: S.activation(xs(first, b, n), T.ps[:, 512 * b + 64 * at:512 * b + 64 * (at + n)], F.Copy)))
-    k_far1 = [unpack(b, 4 + b, T.qr, T.pr, 0, 128, [cr] + k_xo) for b in range(4)]
+    k_far1 = [unpack(b, 4 + b, T.qr, T.pr, 0, 128, [cr, cp] + k_xo) for b in range(4)]
     k_far2 = [unpack(b, b, T.qr, T.pr, 128, 128, [cr] + k_v) for b in range(4)]
     k_v += k_xo
     k_ready = {r: k_v for r in near}

@@ -4,8 +4,9 @@ from concourse.mybir import dt, AluOpType, AxisListType, ActivationFunctionType
 A = AluOpType
 F = ActivationFunctionType
 AX = AxisListType.X
-STEP = 4096.0
-DROP = 1048576.0
+UNIT = 2.0 ** -18
+STEP = 1.0 / 64
+NONE = 32
 
 SCRATCH = {
     "grt": ("sbuf", [128, 2048], "bfloat16"),
@@ -22,21 +23,19 @@ SCRATCH = {
     "es": ("sbuf", [128, 512], "uint8"),
     "pi": ("sbuf", [128, 16], "int32"),
     "p3": ("sbuf", [128, 16], "int32"),
-    "ic": ("sbuf", [128, 3], "int32"),
-    "fc": ("sbuf", [128, 3], "float32"),
+    "ic": ("sbuf", [128, 7], "int32"),
+    "fc": ("sbuf", [128, 7], "float32"),
+    "cc": ("sbuf", [128, 12], "float32"),
     "uoff": ("sbuf", [128, 16], "uint16"),
     "j0": ("sbuf", [128, 64], "float32"),
     "jt": ("sbuf", [128, 64], "float32"),
-    "n0": ("sbuf", [128, 512], "float32"),
-    "n1": ("sbuf", [128, 512], "float32"),
-    "stp": ("sbuf", [128, 512], "float32"),
-    "cor": ("sbuf", [128, 1], "float32"),
-    "sl0": ("sbuf", [128, 512], "float32"),
-    "slot": ("sbuf", [128, 512], "float32"),
-    "pt": ("sbuf", [128, 512], "float32"),
-    "pv": ("sbuf", [128, 512], "float32"),
-    "pts": ("sbuf", [128, 512], "float32"),
-    "pvs": ("sbuf", [128, 448], "float32"),
+    "n0": ("sbuf", [128, 256], "float32"),
+    "stp": ("sbuf", [128, 256], "float32"),
+    "v0": ("sbuf", [128, 128], "float32"),
+    "val": ("sbuf", [128, 128], "float32"),
+    "e0": ("sbuf", [128, 18], "float32"),
+    "eo": ("sbuf", [128, 18], "uint16"),
+    "selo": ("sbuf", [128, 2], "uint16"),
     "sabs": ("sbuf", [128, 512], "float32"),
     "scol": ("sbuf", [128, 4], "float32"),
     "sg": ("sbuf", [128, 512], "bfloat16"),
@@ -52,9 +51,11 @@ SCRATCH = {
     "w": ("sbuf", [128, 512], "float32"),
     "t1": ("sbuf", [128, 128], "float32"),
     "y": ("sbuf", [128, 8], "float32"),
-    "lf": ("sbuf", [128, 32], "float32"),
-    "lx": ("sbuf", [128, 32], "uint16"),
+    "lf": ("sbuf", [128, 36], "float32"),
+    "lo": ("sbuf", [128, 4], "float32"),
     "lown": ("sbuf", [128, 4], "uint16"),
+    "xo": ("sbuf", [128, 32], "float32"),
+    "to": ("sbuf", [128, 32], "float32"),
     "ou": ("sbuf", [128, 16], "uint16"),
     "h": ("sbuf", [128, 512], "bfloat16"),
     "hq": ("sbuf", [128, 128], "float8_e4m3fn_x4"),
@@ -67,9 +68,15 @@ SCRATCH = {
     "d": ("sbuf", [128, 256], "float32"),
     "scg": ("sbuf", [128, 64], "float32"),
     "scp": ("sbuf", [128, 64], "float32"),
+    "ls": ("sbuf", [128, 32], "uint16"),
+    "tb": ("sbuf", [128, 520], "float32"),
+    "got": ("sbuf", [128, 320], "float32"),
+    "run": ("sbuf", [128, 1152], "float32"),
+    "zz": ("sbuf", [128, 64], "float32"),
+    "ex": ("sbuf", [128, 256], "float32"),
+    "tx": ("sbuf", [128, 256], "float32"),
     "x": ("sbuf", [128, 2056], "float32"),
-    "offc": ("sbuf", [128, 112], "uint16"),
-    "offf": ("sbuf", [128, 128], "uint16"),
+    "off": ("sbuf", [128, 256], "uint16"),
     "ac": ("sbuf", [128, 2048], "float32"),
     "ps": ("psum", [128, 4096], "float32"),
 }
@@ -128,9 +135,20 @@ def rank_program(g, core, T, topo):
             return op("v", deps, lambda: V.tensor_scalar(out=out, in0=in0, scalar1=s1, scalar2=None, op0=op0))
         return op("v", deps, lambda: V.tensor_scalar(out=out, in0=in0, scalar1=s1, scalar2=s2, op0=op0, op1=op1))
 
+    def vt(deps, out, in0, in1, how):
+        return op("v", deps, lambda: V.tensor_tensor(out, in0, in1, how))
+
+    def vc(deps, out, in_):
+        return op("v", deps, lambda: V.tensor_copy(out, in_))
+
+    def sa(deps, out, in_, scale=1.0, bias=0.0):
+        return op("s", deps, lambda: S.activation(out, in_, F.Identity, bias=bias, scale=scale))
+
     pieces = ((0, 256), (256, 384), (384, 512))
     lu = load("s", T.uc[:, 0:16], T.u[:, 0:16], "lu")
     lg = [load("y", T.grt[:, 4 * a:4 * b], T.gr[:, 4 * a:4 * b], "l%d" % i) for i, (a, b) in enumerate(pieces)]
+
+    own = 4 * rank
 
     def whole(out, pattern, base=0):
         return op("p", [], lambda: g.iota(out, pattern, base, 0, allow_small_or_imprecise_dtypes=True))
@@ -138,28 +156,53 @@ def rank_program(g, core, T, topo):
     k_ones = op("v", [], lambda: V.memset(T.ones[:, :], 1.0))
     k_id = op("p", [k_ones], lambda: g.affine_select(T.ident[:, :], T.ones[:, :], [[-1, 128]], A.is_equal, 0.0, 0, 1))
     k_j0 = whole(T.j0[:, :], [[128, 4], [1, 16]])
-    k_sl0 = whole(T.sl0[:, :], [[4, 512]], 8)
-    k_n0 = whole(T.n0[:, :], [[0, 128], [4, 4]])
+    whole(T.e0[:, 0:8], [[4, 4], [0, 2]], 16)
+    whole(T.e0[:, 8:16], [[1, 4], [0, 2]])
+    k_e0 = whole(T.e0[:, 16:18], [[0, 2]])
+    k_v0 = whole(T.v0[:, :], [[256, 2], [4, 4], [16, 16]], 8)
+    whole(T.n0[:, 0:128], [[0, 8], [1, 16]])
+    k_n0 = whole(T.n0[:, 128:256], [[0, 4], [1, 32]])
 
     k_et = op("v", [], lambda: V.memset(T.et[:, :], 0.0))
     k_kp = op("v", [], lambda: V.memset(T.keep[:, 0:128], 1.0))
     k_p3 = vs([k_pi], T.p3[:, :], T.pi[:, :], 3, A.bitwise_and)
-    for i, bits in ((0, 3), (1, 12), (2, 112)):
-        k_ic = vs([k_pi], T.ic[:, i:i + 1], T.pi[:, 0:1], bits, A.bitwise_and)
-    k_uoff = op("v", [k_p3], lambda: V.tensor_copy(T.uoff[:, :], T.p3[:, :]))
-    k_fc = op("v", [k_ic], lambda: V.tensor_copy(T.fc[:, :], T.ic[:, :]))
+    names = {"b": 3, "k4": 12, "g16": 112, "m": 15, "r": 31, "a32": 96, "h16": 16}
+    col = {}
+    for i, name in enumerate(names):
+        k_ic = vs([k_pi], T.ic[:, i:i + 1], T.pi[:, 0:1], names[name], A.bitwise_and)
+        col[name] = T.fc[:, i:i + 1]
+    k_uoff = vc([k_p3], T.uoff[:, :], T.p3[:, :])
+    k_fc = vc([k_ic], T.fc[:, :], T.ic[:, :])
     k_w = op("v", [], lambda: V.memset(T.w[:, 0:64], 0.0))
-    k_h0 = op("v", [], lambda: V.memset(T.h[:, 256:512], 0.0))
-    k_x0 = op("v", [], lambda: V.memset(T.x[:, 0:8], 0.0))
     k = vs([k_id], T.keep[:, 128:256], T.ident[:, :], -2.0, A.mult, 1.0, A.add)
+    k_jt = vs([k_j0, k_fc], T.jt[:, :], T.j0[:, :], col["g16"], A.add)
     k_kp = op("v", [k, k_kp], lambda: V.memset(T.keep[:, 128:129], 0.0))
-    k_jt = vs([k_j0, k_fc], T.jt[:, :], T.j0[:, :], T.fc[:, 2:3], A.add)
-    k_cor = vs([k_fc], T.cor[:, :], T.fc[:, 1:2], STEP / 4, A.mult, -3 * STEP, A.add)
     k_e = op("s", [k_id, k_et], lambda: S.activation(T.et[:, 3:515:4], T.ident[:, :], F.Copy))
 
-    k_ut = [op("v", [lu, k_uoff], lambda: V.tensor_copy(T.ut[:, 0:256], T.uc[:, 0:16].indirect(T.uoff[:, 0:16]))),
+    def pack_ones(b):
+        return op("v", [k_e], lambda: V.quantize_mx(T.eq[:, 128 * b:128 * b + 128], T.es[:, 128 * b:128 * b + 128], T.et[:, 3 - b:515 - b]))
+    k_eqz = [pack_ones(b) for b in (0, 1)]
+    k_h0 = op("v", [], lambda: V.memset(T.h[:, 256:512], 0.0))
+    k_none = op("v", [], lambda: V.memset(T.lf[:, NONE:NONE + 4], 512.0))
+    k_x0 = op("v", [], lambda: V.memset(T.x[:, 0:8], 0.0))
+
+    def small(i, deps, in_, scale, bias):
+        return T.cc[:, i:i + 1], sa(deps, T.cc[:, i:i + 1], in_, scale, bias)
+    c_k, k_ck = small(0, [k_fc], col["k4"], 0.25, 0.0)
+    c_back16, k_b16 = small(1, [k_fc], col["m"], STEP, -15 * STEP)
+    c_back32, k_b32 = small(2, [k_fc], col["r"], STEP, -31 * STEP)
+    c_base, k_base = small(3, [k_fc], col["a32"], 16 * UNIT, 0.0)
+    c_b, k_cb = small(4, [k_fc], col["b"], 1.0, -float(NONE))
+    c_t, k = small(5, [k_cb], col["h16"], 0.25, c_b)
+    c_u, k_cu = small(6, [k_cb], col["a32"], 0.25, c_b)
+    c_later, k_later = small(7, [k], col["k4"], 2.0, c_t)
+
+    k_ut = [vc([lu, k_uoff], T.ut[:, 0:256], T.uc[:, 0:16].indirect(T.uoff[:, 0:16])),
             op("s", [lu, k_uoff], lambda: S.activation(T.ut[:, 256:512], T.uc[:, 0:16].indirect(T.uoff[:, 0:16]), F.Copy))]
     k_uq = op("v", k_ut, lambda: V.quantize_mx(T.uq[:, 0:128], T.us[:, 0:128], T.ut[:, 0:512]))
+    k_eqz.append(pack_ones(2))
+    k_tb = sa([k_e], T.tb[:, :], T.et[:, :], 0.0)
+    k_val = sa([k_v0, k_base], T.val[:, :], T.v0[:, :], UNIT, c_base)
 
     k_abs, k_scol, k_sc, k_row = {}, {}, {}, {}
 
@@ -171,6 +214,8 @@ def rank_program(g, core, T, topo):
         for q in range(a // 128, b // 128):
             k_sc[q] = op("t", [k_uq, kq], lambda: g.tensor.matmul_mx(
                 bank(1 + q, 128), T.gq[:, 128 * q:128 * q + 128], T.gs[:, 128 * q:128 * q + 128], T.uq[:, 0:128], T.us[:, 0:128], True, True))
+        if i == 0:
+            k_eqz.append(pack_ones(3))
 
     def sizes(i):
         a, b = pieces[i]
@@ -209,19 +254,22 @@ def rank_program(g, core, T, topo):
     steps = {"scores": scores, "sizes": sizes, "col": column_score, "beats": beats, "signs": signs, "equals": equals, "total": total, "running": running}
     for step in ORDER:
         steps[step[0]](*step[1:])
-    k = op("v", list(k_ts.values()), lambda: V.tensor_tensor(T.z[:, :], T.ts[:, 127:1024:256], T.ts[:, 255:1024:256], A.add))
-    k = op("v", [k] + list(k_cnt.values()), lambda: V.tensor_tensor(T.r2[:, :], T.z[:, :], T.cnt[:, :], A.add))
+    k = vt(list(k_ts.values()), T.z[:, :], T.ts[:, 127:1024:256], T.ts[:, 255:1024:256], A.add)
+    k = vt([k] + list(k_cnt.values()), T.r2[:, :], T.z[:, :], T.cnt[:, :], A.add)
     k_ru = vs([k], T.ru[:, :], T.r2[:, :], -1.0 / 512, A.mult, 64.0, A.add)
+    k_eo = vs([k_e0, k_ck], T.eo[:, 16:18], T.e0[:, 16:18], c_k, A.add)
+    k_abs, k_scol = list(k_abs.values()), list(k_scol.values())
 
-    k_c1 = op("s", lg, lambda: S.activation(T.e32[:, 0:1024], T.grt[:, 0:1024], F.Copy))
+    k_c1 = op("s", lg, lambda: S.activation(T.e32[:, 0:1280], T.grt[:, 0:1280], F.Copy))
 
-    own = 4 * rank
-    k = op("v", [k_w, k_jt, k_ru], lambda: V.tensor_copy(T.w[:, 0:512].indirect(T.ru[:, 0:4]), T.jt[:, 0:64]))
-    k = op("v", [k], lambda: V.tensor_copy(T.w[:, 64:128], T.w[:, 0:64]))
+    def across(deps, src, half, out, how):
+        kh = [vt(deps, half(a, 64), src(a, 64), src(64 - a, 64), how) for a in (0, 64)]
+        return [vt(kh, out(a, 32), half(a, 32), half(a ^ 32, 32), how) for a in (0, 32, 64, 96)]
+    k = vc([k_w, k_jt, k_ru], T.w[:, 0:512].indirect(T.ru[:, 0:4]), T.jt[:, 0:64])
+    k = vc([k], T.w[:, 64:128], T.w[:, 0:64])
     kt = [op("v", [k], lambda: V.transpose(T.t1[:, 32 * c:32 * c + 32], T.w[:, c:128:4])) for c in range(4)]
-    k = op("v", kt, lambda: V.tensor_tensor(T.y[:, 0:4], T.t1[:, 0:128:32], T.t1[:, 16:128:32], A.add))
-    kh = [op("v", [k], lambda: V.tensor_tensor(T.y[a:a + 64, 4:8], T.y[a:a + 64, 0:4], T.y[64 - a:128 - a, 0:4], A.add)) for a in (0, 64)]
-    k_lf = [op("v", kh, lambda: V.tensor_tensor(T.lf[a:a + 32, own:own + 4], T.y[a:a + 32, 4:8], T.y[a ^ 32:(a ^ 32) + 32, 4:8], A.add)) for a in (0, 32, 64, 96)]
+    k = vt(kt, T.y[:, 0:4], T.t1[:, 0:128:32], T.t1[:, 16:128:32], A.add)
+    k_lf = across([k], lambda a, n: T.y[a:a + n, 0:4], lambda a, n: T.y[a:a + n, 4:8], lambda a, n: T.lo[a:a + n, 0:4], A.add)
 
     far_e = topo.engines(core, T.cores[far[0]])
     near_e = [e for e in topo.engines(core, T.cores[near_others[0]]) if e not in far_e]
@@ -242,22 +290,17 @@ def rank_program(g, core, T, topo):
             RemoteDMATransfer(dst_ids=ids(near_others), dma_engine_mask=near_mask, remote_sem=T.sem[near_sem], srcs=[src], dsts=[near_dst(r) for r in near_others]),
         ], local_sem=T.sem["loc"])
 
-    send(k_lf, T.lf[:, own:own + 4], lambda r: T.lf[:, own:own + 4], lambda r: T.lf[:, own:own + 4], "ll", "lr")
+    send(k_lf, T.lo[:, 0:4], lambda r: T.lf[:, own:own + 4], lambda r: T.lf[:, own:own + 4], "ll", "lr")
     ll = ("ll", len(near_others) * len(near_e))
     lr = ("lr", len(far) * len(far_e))
 
-    k_ou = {t: vs(k_lf, T.ou[:, 4 * t:4 * t + 4], T.lf[:, own:own + 4], 4.0, A.mult, float(t), A.add) for t in (2, 0, 3, 1)}
-    k_h = []
-    for t in (2, 3):
-        k_h.append(op("s", [k_ou[t]] + lg, lambda: S.activation(T.h[:, t:256:4], T.grt[:, 0:2048].indirect(T.ou[:, 4 * t:4 * t + 4]), F.Copy)))
-    for t in (0, 1):
-        k_h.append(op("v", [k_ou[t]] + lg, lambda: V.tensor_copy(T.h[:, t:256:4], T.grt[:, 0:2048].indirect(T.ou[:, 4 * t:4 * t + 4]))))
+    k = vc(k_lf + [k_eo], T.xo[:, :], T.lo[:, 0:4].indirect(T.eo[:, 16:18]))
+    k = op("v", [k], lambda: V.transpose(T.to[:, :], T.xo[:, :]))
+    k_ou = vs([k], T.ou[:, :], T.to[:, 0:16], 4.0, A.mult, col["b"], A.add)
+    k_h = [op("s", [k_ou] + lg, lambda: S.activation(T.h[:, 128:256], T.grt[:, 0:2048].indirect(T.ou[:, 8:16]), F.Copy)),
+           vc([k_ou] + lg, T.h[:, 0:128], T.grt[:, 0:2048].indirect(T.ou[:, 0:8]))]
     k_hq = op("v", k_h + [k_h0], lambda: V.quantize_mx(T.hq[:, 0:128], T.hs[:, 0:128], T.h[:, 0:512]))
-    k_eqz = [op("v", [k_e], lambda: V.quantize_mx(T.eq[:, 128 * b:128 * b + 128], T.es[:, 128 * b:128 * b + 128], T.et[:, 3 - b:515 - b])) for b in range(4)]
-    k_c0 = op("s", lg, lambda: S.activation(T.e32[:, 1024:2048], T.grt[:, 1024:2048], F.Copy))
-    k_slot = op("s", [k_sl0, k_fc], lambda: S.activation(T.slot[:, :], T.sl0[:, :], F.Identity, bias=T.fc[:, 0:1]))
-    k_pt = op("s", [k_sl0, k_fc], lambda: S.activation(T.pt[:, :], T.sl0[:, :], F.Identity, bias=T.fc[:, 0:1], scale=0.0))
-    k_abs, k_scol = list(k_abs.values()), list(k_scol.values())
+    k_c0 = op("s", lg, lambda: S.activation(T.e32[:, 1280:2048], T.grt[:, 1280:2048], F.Copy))
 
     fa = 64 * near.index(rank)
     partner = [far[near.index(rank)]]
@@ -275,46 +318,57 @@ def rank_program(g, core, T, topo):
                                               srcs=[piece], dsts=[piece] * len(near_others))], local_sem=T.sem["loc"])
     cr = ("cr", 2 * len(near_others) * (len(far_e) + len(near_e)))
 
+    k1 = vs([k_fc], T.cc[:, 8:9], col["k4"], 8.0, A.mult, col["a32"], A.is_gt)
+    k2 = vs([k_fc], T.cc[:, 9:10], col["m"], col["h16"], A.subtract, 8.0, A.is_lt)
+    k3 = vs([k_fc], T.cc[:, 10:11], col["m"], 4.0, A.is_ge, 4.0, A.mult)
+    k_stp = [vs([k_n0, k_fc], T.stp[:, 0:128], T.n0[:, 0:128], col["m"], A.not_equal, STEP - 1.0, A.add),
+             vs([k_n0, k_fc], T.stp[:, 128:256], T.n0[:, 128:256], col["r"], A.not_equal, STEP - 1.0, A.add)]
+    k3 = vs([k3, k_cu], T.cc[:, 11:12], T.cc[:, 10:11], c_u, A.add)
+    k_eo = [vs([k_e0, k_ck], T.eo[:, 0:8], T.e0[:, 0:8], c_k, A.add), vs([k_e0, k_fc], T.eo[:, 8:16], T.e0[:, 8:16], col["k4"], A.add)]
+    k_selo = [vs([k1, k_later], T.selo[:, 1:2], c_later, T.cc[:, 8:9], A.mult, float(NONE), A.add),
+              vs([k2, k3], T.selo[:, 0:1], T.cc[:, 11:12], T.cc[:, 9:10], A.mult, float(NONE), A.add)]
+
     def unpack(b, to, q, s, a, n, deps):
         return op("t", deps + [k_eqz[b]], lambda: g.tensor.matmul_mx(bank(to, n), T.eq[:, 128 * b:128 * b + 128], T.es[:, 128 * b:128 * b + 128], q[:, a:a + n], s[:, a:a + n], True, True))
 
     def xs(r, b, n):
         return T.x[:, 8 + 256 * r + b:8 + 256 * (r + n):4]
     k_own = [unpack(b, 4 + b, T.hq, T.hs, 0, 128, [k_hq] + k_scol + k_abs) for b in range(4)]
-    k_xo = [op("s", [k_own[b]], lambda: S.activation(xs(rank, b, 1), bank(4 + b, 64), F.Copy)) for b in range(4)]
-    k_lown = op("v", k_lf, lambda: V.tensor_copy(T.lown[:, :], T.lf[:, own:own + 4]))
-    k_n1 = vs([k_n0, k_fc], T.n1[:, :], T.n0[:, :], T.fc[:, 1:2], A.is_equal, -(DROP + STEP), A.mult)
-    k_d = [op("v", [k_xo[b]] + k_h, lambda: V.tensor_tensor(T.d[:, 64 * b:64 * b + 64], T.h[:, b:256:4], xs(rank, b, 1), A.subtract)) for b in range(4)]
-    k_er = op("v", k_d + [k_c0, k_c1] + [k_ou[t] for t in range(4)], lambda: V.tensor_copy(T.e32[:, 0:2048].indirect(T.ou[:, 0:16]), T.d[:, 0:256]))
+    k_lown = vc(k_lf, T.lown[:, :], T.lo[:, 0:4])
+    k_lf = [vc(k_lf, T.lf[:, own:own + 4], T.lo[:, 0:4])]
+    k_d = [vt([k_own[b]] + k_h, T.d[:, b:256:4], T.h[:, b:256:4], bank(4 + b, 64), A.subtract) for b in range(4)]
+    k_er = vc(k_d + [k_c0, k_c1, k_ou], T.e32[:, 0:2048].indirect(T.ou[:, 0:16]), T.d[:, 0:256])
+    k_xo = [op("s", [k_d[b]], lambda: S.activation(xs(rank, b, 1), bank(4 + b, 64), F.Copy)) for b in range(4)]
 
     k_scg = op("s", [k_lown] + k_abs, lambda: S.activation(T.scg[:, :], T.sabs[:, 0:512].indirect(T.lown[:, 0:4]), F.Copy))
     k_scp = [op("s", [k_scg], lambda: S.activation(T.scp[0:1, c:64:4], T.scg[0:1, 16 * c:16 * c + 16], F.Copy)) for c in range(4)]
     store("y", k_scp, T.sc[:, :], T.scp[0:1, 0:64])
-    k_stp = op("s", [k_n1], lambda: S.activation(T.stp[:, :], T.n1[:, :], F.Identity, bias=STEP))
 
-    k_lx = {}
-    for part, arrived in ((near, ll), (far, lr)):
-        a = 4 * part[0]
-        k = op("v", [arrived] + (k_lf if part is near else []), lambda: V.tensor_copy(T.lx[:, a:a + 16], T.lf[:, a:a + 16]))
-        for r in part:
-            k_lx[r] = k
-    k_tab = k_pt
-    for s in range(N):
-        lst = T.lx[:, 4 * s:4 * s + 4]
-        if s:
-            k_tab = op("v", [k_tab, k_lx[s]], lambda: V.tensor_copy(T.pv[:, 64 * s:64 * s + 64], T.pt[:, 0:512].indirect(lst)))
-            k_pv = k_tab
-        k_tab = op("v", [k_tab, k_lx[s], k_slot], lambda: V.tensor_copy(T.pt[:, 0:512].indirect(lst), T.slot[:, 64 * s:64 * s + 64]))
-    k_pvs = op("v", [k_pv, k_stp], lambda: V.tensor_tensor_scan(T.pvs[:, 0:448], T.stp[:, 0:448], T.pv[:, 64:512], 0.0, A.add, A.max))
-    k_offc = vs([k_pvs, k_cor], T.offc[:, 0:112], T.pvs[:, 3:448:4], T.cor[:, 0:1], A.add)
+    table = T.tb[:, 0:520]
+    k_ls = vc([ll, lr, k_none] + k_lf + k_selo, T.ls[:, :], T.lf[:, 0:36].indirect(T.selo[:, 0:2]))
+    k = vc([k_ls, k_tb, k_val], table.indirect(T.ls[:, 0:4]), T.val[:, 0:64])
+    k_g1 = vc([k], T.got[:, 256:320], table.indirect(T.ls[:, 8:12]))
+    k_tab = vc([k_g1], table.indirect(T.ls[:, 4:8]), T.val[:, 64:128])
+    k_g2 = op("s", [k_tab], lambda: S.activation(T.got[:, 0:256], table.indirect(T.ls[:, 16:32]), F.Copy))
 
-    def final_offsets():
-        k = op("v", [k_tab, k_stp], lambda: V.tensor_tensor_scan(T.pts[:, 0:512], T.stp[:, 0:512], T.pt[:, 0:512], 0.0, A.add, A.max))
-        return vs([k, k_cor], T.offf[:, 0:128], T.pts[:, 3:512:4], T.cor[:, 0:1], A.add)
-    for s in near + far:
-        store("y", k_lf if s == rank else [ll if s in near else lr], T.nb[s:s + 1, 0:64], T.lf[0:16, 4 * s:4 * s + 4])
+    def pick(deps, out, step, in_):
+        return op("v", deps + k_stp, lambda: V.tensor_tensor_scan(out, step, in_, 0.0, A.add, A.max))
+    k_run = [pick([k_g1], T.run[:, 1025:1152:2], T.stp[:, 0:64], T.got[:, 256:320])]
+    k_run += [pick([k_tab], blk(T.run, c), T.stp[:, 128:256], T.tb[:, c:512:4]) for c in range(4)]
+    k_run += [pick([k_g2], T.run[:, 513 + 256 * i:768 + 256 * i:2], T.stp[:, 0:128], blk(T.got, i)) for i in range(2)]
+    k = [vc(k_run, T.run[32 * a:32 * a + 32, 543 + 128 * a:640 + 128 * a:32], T.run[32 * a:32 * a + 32, 1055:1152:32]) for a in range(4)]
+    k_zz = across(k, lambda a, n: T.run[a:a + n, 31:1024:32], lambda a, n: T.zz[a:a + n, 32:64], lambda a, n: T.zz[a:a + n, 0:32], A.max)
+    k = vs(k_zz + k_eo + [k_b16], T.ex[:, 0:128], T.zz[:, 0:32].indirect(T.eo[:, 0:8]), c_back16, A.add)
+
+    def wrapped(deps, a, lo):
+        k = op("v", deps, lambda: V.transpose(T.tx[:, a:a + 128], T.ex[:, a:a + 128]))
+        return vs([k], T.off[:, a + lo:a + 128], T.tx[:, a + lo:a + 128], 1.0 / UNIT, A.mult, col["b"], A.add)
+    k_offc = wrapped([k], 0, 16)
+
     store("y", [k_er, left], T.er[:, 0:1024], T.e32[:, 0:1024])
     store("y", [k_er, left], T.er[:, 1024:2048], T.e32[:, 1024:2048])
+    for s in range(N):
+        store("y", k_lf + [ll, lr], T.nb[s:s + 1, 0:64], T.lf[0:16, 4 * s:4 * s + 4])
 
     k_near = [unpack(b, b, T.ql, T.pl, 0, 192, [cl] + k_abs + k_scol) for b in range(4)]
     k_v = []
@@ -327,24 +381,22 @@ def rank_program(g, core, T, topo):
     k_far2 = [unpack(b, b, T.qr, T.pr, 128, 128, [cr] + k_v) for b in range(4)]
     k_v += k_xo
     k_ready = {r: k_v for r in near}
-    k_fv1 = [op("s", [k_far1[b]], lambda: S.activation(xs(far[0], b, 2), bank(4 + b, 128), F.Copy)) for b in (1, 3)]
+    k_fv1 = [op("s", [k_far1[b]], lambda: S.activation(xs(far[0], b, 2), bank(4 + b, 128), F.Copy)) for b in range(4)]
     k_fv2 = [op("s", [k_far2[b]], lambda: S.activation(xs(far[2], b, 2), bank(b, 128), F.Copy)) for b in range(4)]
+    for r in far:
+        k_ready[r] = k_fv1 if r in far[:2] else k_fv2
+    k_last = sa(k_zz + k_eo + [k_b32], T.ex[:, 128:256], T.zz[:, 0:32].indirect(T.eo[:, 8:16]), 1.0, c_back32)
 
     k = k_x0
-    for s in range(N):
-        if s == far[0]:
-            k_offf = final_offsets()
-            k_fv1 += [op("v", [k_far1[b]], lambda: V.tensor_copy(xs(far[0], b, 2), bank(4 + b, 128))) for b in (0, 2)]
-            for r in far:
-                k_ready[r] = k_fv1 if r in far[:2] else k_fv2
-        if s:
-            a = 8 + 256 * s
-            k = op("v", [k, k_offc, k_x0] + k_ready[s] + k_ready[0] + k_d, lambda: V.tensor_tensor(
-                T.x[:, a:a + 256], T.x[:, 0:a].indirect(T.offc[:, 16 * (s - 1):16 * s]), T.x[:, a:a + 256], A.add))
+    for s in range(1, N):
+        a = 8 + 256 * s
+        k = vt([k, k_offc, k_x0] + k_ready[s] + k_ready[0], T.x[:, a:a + 256], T.x[:, 0:a].indirect(T.off[:, 16 * s:16 * s + 16]), T.x[:, a:a + 256], A.add)
+        if s == N - 2:
+            k_offf = wrapped([k_last], 128, 0)
     for e, y, a, b in (("v", "y", 0, 384), ("s", "y", 384, 768), ("v", "y", 768, 1408), ("s", "s", 1408, 2048)):
-        out, src = T.ac[:, a:b], T.x[:, 0:2056].indirect(T.offf[:, a // 16:b // 16])
+        out, src = T.ac[:, a:b], T.x[:, 0:2056].indirect(T.off[:, 128 + a // 16:128 + b // 16])
         if e == "v":
-            ka = op("v", [k, k_offf], lambda: V.tensor_copy(out, src))
+            ka = vc([k, k_offf], out, src)
         else:
             ka = op("s", [k, k_offf], lambda: S.activation(out, src, F.Copy))
         store(y, [ka], T.acc[:, a:b], out)

@@ -16,16 +16,15 @@ SCRATCH = {
     "us": ("sbuf", [128, 128], "uint8"),
     "gq": ("sbuf", [128, 512], "float8_e4m3fn_x4"),
     "gs": ("sbuf", [128, 512], "uint8"),
-    "ones": ("sbuf", [128, 128], "bfloat16"),
     "ident": ("sbuf", [128, 128], "bfloat16"),
     "et": ("sbuf", [128, 520], "bfloat16"),
     "eq": ("sbuf", [128, 512], "float8_e4m3fn_x4"),
     "es": ("sbuf", [128, 512], "uint8"),
     "pi": ("sbuf", [128, 16], "int32"),
     "p3": ("sbuf", [128, 16], "int32"),
-    "ic": ("sbuf", [128, 7], "int32"),
-    "fc": ("sbuf", [128, 7], "float32"),
-    "cc": ("sbuf", [128, 12], "float32"),
+    "ic": ("sbuf", [128, 6], "int32"),
+    "fc": ("sbuf", [128, 6], "float32"),
+    "cc": ("sbuf", [128, 7], "float32"),
     "uoff": ("sbuf", [128, 16], "uint16"),
     "j0": ("sbuf", [128, 64], "float32"),
     "jt": ("sbuf", [128, 64], "float32"),
@@ -45,14 +44,12 @@ SCRATCH = {
     "junk": ("sbuf", [128, 1024], "float32"),
     "sd": ("sbuf", [128, 4], "float32"),
     "cnt": ("sbuf", [128, 4], "float32"),
-    "z": ("sbuf", [128, 4], "float32"),
-    "r2": ("sbuf", [128, 4], "float32"),
     "ru": ("sbuf", [128, 4], "uint16"),
     "w": ("sbuf", [128, 512], "float32"),
     "t1": ("sbuf", [128, 128], "float32"),
     "y": ("sbuf", [128, 8], "float32"),
-    "lf": ("sbuf", [128, 36], "float32"),
     "lo": ("sbuf", [128, 4], "float32"),
+    "lf": ("sbuf", [128, 40], "float32"),
     "lown": ("sbuf", [128, 4], "uint16"),
     "xo": ("sbuf", [128, 32], "float32"),
     "to": ("sbuf", [128, 32], "float32"),
@@ -70,8 +67,8 @@ SCRATCH = {
     "scp": ("sbuf", [128, 64], "float32"),
     "ls": ("sbuf", [128, 32], "uint16"),
     "tb": ("sbuf", [128, 520], "float32"),
-    "got": ("sbuf", [128, 320], "float32"),
-    "run": ("sbuf", [128, 1152], "float32"),
+    "got": ("sbuf", [128, 256], "float32"),
+    "run": ("sbuf", [128, 1408], "float32"),
     "zz": ("sbuf", [128, 64], "float32"),
     "ex": ("sbuf", [128, 256], "float32"),
     "tx": ("sbuf", [128, 256], "float32"),
@@ -80,12 +77,15 @@ SCRATCH = {
     "ac": ("sbuf", [128, 2048], "float32"),
     "ps": ("psum", [128, 4096], "float32"),
 }
-ORDER = [("scores", 0), ("scores", 1), ("sizes", 0), ("col", 0, "v"), ("col", 1, "v"), ("scores", 2), ("signs", 0), ("sizes", 1),
+PIECES = ((0, 256), (256, 384), (384, 512))
+ORDER = [("scores", 0), ("scores", 1), ("fill", 1), ("scores", 2), ("fill", 1), ("sizes", 0), ("col", 0, "v"), ("col", 1, "v"), ("signs", 0), ("sizes", 1),
          ("col", 2, "s"), ("signs", 1), ("beats", 0, 1), ("beats", 1, 0), ("sizes", 2), ("col", 3, "s"), ("beats", 2, 0, 2),
          ("beats", 1, 2, 2), ("beats", 0, 2, 2), ("signs", 2), ("signs", 3), ("beats", 3, 0, 3), ("total", 2), ("total", 1),
          ("total", 0), ("total", 3), ("equals", 0), ("equals", 1), ("beats", 2, 3), ("running", 0), ("equals", 2), ("running", 1),
-         ("equals", 3), ("running", 2), ("running", 3)]
-SEMAPHORES = ["qv", "qs", "qt", "qp", "lu", "l0", "l1", "l2", "st", "ll", "lr", "cl", "cr", "cp", "loc"]
+         ("equals", 3), ("running", 2), ("place", 0), ("running", 3), ("place", 1), ("place", 2), ("place", 3)]
+ER_FIRST = 6
+STORES = (("v", "y", 0, 192), ("s", "y", 192, 512), ("v", "y", 512, 1280), ("s", "s", 1280, 2048))
+SEMAPHORES = ["qv", "qs", "qt", "qp", "lu", "l0", "l1", "l2", "l3", "st", "ll", "lr", "cl", "cr", "cp", "cq", "loc"]
 
 
 def rank_program(g, core, T, topo):
@@ -130,6 +130,9 @@ def rank_program(g, core, T, topo):
     def bank(b, n):
         return T.ps[:, 512 * b:512 * b + n]
 
+    def blk(t, j, n=1):
+        return t[:, 128 * j:128 * (j + n)]
+
     def vs(deps, out, in0, s1, op0, s2=None, op1=None):
         if op1 is None:
             return op("v", deps, lambda: V.tensor_scalar(out=out, in0=in0, scalar1=s1, scalar2=None, op0=op0))
@@ -141,20 +144,35 @@ def rank_program(g, core, T, topo):
     def vc(deps, out, in_):
         return op("v", deps, lambda: V.tensor_copy(out, in_))
 
+    def vm(out, value):
+        return op("v", [], lambda: V.memset(out, value))
+
+    def turn(deps, out, in_):
+        return op("v", deps, lambda: V.transpose(out, in_))
+
     def sa(deps, out, in_, scale=1.0, bias=0.0):
         return op("s", deps, lambda: S.activation(out, in_, F.Identity, bias=bias, scale=scale))
 
-    pieces = ((0, 256), (256, 384), (384, 512))
+    def sc(deps, out, in_):
+        return op("s", deps, lambda: S.activation(out, in_, F.Copy))
+
+    spare, made = [], {}
+
+    def fill(n=1):
+        for _ in range(min(n, len(spare))):
+            name, call = spare.pop(0)
+            made[name] = call()
+
     lu = load("s", T.uc[:, 0:16], T.u[:, 0:16], "lu")
-    lg = [load("y", T.grt[:, 4 * a:4 * b], T.gr[:, 4 * a:4 * b], "l%d" % i) for i, (a, b) in enumerate(pieces)]
+    lg = [load("y", T.grt[:, 4 * a:4 * b], T.gr[:, 4 * a:4 * b], "l%d" % i) for i, (a, b) in enumerate(PIECES)]
 
     own = 4 * rank
 
     def whole(out, pattern, base=0):
         return op("p", [], lambda: g.iota(out, pattern, base, 0, allow_small_or_imprecise_dtypes=True))
     k_pi = op("p", [], lambda: g.iota(T.pi[:, 0:16], [[0, 16]], 0, 1))
-    k_ones = op("v", [], lambda: V.memset(T.ones[:, :], 1.0))
-    k_id = op("p", [k_ones], lambda: g.affine_select(T.ident[:, :], T.ones[:, :], [[-1, 128]], A.is_equal, 0.0, 0, 1))
+    k_ones = vm(blk(T.keep, 0), 1.0)
+    k_id = op("p", [k_ones], lambda: g.affine_select(T.ident[:, :], blk(T.keep, 0), [[-1, 128]], A.is_equal, 0.0, 0, 1))
     k_j0 = whole(T.j0[:, :], [[128, 4], [1, 16]])
     whole(T.e0[:, 0:8], [[4, 4], [0, 2]], 16)
     whole(T.e0[:, 8:16], [[1, 4], [0, 2]])
@@ -163,62 +181,65 @@ def rank_program(g, core, T, topo):
     whole(T.n0[:, 0:128], [[0, 8], [1, 16]])
     k_n0 = whole(T.n0[:, 128:256], [[0, 4], [1, 32]])
 
-    k_et = op("v", [], lambda: V.memset(T.et[:, :], 0.0))
-    k_kp = op("v", [], lambda: V.memset(T.keep[:, 0:128], 1.0))
+    k_et = vm(T.et[:, :], 0.0)
     k_p3 = vs([k_pi], T.p3[:, :], T.pi[:, :], 3, A.bitwise_and)
-    names = {"b": 3, "k4": 12, "g16": 112, "m": 15, "r": 31, "a32": 96, "h16": 16}
+    parts = {"b": 3, "k4": 12, "g16": 112, "m": 15, "r": 31, "a32": 96}
     col = {}
-    for i, name in enumerate(names):
-        k_ic = vs([k_pi], T.ic[:, i:i + 1], T.pi[:, 0:1], names[name], A.bitwise_and)
+    for i, name in enumerate(parts):
+        k_ic = vs([k_pi], T.ic[:, i:i + 1], T.pi[:, 0:1], parts[name], A.bitwise_and)
         col[name] = T.fc[:, i:i + 1]
     k_uoff = vc([k_p3], T.uoff[:, :], T.p3[:, :])
+    k_w = vm(T.w[:, 0:64], 0.0)
     k_fc = vc([k_ic], T.fc[:, :], T.ic[:, :])
-    k_w = op("v", [], lambda: V.memset(T.w[:, 0:64], 0.0))
-    k = vs([k_id], T.keep[:, 128:256], T.ident[:, :], -2.0, A.mult, 1.0, A.add)
+    k_kp = vs([k_id], blk(T.keep, 1), T.ident[:, :], -2.0, A.mult, 1.0, A.add)
+    k_h0 = vm(T.h[:, 256:512], 0.0)
     k_jt = vs([k_j0, k_fc], T.jt[:, :], T.j0[:, :], col["g16"], A.add)
-    k_kp = op("v", [k, k_kp], lambda: V.memset(T.keep[:, 128:129], 0.0))
-    k_e = op("s", [k_id, k_et], lambda: S.activation(T.et[:, 3:515:4], T.ident[:, :], F.Copy))
-
-    def pack_ones(b):
-        return op("v", [k_e], lambda: V.quantize_mx(T.eq[:, 128 * b:128 * b + 128], T.es[:, 128 * b:128 * b + 128], T.et[:, 3 - b:515 - b]))
-    k_eqz = [pack_ones(b) for b in (0, 1)]
-    k_h0 = op("v", [], lambda: V.memset(T.h[:, 256:512], 0.0))
-    k_none = op("v", [], lambda: V.memset(T.lf[:, NONE:NONE + 4], 512.0))
-    k_x0 = op("v", [], lambda: V.memset(T.x[:, 0:8], 0.0))
+    k_e = sc([k_id, k_et], T.et[:, 3:515:4], T.ident[:, :])
 
     def small(i, deps, in_, scale, bias):
         return T.cc[:, i:i + 1], sa(deps, T.cc[:, i:i + 1], in_, scale, bias)
     c_k, k_ck = small(0, [k_fc], col["k4"], 0.25, 0.0)
-    c_back16, k_b16 = small(1, [k_fc], col["m"], STEP, -15 * STEP)
-    c_back32, k_b32 = small(2, [k_fc], col["r"], STEP, -31 * STEP)
-    c_base, k_base = small(3, [k_fc], col["a32"], 16 * UNIT, 0.0)
-    c_b, k_cb = small(4, [k_fc], col["b"], 1.0, -float(NONE))
-    c_t, k = small(5, [k_cb], col["h16"], 0.25, c_b)
-    c_u, k_cu = small(6, [k_cb], col["a32"], 0.25, c_b)
-    c_later, k_later = small(7, [k], col["k4"], 2.0, c_t)
+    c_t, k = small(1, [k_fc], col["g16"], 0.25, col["b"])
+    c_back16, k_b16 = small(2, [k_fc], col["m"], STEP, -15 * STEP)
+    c_back32, k_b32 = small(3, [k_fc], col["r"], STEP, -31 * STEP)
+    c_base, k_base = small(4, [k_fc], col["a32"], 16 * UNIT, 0.0)
+    c_later, k_later = small(5, [k], col["k4"], 2.0, c_t)
 
+    for b in range(4):
+        spare.append(("ones%d" % b, lambda b=b: op("v", [k_e], lambda: V.quantize_mx(blk(T.eq, b), blk(T.es, b), T.et[:, 3 - b:515 - b]))))
+    spare.extend([
+        ("own", lambda: vs([k_e0, k_ck], T.eo[:, 16:18], T.e0[:, 16:18], c_k, A.add)),
+        ("none", lambda: vm(T.lf[:, NONE:NONE + 8], 512.0)),
+        ("x0", lambda: vm(T.x[:, 0:8], 0.0)),
+        ("pad", lambda: vm(T.run[:, 543:896:32], 0.0)),
+        ("first", lambda: vs([k_fc], T.cc[:, 6:7], col["r"], 4.0, A.is_lt, float(NONE), A.mult)),
+        ("sel0", lambda: vs([k_fc], T.selo[:, 0:1], col["a32"], 0.25, A.mult, col["m"], A.add)),
+        ("sel1", lambda: vs([made["first"], k_later], T.selo[:, 1:2], c_later, float(NONE), A.min, T.cc[:, 6:7], A.max)),
+        ("before", lambda: vs([k_e0, k_ck], T.eo[:, 0:8], T.e0[:, 0:8], c_k, A.add)),
+        ("last", lambda: vs([k_e0, k_fc], T.eo[:, 8:16], T.e0[:, 8:16], col["k4"], A.add)),
+        ("step16", lambda: vs([k_n0, k_fc], blk(T.stp, 0), blk(T.n0, 0), col["m"], A.not_equal, STEP - 1.0, A.add)),
+        ("step32", lambda: vs([k_n0, k_fc], blk(T.stp, 1), blk(T.n0, 1), col["r"], A.not_equal, STEP - 1.0, A.add)),
+    ])
+
+    fill(2)
     k_ut = [vc([lu, k_uoff], T.ut[:, 0:256], T.uc[:, 0:16].indirect(T.uoff[:, 0:16])),
-            op("s", [lu, k_uoff], lambda: S.activation(T.ut[:, 256:512], T.uc[:, 0:16].indirect(T.uoff[:, 0:16]), F.Copy))]
+            sc([lu, k_uoff], T.ut[:, 256:512], T.uc[:, 0:16].indirect(T.uoff[:, 0:16]))]
     k_uq = op("v", k_ut, lambda: V.quantize_mx(T.uq[:, 0:128], T.us[:, 0:128], T.ut[:, 0:512]))
-    k_eqz.append(pack_ones(2))
     k_tb = sa([k_e], T.tb[:, :], T.et[:, :], 0.0)
     k_val = sa([k_v0, k_base], T.val[:, :], T.v0[:, :], UNIT, c_base)
 
     k_abs, k_scol, k_sc, k_row = {}, {}, {}, {}
 
     def scores(i):
-        a, b = pieces[i]
+        a, b = PIECES[i]
         kq = op("v", [lg[i]], lambda: V.quantize_mx(T.gq[:, a:b], T.gs[:, a:b], T.grt[:, 4 * a:4 * b]))
-        row = bank((0, 5, 6)[i], b - a)
+        row = bank((0, 5, 6, 7)[i], b - a)
         k_row[i] = (op("t", [k_uq, kq], lambda: g.tensor.matmul_mx(row, T.uq[:, 0:128], T.us[:, 0:128], T.gq[:, a:b], T.gs[:, a:b], True, True)), row)
         for q in range(a // 128, b // 128):
-            k_sc[q] = op("t", [k_uq, kq], lambda: g.tensor.matmul_mx(
-                bank(1 + q, 128), T.gq[:, 128 * q:128 * q + 128], T.gs[:, 128 * q:128 * q + 128], T.uq[:, 0:128], T.us[:, 0:128], True, True))
-        if i == 0:
-            k_eqz.append(pack_ones(3))
+            k_sc[q] = op("t", [k_uq, kq], lambda: g.tensor.matmul_mx(bank(1 + q, 128), blk(T.gq, q), blk(T.gs, q), T.uq[:, 0:128], T.us[:, 0:128], True, True))
 
     def sizes(i):
-        a, b = pieces[i]
+        a, b = PIECES[i]
         k = op("s", [k_row[i][0]], lambda: S.activation(T.sabs[:, a:b], k_row[i][1], F.Abs))
         for j in range(a // 128, b // 128):
             k_abs[j] = k
@@ -228,14 +249,11 @@ def rank_program(g, core, T, topo):
             k_scol[q] = op("v", [k_sc[q]], lambda: V.tensor_reduce(T.scol[:, q:q + 1], bank(1 + q, 1), AX, A.max, apply_absolute_value=True))
         else:
             k_scol[q] = op("s", [k_sc[q]], lambda: S.activation(T.scol[:, q:q + 1], bank(1 + q, 1), F.Abs))
-
-    def blk(t, j, n=1):
-        return t[:, 128 * j:128 * (j + n)]
-    k_b, k_sg, k_cnt, k_ts = {q: {} for q in range(4)}, {}, {}, {}
+    k_b, k_sg, k_cnt, k_ts, k_ru = {q: {} for q in range(4)}, {}, {}, {}, []
 
     def beats(q, j, n=1):
         at = 4 * q + j - (j > q)
-        k = vs([k_abs[i] for i in range(j, j + n)] + [k_scol[q]], blk(T.cmp, at, n), blk(T.sabs, j, n), T.scol[:, q:q + 1], A.is_ge if j < q else A.is_gt, -512.0, A.mult)
+        k = vs([k_abs[i] for i in range(j, j + n)] + [k_scol[q]], blk(T.cmp, at, n), blk(T.sabs, j, n), T.scol[:, q:q + 1], A.is_ge if j < q else A.is_gt, 0.5, A.add)
         for i in range(n):
             k_b[q][at + i - 4 * q] = k
 
@@ -243,33 +261,38 @@ def rank_program(g, core, T, topo):
         k_sg[q] = op("s", [k_abs[q], k_scol[q]], lambda: S.activation(blk(T.sg, q), blk(T.sabs, q), F.Sign, bias=T.scol[:, q:q + 1], scale=-1.0, accum_out=T.sd[:, q:q + 1]))
 
     def equals(q):
-        k_b[q][3] = vs([k_sg[q]], blk(T.cmp, 4 * q + 3), blk(T.sg, q), 0.0, A.is_equal, 256.0, A.mult)
+        k_b[q][3] = vs([k_sg[q]], blk(T.cmp, 4 * q + 3), blk(T.sg, q), 0.0, A.is_equal, 0.5, A.mult)
 
     def total(q):
-        k_cnt[q] = op("s", [k_b[q][0], k_b[q][1], k_sg[q]], lambda: S.activation(blk(T.junk, 2 * q, 2), blk(T.cmp, 4 * q, 2), F.Identity, bias=T.sd[:, q:q + 1], accum_out=T.cnt[:, q:q + 1]))
+        k_cnt[q] = op("s", [k_b[q][0], k_b[q][1], k_sg[q]], lambda: S.activation(
+            blk(T.junk, 2 * q, 2), blk(T.cmp, 4 * q, 2), F.Identity, bias=T.sd[:, q:q + 1], scale=-512.0, accum_out=T.cnt[:, q:q + 1]))
 
     def running(q):
-        k_ts[q] = op("v", [k_b[q][2], k_b[q][3], k_kp], lambda: V.tensor_tensor_scan(blk(T.ts, 2 * q, 2), T.keep[:, :], blk(T.cmp, 4 * q + 2, 2), 0.0, A.mult, A.add))
+        k_ts[q] = op("v", [k_b[q][2], k_b[q][3], k_kp], lambda: V.tensor_tensor_scan(blk(T.ts, 2 * q, 2), T.keep[:, :], blk(T.cmp, 4 * q + 2, 2), -128.0, A.mult, A.add))
 
-    steps = {"scores": scores, "sizes": sizes, "col": column_score, "beats": beats, "signs": signs, "equals": equals, "total": total, "running": running}
+    def place(q):
+        k_ru.append(vs([k_ts[q], k_cnt[q]], T.ru[:, q:q + 1], T.cnt[:, q:q + 1], -1.0 / 512, A.mult, T.ts[:, 256 * q + 255:256 * q + 256], A.subtract))
+
+    steps = {"scores": scores, "sizes": sizes, "col": column_score, "beats": beats, "signs": signs, "equals": equals, "total": total,
+             "running": running, "place": place, "fill": fill}
     for step in ORDER:
         steps[step[0]](*step[1:])
-    k = vt(list(k_ts.values()), T.z[:, :], T.ts[:, 127:1024:256], T.ts[:, 255:1024:256], A.add)
-    k = vt([k] + list(k_cnt.values()), T.r2[:, :], T.z[:, :], T.cnt[:, :], A.add)
-    k_ru = vs([k], T.ru[:, :], T.r2[:, :], -1.0 / 512, A.mult, 64.0, A.add)
-    k_eo = vs([k_e0, k_ck], T.eo[:, 16:18], T.e0[:, 16:18], c_k, A.add)
     k_abs, k_scol = list(k_abs.values()), list(k_scol.values())
 
-    k_c1 = op("s", lg, lambda: S.activation(T.e32[:, 0:1280], T.grt[:, 0:1280], F.Copy))
+    k_c1 = sc(lg, T.e32[:, 0:1280], T.grt[:, 0:1280])
 
-    def across(deps, src, half, out, how):
-        kh = [vt(deps, half(a, 64), src(a, 64), src(64 - a, 64), how) for a in (0, 64)]
-        return [vt(kh, out(a, 32), half(a, 32), half(a ^ 32, 32), how) for a in (0, 32, 64, 96)]
-    k = vc([k_w, k_jt, k_ru], T.w[:, 0:512].indirect(T.ru[:, 0:4]), T.jt[:, 0:64])
+    fill()
+    k = vc([k_w, k_jt] + k_ru, T.w[:, 0:512].indirect(T.ru[:, 0:4]), T.jt[:, 0:64])
+    fill()
     k = vc([k], T.w[:, 64:128], T.w[:, 0:64])
-    kt = [op("v", [k], lambda: V.transpose(T.t1[:, 32 * c:32 * c + 32], T.w[:, c:128:4])) for c in range(4)]
-    k = vt(kt, T.y[:, 0:4], T.t1[:, 0:128:32], T.t1[:, 16:128:32], A.add)
-    k_lf = across([k], lambda a, n: T.y[a:a + n, 0:4], lambda a, n: T.y[a:a + n, 4:8], lambda a, n: T.lo[a:a + n, 0:4], A.add)
+    fill()
+    k = [turn([k], T.t1[:, 32 * c:32 * c + 32], T.w[:, c:128:4]) for c in range(4)]
+    fill()
+    k = vt(k, T.y[:, 0:4], T.t1[:, 0:128:32], T.t1[:, 16:128:32], A.add)
+    fill()
+    k = [vt([k], T.y[a:a + 64, 4:8], T.y[a:a + 64, 0:4], T.y[64 - a:128 - a, 0:4], A.add) for a in (0, 64)]
+    fill()
+    k_lo = [vt(k, T.lo[a:a + 32, :], T.y[a:a + 32, 4:8], T.y[a ^ 32:(a ^ 32) + 32, 4:8], A.add) for a in (0, 32, 64, 96)]
 
     far_e = topo.engines(core, T.cores[far[0]])
     near_e = [e for e in topo.engines(core, T.cores[near_others[0]]) if e not in far_e]
@@ -290,17 +313,23 @@ def rank_program(g, core, T, topo):
             RemoteDMATransfer(dst_ids=ids(near_others), dma_engine_mask=near_mask, remote_sem=T.sem[near_sem], srcs=[src], dsts=[near_dst(r) for r in near_others]),
         ], local_sem=T.sem["loc"])
 
-    send(k_lf, T.lo[:, 0:4], lambda r: T.lf[:, own:own + 4], lambda r: T.lf[:, own:own + 4], "ll", "lr")
+    send(k_lo, T.lo[:, :], lambda r: T.lf[:, own:own + 4], lambda r: T.lf[:, own:own + 4], "ll", "lr")
     ll = ("ll", len(near_others) * len(near_e))
     lr = ("lr", len(far) * len(far_e))
 
-    k = vc(k_lf + [k_eo], T.xo[:, :], T.lo[:, 0:4].indirect(T.eo[:, 16:18]))
-    k = op("v", [k], lambda: V.transpose(T.to[:, :], T.xo[:, :]))
+    fill()
+    k = vc(k_lo + [made["own"]], T.xo[:, :], T.lo[:, :].indirect(T.eo[:, 16:18]))
+    k_lown = vc(k_lo, T.lown[:, :], T.lo[:, :])
+    k = turn([k], T.to[:, :], T.xo[:, :])
+    k_lf = vc(k_lo, T.lf[:, own:own + 4], T.lo[:, :])
     k_ou = vs([k], T.ou[:, :], T.to[:, 0:16], 4.0, A.mult, col["b"], A.add)
-    k_h = [op("s", [k_ou] + lg, lambda: S.activation(T.h[:, 128:256], T.grt[:, 0:2048].indirect(T.ou[:, 8:16]), F.Copy)),
+    fill()
+    k_h = [sc([k_ou] + lg, T.h[:, 128:256], T.grt[:, 0:2048].indirect(T.ou[:, 8:16])),
            vc([k_ou] + lg, T.h[:, 0:128], T.grt[:, 0:2048].indirect(T.ou[:, 0:8]))]
+    fill()
     k_hq = op("v", k_h + [k_h0], lambda: V.quantize_mx(T.hq[:, 0:128], T.hs[:, 0:128], T.h[:, 0:512]))
-    k_c0 = op("s", lg, lambda: S.activation(T.e32[:, 1280:2048], T.grt[:, 1280:2048], F.Copy))
+    k_c0 = sc(lg, T.e32[:, 1280:2048], T.grt[:, 1280:2048])
+    fill(len(spare))
 
     fa = 64 * near.index(rank)
     partner = [far[near.index(rank)]]
@@ -309,66 +338,44 @@ def rank_program(g, core, T, topo):
          lambda r: T.qr[:, fa:fa + 64].bitcast(dt.uint8), "cl", "cp", partner)
     send([k_hq], T.hs[:, 0:64],
          lambda r: T.pl[:, 64 * near_at(r):64 * near_at(r) + 64],
-         lambda r: T.pr[:, fa:fa + 64], "cl", "cp", partner)
+         lambda r: T.pr[:, fa:fa + 64], "cl", "cq", partner)
     cl = ("cl", 2 * len(near_others) * len(near_e))
-    cp = ("cp", 2 * len(far_e))
-    need("p", [cp])
-    for piece in (T.qr[:, fa:fa + 64].bitcast(dt.uint8), T.pr[:, fa:fa + 64]):
+    cp = [("cp", len(far_e)), ("cq", len(far_e))]
+    for arrived, piece in zip(cp, (T.qr[:, fa:fa + 64].bitcast(dt.uint8), T.pr[:, fa:fa + 64])):
+        need("p", [arrived])
         g.remote_dma_fused([RemoteDMATransfer(dst_ids=ids(near_others), dma_engine_mask=far_mask + near_mask, remote_sem=T.sem["cr"],
                                               srcs=[piece], dsts=[piece] * len(near_others))], local_sem=T.sem["loc"])
     cr = ("cr", 2 * len(near_others) * (len(far_e) + len(near_e)))
 
-    k1 = vs([k_fc], T.cc[:, 8:9], col["k4"], 8.0, A.mult, col["a32"], A.is_gt)
-    k2 = vs([k_fc], T.cc[:, 9:10], col["m"], col["h16"], A.subtract, 8.0, A.is_lt)
-    k3 = vs([k_fc], T.cc[:, 10:11], col["m"], 4.0, A.is_ge, 4.0, A.mult)
-    k_stp = [vs([k_n0, k_fc], T.stp[:, 0:128], T.n0[:, 0:128], col["m"], A.not_equal, STEP - 1.0, A.add),
-             vs([k_n0, k_fc], T.stp[:, 128:256], T.n0[:, 128:256], col["r"], A.not_equal, STEP - 1.0, A.add)]
-    k3 = vs([k3, k_cu], T.cc[:, 11:12], T.cc[:, 10:11], c_u, A.add)
-    k_eo = [vs([k_e0, k_ck], T.eo[:, 0:8], T.e0[:, 0:8], c_k, A.add), vs([k_e0, k_fc], T.eo[:, 8:16], T.e0[:, 8:16], col["k4"], A.add)]
-    k_selo = [vs([k1, k_later], T.selo[:, 1:2], c_later, T.cc[:, 8:9], A.mult, float(NONE), A.add),
-              vs([k2, k3], T.selo[:, 0:1], T.cc[:, 11:12], T.cc[:, 9:10], A.mult, float(NONE), A.add)]
-
     def unpack(b, to, q, s, a, n, deps):
-        return op("t", deps + [k_eqz[b]], lambda: g.tensor.matmul_mx(bank(to, n), T.eq[:, 128 * b:128 * b + 128], T.es[:, 128 * b:128 * b + 128], q[:, a:a + n], s[:, a:a + n], True, True))
+        return op("t", deps + [made["ones%d" % b]], lambda: g.tensor.matmul_mx(bank(to, n), blk(T.eq, b), blk(T.es, b), q[:, a:a + n], s[:, a:a + n], True, True))
 
     def xs(r, b, n):
         return T.x[:, 8 + 256 * r + b:8 + 256 * (r + n):4]
     k_own = [unpack(b, 4 + b, T.hq, T.hs, 0, 128, [k_hq] + k_scol + k_abs) for b in range(4)]
-    k_lown = vc(k_lf, T.lown[:, :], T.lo[:, 0:4])
-    k_lf = [vc(k_lf, T.lf[:, own:own + 4], T.lo[:, 0:4])]
     k_d = [vt([k_own[b]] + k_h, T.d[:, b:256:4], T.h[:, b:256:4], bank(4 + b, 64), A.subtract) for b in range(4)]
-    k_er = vc(k_d + [k_c0, k_c1, k_ou], T.e32[:, 0:2048].indirect(T.ou[:, 0:16]), T.d[:, 0:256])
-    k_xo = [op("s", [k_d[b]], lambda: S.activation(xs(rank, b, 1), bank(4 + b, 64), F.Copy)) for b in range(4)]
 
-    k_scg = op("s", [k_lown] + k_abs, lambda: S.activation(T.scg[:, :], T.sabs[:, 0:512].indirect(T.lown[:, 0:4]), F.Copy))
-    k_scp = [op("s", [k_scg], lambda: S.activation(T.scp[0:1, c:64:4], T.scg[0:1, 16 * c:16 * c + 16], F.Copy)) for c in range(4)]
-    store("y", k_scp, T.sc[:, :], T.scp[0:1, 0:64])
+    def put_er(a, b):
+        return vc(k_d + [k_c0, k_c1, k_ou, made["er"]], T.e32[:, 0:2048].indirect(T.ou[:, a:b]), T.d[:, 16 * a:16 * b])
+    made["er"] = k_ou
+    made["er"] = put_er(0, ER_FIRST)
+    spare.extend([("er", lambda a=a: put_er(a, a + 2)) for a in range(ER_FIRST, 16, 2)])
+    k_xo = [sc([k_d[b]], xs(rank, b, 1), bank(4 + b, 64)) for b in range(4)]
+
+    k = sc([k_lown] + k_abs, T.scg[:, :], T.sabs[:, 0:512].indirect(T.lown[:, 0:4]))
+    k = [sc([k], T.scp[0:1, c:64:4], T.scg[0:1, 16 * c:16 * c + 16]) for c in range(4)]
+    store("y", k, T.sc[:, :], T.scp[0:1, 0:64])
 
     table = T.tb[:, 0:520]
-    k_ls = vc([ll, lr, k_none] + k_lf + k_selo, T.ls[:, :], T.lf[:, 0:36].indirect(T.selo[:, 0:2]))
+    k_ls = vc([ll, lr, k_lf, made["none"], made["sel0"], made["sel1"]], T.ls[:, :], T.lf[:, 0:40].indirect(T.selo[:, 0:2]))
+    fill()
     k = vc([k_ls, k_tb, k_val], table.indirect(T.ls[:, 0:4]), T.val[:, 0:64])
-    k_g1 = vc([k], T.got[:, 256:320], table.indirect(T.ls[:, 8:12]))
+    fill()
+    k_g1 = vc([k], T.got[:, 0:64], table.indirect(T.ls[:, 16:20]))
+    fill()
     k_tab = vc([k_g1], table.indirect(T.ls[:, 4:8]), T.val[:, 64:128])
-    k_g2 = op("s", [k_tab], lambda: S.activation(T.got[:, 0:256], table.indirect(T.ls[:, 16:32]), F.Copy))
-
-    def pick(deps, out, step, in_):
-        return op("v", deps + k_stp, lambda: V.tensor_tensor_scan(out, step, in_, 0.0, A.add, A.max))
-    k_run = [pick([k_g1], T.run[:, 1025:1152:2], T.stp[:, 0:64], T.got[:, 256:320])]
-    k_run += [pick([k_tab], blk(T.run, c), T.stp[:, 128:256], T.tb[:, c:512:4]) for c in range(4)]
-    k_run += [pick([k_g2], T.run[:, 513 + 256 * i:768 + 256 * i:2], T.stp[:, 0:128], blk(T.got, i)) for i in range(2)]
-    k = [vc(k_run, T.run[32 * a:32 * a + 32, 543 + 128 * a:640 + 128 * a:32], T.run[32 * a:32 * a + 32, 1055:1152:32]) for a in range(4)]
-    k_zz = across(k, lambda a, n: T.run[a:a + n, 31:1024:32], lambda a, n: T.zz[a:a + n, 32:64], lambda a, n: T.zz[a:a + n, 0:32], A.max)
-    k = vs(k_zz + k_eo + [k_b16], T.ex[:, 0:128], T.zz[:, 0:32].indirect(T.eo[:, 0:8]), c_back16, A.add)
-
-    def wrapped(deps, a, lo):
-        k = op("v", deps, lambda: V.transpose(T.tx[:, a:a + 128], T.ex[:, a:a + 128]))
-        return vs([k], T.off[:, a + lo:a + 128], T.tx[:, a + lo:a + 128], 1.0 / UNIT, A.mult, col["b"], A.add)
-    k_offc = wrapped([k], 0, 16)
-
-    store("y", [k_er, left], T.er[:, 0:1024], T.e32[:, 0:1024])
-    store("y", [k_er, left], T.er[:, 1024:2048], T.e32[:, 1024:2048])
-    for s in range(N):
-        store("y", k_lf + [ll, lr], T.nb[s:s + 1, 0:64], T.lf[0:16, 4 * s:4 * s + 4])
+    fill()
+    k_g2 = sc([k_tab], T.got[:, 64:256], table.indirect(T.ls[:, 20:32]))
 
     k_near = [unpack(b, b, T.ql, T.pl, 0, 192, [cl] + k_abs + k_scol) for b in range(4)]
     k_v = []
@@ -376,29 +383,63 @@ def rank_program(g, core, T, topo):
         i = near.index(rank)
         for at, first, n in ((0, near[0], i), (i, rank + 1, len(near) - 1 - i)):
             if n:
-                k_v.append(op("s", [k_near[b]], lambda: S.activation(xs(first, b, n), T.ps[:, 512 * b + 64 * at:512 * b + 64 * (at + n)], F.Copy)))
-    k_far1 = [unpack(b, 4 + b, T.qr, T.pr, 0, 128, [cr, cp] + k_xo) for b in range(4)]
-    k_far2 = [unpack(b, b, T.qr, T.pr, 128, 128, [cr] + k_v) for b in range(4)]
-    k_v += k_xo
-    k_ready = {r: k_v for r in near}
-    k_fv1 = [op("s", [k_far1[b]], lambda: S.activation(xs(far[0], b, 2), bank(4 + b, 128), F.Copy)) for b in range(4)]
-    k_fv2 = [op("s", [k_far2[b]], lambda: S.activation(xs(far[2], b, 2), bank(b, 128), F.Copy)) for b in range(4)]
+                k_v.append(sc([k_near[b]], xs(first, b, n), T.ps[:, 512 * b + 64 * at:512 * b + 64 * (at + n)]))
+    k_far = [[unpack(b, 4 + b, T.qr, T.pr, 0, 128, [cr] + cp + k_xo) for b in range(4)],
+             [unpack(b, b, T.qr, T.pr, 128, 128, [cr] + k_v) for b in range(4)]]
+
+    def copy_far(i):
+        return [sc([k_far[i][b]], xs(far[2 * i], b, 2), bank(4 * (1 - i) + b, 128)) for b in range(4)]
+
+    def pick(deps, out, step, in_):
+        return op("v", deps + [made["step16"], made["step32"]], lambda: V.tensor_tensor_scan(out, step, in_, 0.0, A.add, A.max))
+    k_last = [pick([k_tab], blk(T.run, c), blk(T.stp, 1), T.tb[:, c:512:4]) for c in range(4)]
+    k_run = [pick([k_g1, k_g2], T.run[:, 897 + 256 * i:1152 + 256 * i:2], blk(T.stp, 0), blk(T.got, i)) for i in range(2)]
+    k = [vt(k_last, T.zz[a:a + 64, 32:48], T.run[a:a + 64, 31:512:32], T.run[64 - a:128 - a, 31:512:32], A.max) for a in (0, 64)]
+
+    def later(a):
+        return T.run[32 * a:32 * a + 32, 927 - 128 * a:1408 - 128 * a:32]
+    k += [vt(k_run + [made["pad"]], T.zz[32 * a:32 * a + 32, 48:64], later(a), later(a ^ 2), A.max) for a in range(4)]
+    k_zz = [vt(k, T.zz[a:a + 32, 0:32], T.zz[a:a + 32, 32:64], T.zz[a ^ 32:(a ^ 32) + 32, 32:64], A.max) for a in (0, 32, 64, 96)]
+    found = T.zz[:, 0:32]
+    k_ex = vs(k_zz + [made["before"], k_b16], T.ex[:, 0:64], found.indirect(T.eo[:, 0:4]), c_back16, A.add)
+    if far[0] == 0:
+        k_fv1 = copy_far(0)
+    k_ex2 = sa(k_zz + [made["before"], k_b16], T.ex[:, 64:128], found.indirect(T.eo[:, 4:8]), 1.0, c_back16)
+    k_ex3 = sa(k_zz + [made["last"], k_b32], T.ex[:, 128:256], found.indirect(T.eo[:, 8:16]), 1.0, c_back32)
+    if far[0] != 0:
+        k_fv1 = copy_far(0)
+    k_fv2 = copy_far(1)
+
+    def offsets(deps, a, b):
+        return vs(deps, T.off[:, a:b], T.tx[:, a:b], 1.0 / UNIT, A.mult, col["b"], A.add)
+    fill()
+    k = turn([k_ex], T.tx[:, 0:64], T.ex[:, 0:64])
+    fill()
+    k_off = offsets([k], 16, 64)
+    fill(len(spare))
+    k_er = made["er"]
+    spare.extend([
+        ("t1", lambda: turn([k_ex2], T.tx[:, 64:128], T.ex[:, 64:128])),
+        ("o1", lambda: offsets([made["t1"]], 64, 128)),
+        ("t2", lambda: turn([k_ex3], T.tx[:, 128:256], T.ex[:, 128:256])),
+        ("o2", lambda: offsets([made["t2"]], 128, 256)),
+    ])
+
+    store("y", [k_er, left], T.er[:, 0:1024], T.e32[:, 0:1024])
+    store("y", [k_er, left], T.er[:, 1024:2048], T.e32[:, 1024:2048])
+    for s in range(N):
+        store("y", [k_lf, ll, lr], T.nb[s:s + 1, 0:64], T.lf[0:16, 4 * s:4 * s + 4])
+
+    k_ready = {r: k_v + k_xo for r in near}
     for r in far:
         k_ready[r] = k_fv1 if r in far[:2] else k_fv2
-    k_last = sa(k_zz + k_eo + [k_b32], T.ex[:, 128:256], T.zz[:, 0:32].indirect(T.eo[:, 8:16]), 1.0, c_back32)
-
-    k = k_x0
+    k = made["x0"]
     for s in range(1, N):
         a = 8 + 256 * s
-        k = vt([k, k_offc, k_x0] + k_ready[s] + k_ready[0], T.x[:, a:a + 256], T.x[:, 0:a].indirect(T.off[:, 16 * s:16 * s + 16]), T.x[:, a:a + 256], A.add)
-        if s == N - 2:
-            k_offf = wrapped([k_last], 128, 0)
-    for e, y, a, b in (("v", "y", 0, 384), ("s", "y", 384, 768), ("v", "y", 768, 1408), ("s", "s", 1408, 2048)):
+        k = vt([k, k_off if s < 4 else made["o1"]] + k_ready[s] + k_ready[0], T.x[:, a:a + 256], T.x[:, 0:a].indirect(T.off[:, 16 * s:16 * s + 16]), T.x[:, a:a + 256], A.add)
+        fill()
+    for e, y, a, b in STORES:
         out, src = T.ac[:, a:b], T.x[:, 0:2056].indirect(T.off[:, 128 + a // 16:128 + b // 16])
-        if e == "v":
-            ka = vc([k, k_offf], out, src)
-        else:
-            ka = op("s", [k, k_offf], lambda: S.activation(out, src, F.Copy))
-        store(y, [ka], T.acc[:, a:b], out)
+        store(y, [(vc if e == "v" else sc)([k, made["o2"]], out, src)], T.acc[:, a:b], out)
 
     need("p", [("q" + e, count[e]) for e in "vstp"] + [("st", count["st"]), left])

@@ -37,8 +37,8 @@ SCRATCH = {
     "selo": ("sbuf", [128, 2], "uint16"),
     "sabs": ("sbuf", [128, 512], "float32"),
     "scol": ("sbuf", [128, 4], "float32"),
-    "sg": ("sbuf", [128, 512], "bfloat16"),
-    "keep": ("sbuf", [128, 256], "bfloat16"),
+    "sg": ("sbuf", [128, 1024], "bfloat16"),
+    "keep": ("sbuf", [128, 384], "bfloat16"),
     "ts": ("sbuf", [128, 1024], "bfloat16"),
     "cmp": ("sbuf", [128, 2048], "bfloat16"),
     "junk": ("sbuf", [128, 1024], "float32"),
@@ -77,14 +77,15 @@ SCRATCH = {
     "ac": ("sbuf", [128, 2048], "float32"),
     "ps": ("psum", [128, 4096], "float32"),
 }
-PIECES = ((0, 256), (256, 384), (384, 512))
-ORDER = [("scores", 0), ("scores", 1), ("fill", 1), ("scores", 2), ("fill", 1), ("sizes", 0), ("col", 0, "v"), ("col", 1, "v"), ("signs", 0), ("sizes", 1),
-         ("col", 2, "s"), ("signs", 1), ("beats", 0, 1), ("beats", 1, 0), ("sizes", 2), ("col", 3, "s"), ("beats", 2, 0, 2),
-         ("beats", 1, 2, 2), ("beats", 0, 2, 2), ("signs", 2), ("signs", 3), ("beats", 3, 0, 3), ("total", 2), ("total", 1),
-         ("total", 0), ("total", 3), ("equals", 0), ("equals", 1), ("beats", 2, 3), ("running", 0), ("equals", 2), ("running", 1),
-         ("equals", 3), ("running", 2), ("place", 0), ("running", 3), ("place", 1), ("place", 2), ("place", 3)]
-ER_FIRST = 6
-STORES = (("v", "y", 0, 192), ("s", "y", 192, 512), ("v", "y", 512, 1280), ("s", "s", 1280, 2048))
+ORDER = [("pack", 0), ("pack", "u"), ("scores", 0), ("pack", 1), ("scores", 1), ("fill", 2), ("pack", 2), ("scores", 2), ("fill", 1), ("pack", 3), ("scores", 3),
+         ("sizes", 0), ("col", 0), ("sizes", 1), ("col", 1), ("beats", 0, 1), ("beats", 1, 0),
+         ("sizes", 2), ("col", 2), ("signs", 0), ("beats", 0, 2), ("beats", 1, 2), ("beats", 2, 0, 2),
+         ("sizes", 3), ("col", 3), ("signs", 1), ("beats", 3, 0, 2), ("signs", 2), ("signs", 3),
+         ("total", 0), ("total", 1), ("total", 2), ("total", 3),
+         ("equals", 0), ("beats", 0, 3), ("equals", 1), ("beats", 1, 3), ("running", 0), ("equals", 2), ("running", 1), ("equals", 3),
+         ("place", 0), ("running", 2), ("place", 1), ("running", 3), ("place", 2), ("place", 3)]
+ER_FIRST = 4
+STORES = (("v", "y", 0, 96), ("s", "y", 96, 320), ("v", "y", 320, 704), ("s", "y", 704, 1216), ("v", "y", 1216, 1760), ("s", "s", 1760, 2048))
 SEMAPHORES = ["qv", "qs", "qt", "qp", "lu", "l0", "l1", "l2", "l3", "st", "ll", "lr", "cl", "cr", "cp", "cq", "loc"]
 
 
@@ -164,7 +165,7 @@ def rank_program(g, core, T, topo):
             made[name] = call()
 
     lu = load("s", T.uc[:, 0:16], T.u[:, 0:16], "lu")
-    lg = [load("y", T.grt[:, 4 * a:4 * b], T.gr[:, 4 * a:4 * b], "l%d" % i) for i, (a, b) in enumerate(PIECES)]
+    lg = [load("y", blk(T.grt, 4 * q, 4), blk(T.gr, 4 * q, 4), "l%d" % q) for q in range(4)]
 
     own = 4 * rank
 
@@ -181,6 +182,8 @@ def rank_program(g, core, T, topo):
     whole(T.n0[:, 0:128], [[0, 8], [1, 16]])
     k_n0 = whole(T.n0[:, 128:256], [[0, 4], [1, 32]])
 
+    k_tb = whole(T.tb[:, :], [[0, 520]])
+
     k_et = vm(T.et[:, :], 0.0)
     k_p3 = vs([k_pi], T.p3[:, :], T.pi[:, :], 3, A.bitwise_and)
     parts = {"b": 3, "k4": 12, "g16": 112, "m": 15, "r": 31, "a32": 96}
@@ -189,10 +192,10 @@ def rank_program(g, core, T, topo):
         k_ic = vs([k_pi], T.ic[:, i:i + 1], T.pi[:, 0:1], parts[name], A.bitwise_and)
         col[name] = T.fc[:, i:i + 1]
     k_uoff = vc([k_p3], T.uoff[:, :], T.p3[:, :])
+    vm(blk(T.keep, 2), 1.0)
     k_w = vm(T.w[:, 0:64], 0.0)
     k_fc = vc([k_ic], T.fc[:, :], T.ic[:, :])
     k_kp = vs([k_id], blk(T.keep, 1), T.ident[:, :], -2.0, A.mult, 1.0, A.add)
-    k_h0 = vm(T.h[:, 256:512], 0.0)
     k_jt = vs([k_j0, k_fc], T.jt[:, :], T.j0[:, :], col["g16"], A.add)
     k_e = sc([k_id, k_et], T.et[:, 3:515:4], T.ident[:, :])
 
@@ -205,50 +208,46 @@ def rank_program(g, core, T, topo):
     c_base, k_base = small(4, [k_fc], col["a32"], 16 * UNIT, 0.0)
     c_later, k_later = small(5, [k], col["k4"], 2.0, c_t)
 
-    for b in range(4):
-        spare.append(("ones%d" % b, lambda b=b: op("v", [k_e], lambda: V.quantize_mx(blk(T.eq, b), blk(T.es, b), T.et[:, 3 - b:515 - b]))))
+    def ones(b):
+        return "ones%d" % b, lambda: op("v", [k_e], lambda: V.quantize_mx(blk(T.eq, b), blk(T.es, b), T.et[:, 3 - b:515 - b]))
     spare.extend([
+        ones(0), ones(1), ones(2),
         ("own", lambda: vs([k_e0, k_ck], T.eo[:, 16:18], T.e0[:, 16:18], c_k, A.add)),
         ("none", lambda: vm(T.lf[:, NONE:NONE + 8], 512.0)),
+        ones(3),
+        ("step16", lambda: vs([k_n0, k_fc], blk(T.stp, 0), blk(T.n0, 0), col["m"], A.not_equal, STEP - 1.0, A.add)),
+        ("step32", lambda: vs([k_n0, k_fc], blk(T.stp, 1), blk(T.n0, 1), col["r"], A.not_equal, STEP - 1.0, A.add)),
+        ("h0", lambda: vm(T.h[:, 256:512], 0.0)),
         ("x0", lambda: vm(T.x[:, 0:8], 0.0)),
-        ("pad", lambda: vm(T.run[:, 543:896:32], 0.0)),
         ("first", lambda: vs([k_fc], T.cc[:, 6:7], col["r"], 4.0, A.is_lt, float(NONE), A.mult)),
         ("sel0", lambda: vs([k_fc], T.selo[:, 0:1], col["a32"], 0.25, A.mult, col["m"], A.add)),
         ("sel1", lambda: vs([made["first"], k_later], T.selo[:, 1:2], c_later, float(NONE), A.min, T.cc[:, 6:7], A.max)),
         ("before", lambda: vs([k_e0, k_ck], T.eo[:, 0:8], T.e0[:, 0:8], c_k, A.add)),
         ("last", lambda: vs([k_e0, k_fc], T.eo[:, 8:16], T.e0[:, 8:16], col["k4"], A.add)),
-        ("step16", lambda: vs([k_n0, k_fc], blk(T.stp, 0), blk(T.n0, 0), col["m"], A.not_equal, STEP - 1.0, A.add)),
-        ("step32", lambda: vs([k_n0, k_fc], blk(T.stp, 1), blk(T.n0, 1), col["r"], A.not_equal, STEP - 1.0, A.add)),
+        ("pad", lambda: vm(T.run[:, 543:896:32], 0.0)),
     ])
 
-    fill(2)
+    fill(3)
     k_ut = [vc([lu, k_uoff], T.ut[:, 0:256], T.uc[:, 0:16].indirect(T.uoff[:, 0:16])),
             sc([lu, k_uoff], T.ut[:, 256:512], T.uc[:, 0:16].indirect(T.uoff[:, 0:16]))]
-    k_uq = op("v", k_ut, lambda: V.quantize_mx(T.uq[:, 0:128], T.us[:, 0:128], T.ut[:, 0:512]))
-    k_tb = sa([k_e], T.tb[:, :], T.et[:, :], 0.0)
-    k_val = sa([k_v0, k_base], T.val[:, :], T.v0[:, :], UNIT, c_base)
 
-    k_abs, k_scol, k_sc, k_row = {}, {}, {}, {}
+    k_q, k_abs, k_scol, k_sc, k_row = {}, {}, {}, {}, {}
 
-    def scores(i):
-        a, b = PIECES[i]
-        kq = op("v", [lg[i]], lambda: V.quantize_mx(T.gq[:, a:b], T.gs[:, a:b], T.grt[:, 4 * a:4 * b]))
-        row = bank((0, 5, 6, 7)[i], b - a)
-        k_row[i] = (op("t", [k_uq, kq], lambda: g.tensor.matmul_mx(row, T.uq[:, 0:128], T.us[:, 0:128], T.gq[:, a:b], T.gs[:, a:b], True, True)), row)
-        for q in range(a // 128, b // 128):
-            k_sc[q] = op("t", [k_uq, kq], lambda: g.tensor.matmul_mx(bank(1 + q, 128), blk(T.gq, q), blk(T.gs, q), T.uq[:, 0:128], T.us[:, 0:128], True, True))
-
-    def sizes(i):
-        a, b = PIECES[i]
-        k = op("s", [k_row[i][0]], lambda: S.activation(T.sabs[:, a:b], k_row[i][1], F.Abs))
-        for j in range(a // 128, b // 128):
-            k_abs[j] = k
-
-    def column_score(q, e):
-        if e == "v":
-            k_scol[q] = op("v", [k_sc[q]], lambda: V.tensor_reduce(T.scol[:, q:q + 1], bank(1 + q, 1), AX, A.max, apply_absolute_value=True))
+    def pack(q):
+        if q == "u":
+            k_q[q] = op("v", k_ut, lambda: V.quantize_mx(T.uq[:, :], T.us[:, :], T.ut[:, :]))
         else:
-            k_scol[q] = op("s", [k_sc[q]], lambda: S.activation(T.scol[:, q:q + 1], bank(1 + q, 1), F.Abs))
+            k_q[q] = op("v", [lg[q]], lambda: V.quantize_mx(blk(T.gq, q), blk(T.gs, q), blk(T.grt, 4 * q, 4)))
+
+    def scores(q):
+        k_row[q] = op("t", [k_q["u"], k_q[q]], lambda: g.tensor.matmul_mx(bank(4 + q, 128), T.uq[:, :], T.us[:, :], blk(T.gq, q), blk(T.gs, q), True, True))
+        k_sc[q] = op("t", [k_q["u"], k_q[q]], lambda: g.tensor.matmul_mx(bank(q, 128), blk(T.gq, q), blk(T.gs, q), T.uq[:, :], T.us[:, :], True, True))
+
+    def sizes(q):
+        k_abs[q] = op("s", [k_row[q]], lambda: S.activation(blk(T.sabs, q), bank(4 + q, 128), F.Abs))
+
+    def column_score(q):
+        k_scol[q] = op("s", [k_sc[q]], lambda: S.activation(T.scol[:, q:q + 1], bank(q, 1), F.Abs))
     k_b, k_sg, k_cnt, k_ts, k_ru = {q: {} for q in range(4)}, {}, {}, {}, []
 
     def beats(q, j, n=1):
@@ -258,30 +257,33 @@ def rank_program(g, core, T, topo):
             k_b[q][at + i - 4 * q] = k
 
     def signs(q):
-        k_sg[q] = op("s", [k_abs[q], k_scol[q]], lambda: S.activation(blk(T.sg, q), blk(T.sabs, q), F.Sign, bias=T.scol[:, q:q + 1], scale=-1.0, accum_out=T.sd[:, q:q + 1]))
+        j, n = (q, 1) if q < 2 else (2, 2)
+        k_sg[q] = op("s", [k_abs[j], k_abs[j + n - 1], k_scol[q]], lambda: S.activation(
+            blk(T.sg, 2 * q, n), blk(T.sabs, j, n), F.Sign, bias=T.scol[:, q:q + 1], scale=-1.0, accum_out=T.sd[:, q:q + 1]))
 
     def equals(q):
-        k_b[q][3] = vs([k_sg[q]], blk(T.cmp, 4 * q + 3), blk(T.sg, q), 0.0, A.is_equal, 0.5, A.mult)
+        n = 1 if q < 2 else 2
+        k_b[q][3] = k_b[q][4 - n] = vs([k_sg[q]], blk(T.cmp, 4 * q + 4 - n, n), blk(T.sg, 2 * q, n), 0.0, A.is_equal, 0.5, A.mult)
 
     def total(q):
         k_cnt[q] = op("s", [k_b[q][0], k_b[q][1], k_sg[q]], lambda: S.activation(
             blk(T.junk, 2 * q, 2), blk(T.cmp, 4 * q, 2), F.Identity, bias=T.sd[:, q:q + 1], scale=-512.0, accum_out=T.cnt[:, q:q + 1]))
 
     def running(q):
-        k_ts[q] = op("v", [k_b[q][2], k_b[q][3], k_kp], lambda: V.tensor_tensor_scan(blk(T.ts, 2 * q, 2), T.keep[:, :], blk(T.cmp, 4 * q + 2, 2), -128.0, A.mult, A.add))
+        k_ts[q] = op("v", [k_b[q][2], k_b[q][3], k_kp], lambda: V.tensor_tensor_scan(blk(T.ts, 2 * q, 2), blk(T.keep, int(q == 2), 2), blk(T.cmp, 4 * q + 2, 2), -128.0 if q < 2 else 0.0, A.mult, A.add))
 
     def place(q):
         k_ru.append(vs([k_ts[q], k_cnt[q]], T.ru[:, q:q + 1], T.cnt[:, q:q + 1], -1.0 / 512, A.mult, T.ts[:, 256 * q + 255:256 * q + 256], A.subtract))
 
-    steps = {"scores": scores, "sizes": sizes, "col": column_score, "beats": beats, "signs": signs, "equals": equals, "total": total,
+    steps = {"pack": pack, "scores": scores, "sizes": sizes, "col": column_score, "beats": beats, "signs": signs, "equals": equals, "total": total,
              "running": running, "place": place, "fill": fill}
     for step in ORDER:
         steps[step[0]](*step[1:])
     k_abs, k_scol = list(k_abs.values()), list(k_scol.values())
 
+    k_val = sa([k_v0, k_base], T.val[:, :], T.v0[:, :], UNIT, c_base)
     k_c1 = sc(lg, T.e32[:, 0:1280], T.grt[:, 0:1280])
 
-    fill()
     k = vc([k_w, k_jt] + k_ru, T.w[:, 0:512].indirect(T.ru[:, 0:4]), T.jt[:, 0:64])
     fill()
     k = vc([k], T.w[:, 64:128], T.w[:, 0:64])
@@ -289,7 +291,7 @@ def rank_program(g, core, T, topo):
     k = [turn([k], T.t1[:, 32 * c:32 * c + 32], T.w[:, c:128:4]) for c in range(4)]
     fill()
     k = vt(k, T.y[:, 0:4], T.t1[:, 0:128:32], T.t1[:, 16:128:32], A.add)
-    fill()
+    fill(2)
     k = [vt([k], T.y[a:a + 64, 4:8], T.y[a:a + 64, 0:4], T.y[64 - a:128 - a, 0:4], A.add) for a in (0, 64)]
     fill()
     k_lo = [vt(k, T.lo[a:a + 32, :], T.y[a:a + 32, 4:8], T.y[a ^ 32:(a ^ 32) + 32, 4:8], A.add) for a in (0, 32, 64, 96)]
@@ -323,13 +325,12 @@ def rank_program(g, core, T, topo):
     k = turn([k], T.to[:, :], T.xo[:, :])
     k_lf = vc(k_lo, T.lf[:, own:own + 4], T.lo[:, :])
     k_ou = vs([k], T.ou[:, :], T.to[:, 0:16], 4.0, A.mult, col["b"], A.add)
-    fill()
+    fill(2)
     k_h = [sc([k_ou] + lg, T.h[:, 128:256], T.grt[:, 0:2048].indirect(T.ou[:, 8:16])),
            vc([k_ou] + lg, T.h[:, 0:128], T.grt[:, 0:2048].indirect(T.ou[:, 0:8]))]
     fill()
-    k_hq = op("v", k_h + [k_h0], lambda: V.quantize_mx(T.hq[:, 0:128], T.hs[:, 0:128], T.h[:, 0:512]))
+    k_hq = op("v", k_h + [made["h0"]], lambda: V.quantize_mx(T.hq[:, 0:128], T.hs[:, 0:128], T.h[:, 0:512]))
     k_c0 = sc(lg, T.e32[:, 1280:2048], T.grt[:, 1280:2048])
-    fill(len(spare))
 
     fa = 64 * near.index(rank)
     partner = [far[near.index(rank)]]
@@ -405,10 +406,10 @@ def rank_program(g, core, T, topo):
     if far[0] == 0:
         k_fv1 = copy_far(0)
     k_ex2 = sa(k_zz + [made["before"], k_b16], T.ex[:, 64:128], found.indirect(T.eo[:, 4:8]), 1.0, c_back16)
-    k_ex3 = sa(k_zz + [made["last"], k_b32], T.ex[:, 128:256], found.indirect(T.eo[:, 8:16]), 1.0, c_back32)
     if far[0] != 0:
         k_fv1 = copy_far(0)
     k_fv2 = copy_far(1)
+    k_ex3 = sa(k_zz + [made["last"], k_b32], T.ex[:, 128:256], found.indirect(T.eo[:, 8:16]), 1.0, c_back32)
 
     def offsets(deps, a, b):
         return vs(deps, T.off[:, a:b], T.tx[:, a:b], 1.0 / UNIT, A.mult, col["b"], A.add)
@@ -416,8 +417,6 @@ def rank_program(g, core, T, topo):
     k = turn([k_ex], T.tx[:, 0:64], T.ex[:, 0:64])
     fill()
     k_off = offsets([k], 16, 64)
-    fill(len(spare))
-    k_er = made["er"]
     spare.extend([
         ("t1", lambda: turn([k_ex2], T.tx[:, 64:128], T.ex[:, 64:128])),
         ("o1", lambda: offsets([made["t1"]], 64, 128)),
@@ -425,10 +424,9 @@ def rank_program(g, core, T, topo):
         ("o2", lambda: offsets([made["t2"]], 128, 256)),
     ])
 
-    store("y", [k_er, left], T.er[:, 0:1024], T.e32[:, 0:1024])
-    store("y", [k_er, left], T.er[:, 1024:2048], T.e32[:, 1024:2048])
+    store("y", [made["er"], left], T.er[:, :], T.e32[:, :])
     for s in range(N):
-        store("y", [k_lf, ll, lr], T.nb[s:s + 1, 0:64], T.lf[0:16, 4 * s:4 * s + 4])
+        store("y", [k_lf, ll, lr, left], T.nb[s:s + 1, 0:64], T.lf[0:16, 4 * s:4 * s + 4])
 
     k_ready = {r: k_v + k_xo for r in near}
     for r in far:

@@ -3,10 +3,9 @@ from concourse.mybir import dt, AluOpType, AxisListType, ActivationFunctionType
 
 A = AluOpType
 F = ActivationFunctionType
-AX = AxisListType.X
-UNIT = 2.0 ** -18
-STEP = 1.0 / 64
-NONE = 32
+LW = 5
+NONE = 64
+EMPTY = -1024
 
 SCRATCH = {
     "grt": ("sbuf", [128, 2048], "bfloat16"),
@@ -16,25 +15,17 @@ SCRATCH = {
     "us": ("sbuf", [128, 128], "uint8"),
     "gq": ("sbuf", [128, 512], "float8_e4m3fn_x4"),
     "gs": ("sbuf", [128, 512], "uint8"),
-    "ident": ("sbuf", [128, 128], "bfloat16"),
     "et": ("sbuf", [128, 520], "bfloat16"),
     "eq": ("sbuf", [128, 512], "float8_e4m3fn_x4"),
     "es": ("sbuf", [128, 512], "uint8"),
-    "pi": ("sbuf", [128, 16], "int32"),
-    "p3": ("sbuf", [128, 16], "int32"),
-    "ic": ("sbuf", [128, 6], "int32"),
-    "fc": ("sbuf", [128, 6], "float32"),
-    "cc": ("sbuf", [128, 7], "float32"),
-    "uoff": ("sbuf", [128, 16], "uint16"),
-    "j0": ("sbuf", [128, 64], "float32"),
+    "cw": ("sbuf", [128, 224], "float32"),
+    "ck": ("sbuf", [128, 224], "float32"),
+    "cc": ("sbuf", [128, 5], "float32"),
     "jt": ("sbuf", [128, 64], "float32"),
-    "n0": ("sbuf", [128, 256], "float32"),
-    "stp": ("sbuf", [128, 256], "float32"),
-    "v0": ("sbuf", [128, 128], "float32"),
     "val": ("sbuf", [128, 128], "float32"),
-    "e0": ("sbuf", [128, 18], "float32"),
-    "eo": ("sbuf", [128, 18], "uint16"),
-    "selo": ("sbuf", [128, 2], "uint16"),
+    "e0": ("sbuf", [128, 20], "float32"),
+    "eo": ("sbuf", [128, 16], "uint16"),
+    "so": ("sbuf", [128, 10], "uint16"),
     "sabs": ("sbuf", [128, 512], "float32"),
     "scol": ("sbuf", [128, 4], "float32"),
     "sg": ("sbuf", [128, 1024], "bfloat16"),
@@ -45,30 +36,31 @@ SCRATCH = {
     "sd": ("sbuf", [128, 4], "float32"),
     "cnt": ("sbuf", [128, 4], "float32"),
     "ru": ("sbuf", [128, 4], "uint16"),
-    "w": ("sbuf", [128, 512], "float32"),
-    "t1": ("sbuf", [128, 128], "float32"),
-    "y": ("sbuf", [128, 8], "float32"),
-    "lo": ("sbuf", [128, 4], "float32"),
-    "lf": ("sbuf", [128, 40], "float32"),
-    "lown": ("sbuf", [128, 4], "uint16"),
+    "w": ("sbuf", [128, 528], "float32"),
+    "t1": ("sbuf", [128, 160], "float32"),
+    "y": ("sbuf", [128, 20], "float32"),
+    "lf": ("sbuf", [128, NONE + 4], "float32"),
+    "lown": ("sbuf", [128, 16], "uint16"),
     "xo": ("sbuf", [128, 32], "float32"),
     "to": ("sbuf", [128, 32], "float32"),
     "ou": ("sbuf", [128, 16], "uint16"),
+    "oe": ("sbuf", [128, 32], "uint16"),
     "h": ("sbuf", [128, 512], "bfloat16"),
-    "hq": ("sbuf", [128, 128], "float8_e4m3fn_x4"),
-    "hs": ("sbuf", [128, 128], "uint8"),
-    "ql": ("sbuf", [128, 192], "float8_e4m3fn_x4"),
-    "pl": ("sbuf", [128, 192], "uint8"),
+    "ql": ("sbuf", [128, 320], "float8_e4m3fn_x4"),
+    "pl": ("sbuf", [128, 320], "uint8"),
     "qr": ("sbuf", [128, 256], "float8_e4m3fn_x4"),
     "pr": ("sbuf", [128, 256], "uint8"),
     "e32": ("sbuf", [128, 2048], "float32"),
     "d": ("sbuf", [128, 256], "float32"),
     "scg": ("sbuf", [128, 64], "float32"),
-    "scp": ("sbuf", [128, 64], "float32"),
-    "ls": ("sbuf", [128, 32], "uint16"),
-    "tb": ("sbuf", [128, 520], "float32"),
-    "got": ("sbuf", [128, 256], "float32"),
-    "run": ("sbuf", [128, 1408], "float32"),
+    "nbg": ("sbuf", [128, 32], "float32"),
+    "nbt": ("sbuf", [128, 32], "float32"),
+    "ls": ("sbuf", [128, 48], "uint16"),
+    "tb": ("sbuf", [128, 520], "bfloat16"),
+    "got": ("sbuf", [128, 512], "bfloat16"),
+    "tt": ("sbuf", [128, 1024], "bfloat16"),
+    "stp": ("sbuf", [128, 128], "float32"),
+    "run": ("sbuf", [128, 128], "float32"),
     "zz": ("sbuf", [128, 64], "float32"),
     "ex": ("sbuf", [128, 256], "float32"),
     "tx": ("sbuf", [128, 256], "float32"),
@@ -77,16 +69,17 @@ SCRATCH = {
     "ac": ("sbuf", [128, 2048], "float32"),
     "ps": ("psum", [128, 4096], "float32"),
 }
-ORDER = [("pack", 0), ("pack", "u"), ("scores", 0), ("pack", 1), ("scores", 1), ("fill", 2), ("pack", 2), ("scores", 2), ("fill", 1), ("pack", 3), ("scores", 3),
+ORDER = [("pack", 0), ("pack", "u"), ("scores", 0), ("pack", 1), ("scores", 1), ("pack", 2), ("scores", 2), ("pack", 3), ("scores", 3), ("fill", "turned"),
          ("sizes", 0), ("col", 0), ("sizes", 1), ("col", 1), ("beats", 0, 1), ("beats", 1, 0),
          ("sizes", 2), ("col", 2), ("signs", 0), ("beats", 0, 2), ("beats", 1, 2), ("beats", 2, 0, 2),
          ("sizes", 3), ("col", 3), ("signs", 1), ("beats", 3, 0, 2), ("signs", 2), ("signs", 3),
          ("total", 0), ("total", 1), ("total", 2), ("total", 3),
          ("equals", 0), ("beats", 0, 3), ("equals", 1), ("beats", 1, 3), ("running", 0), ("equals", 2), ("running", 1), ("equals", 3),
          ("place", 0), ("running", 2), ("place", 1), ("running", 3), ("place", 2), ("place", 3)]
-ER_FIRST = 4
-STORES = (("v", "y", 0, 96), ("s", "y", 96, 320), ("v", "y", 320, 704), ("s", "y", 704, 1216), ("v", "y", 1216, 1760), ("s", "s", 1760, 2048))
-SEMAPHORES = ["qv", "qs", "qt", "qp", "lu", "l0", "l1", "l2", "l3", "st", "ll", "lr", "cl", "cr", "cp", "cq", "loc"]
+ER_FIRST, ER_TABLE = 4, 6
+TABLE_V = 10
+STORES = (("v", "y", 0, 128), ("s", "y", 128, 352), ("v", "y", 352, 704), ("s", "y", 704, 1152), ("v", "y", 1152, 1600), ("s", "s", 1600, 2048))
+SEMAPHORES = ["qv", "qs", "qt", "qp", "lu", "l0", "l1", "l2", "l3", "st", "ll", "lr", "cl", "cr0", "cr1", "cp", "cq", "loc", "rel"]
 
 
 def rank_program(g, core, T, topo):
@@ -157,79 +150,79 @@ def rank_program(g, core, T, topo):
     def sc(deps, out, in_):
         return op("s", deps, lambda: S.activation(out, in_, F.Copy))
 
-    spare, made = [], {}
+    spare, made = {}, {}
 
-    def fill(n=1):
-        for _ in range(min(n, len(spare))):
-            name, call = spare.pop(0)
-            made[name] = call()
+    def fill(*names):
+        for name in names:
+            made[name] = spare.pop(name)()
 
     lu = load("s", T.uc[:, 0:16], T.u[:, 0:16], "lu")
     lg = [load("y", blk(T.grt, 4 * q, 4), blk(T.gr, 4 * q, 4), "l%d" % q) for q in range(4)]
 
-    own = 4 * rank
-
-    def whole(out, pattern, base=0):
-        return op("p", [], lambda: g.iota(out, pattern, base, 0, allow_small_or_imprecise_dtypes=True))
-    k_pi = op("p", [], lambda: g.iota(T.pi[:, 0:16], [[0, 16]], 0, 1))
+    def whole(out, pattern, base=0, step=0):
+        return op("p", [], lambda: g.iota(out, pattern, base, step, allow_small_or_imprecise_dtypes=True))
     k_ones = vm(blk(T.keep, 0), 1.0)
-    k_id = op("p", [k_ones], lambda: g.affine_select(T.ident[:, :], blk(T.keep, 0), [[-1, 128]], A.is_equal, 0.0, 0, 1))
-    k_j0 = whole(T.j0[:, :], [[128, 4], [1, 16]])
-    whole(T.e0[:, 0:8], [[4, 4], [0, 2]], 16)
-    whole(T.e0[:, 8:16], [[1, 4], [0, 2]])
-    k_e0 = whole(T.e0[:, 16:18], [[0, 2]])
-    k_v0 = whole(T.v0[:, :], [[256, 2], [4, 4], [16, 16]], 8)
-    whole(T.n0[:, 0:128], [[0, 8], [1, 16]])
-    k_n0 = whole(T.n0[:, 128:256], [[0, 4], [1, 32]])
-
-    k_tb = whole(T.tb[:, :], [[0, 520]])
-
     k_et = vm(T.et[:, :], 0.0)
-    k_p3 = vs([k_pi], T.p3[:, :], T.pi[:, :], 3, A.bitwise_and)
-    parts = {"b": 3, "k4": 12, "g16": 112, "m": 15, "r": 31, "a32": 96}
-    col = {}
-    for i, name in enumerate(parts):
-        k_ic = vs([k_pi], T.ic[:, i:i + 1], T.pi[:, 0:1], parts[name], A.bitwise_and)
-        col[name] = T.fc[:, i:i + 1]
-    k_uoff = vc([k_p3], T.uoff[:, :], T.p3[:, :])
-    vm(blk(T.keep, 2), 1.0)
-    k_w = vm(T.w[:, 0:64], 0.0)
-    k_fc = vc([k_ic], T.fc[:, :], T.ic[:, :])
-    k_kp = vs([k_id], blk(T.keep, 1), T.ident[:, :], -2.0, A.mult, 1.0, A.add)
-    k_jt = vs([k_j0, k_fc], T.jt[:, :], T.j0[:, :], col["g16"], A.add)
-    k_e = sc([k_id, k_et], T.et[:, 3:515:4], T.ident[:, :])
 
-    def small(i, deps, in_, scale, bias):
-        return T.cc[:, i:i + 1], sa(deps, T.cc[:, i:i + 1], in_, scale, bias)
-    c_k, k_ck = small(0, [k_fc], col["k4"], 0.25, 0.0)
-    c_t, k = small(1, [k_fc], col["g16"], 0.25, col["b"])
-    c_back16, k_b16 = small(2, [k_fc], col["m"], STEP, -15 * STEP)
-    c_back32, k_b32 = small(3, [k_fc], col["r"], STEP, -31 * STEP)
-    c_base, k_base = small(4, [k_fc], col["a32"], 16 * UNIT, 0.0)
-    c_later, k_later = small(5, [k], col["k4"], 2.0, c_t)
+    def diagonal(deps, out, how, other):
+        return op("p", deps, lambda: g.affine_select(out, blk(T.keep, 0), [[-1, 128]], how, other, 0, 1))
+    k_e = diagonal([k_ones, k_et], T.et[:, 3:515:4], A.is_equal, 0.0)
+    whole(T.cw[:, 0:32], [[0, 8], [1, 4]])
+    whole(T.cw[:, 32:64], [[0, 2], [2, 4], [0, 4]])
+    for h, base, step in ((0, 3, -2), (1, 0, 3)):
+        whole(T.cw[:, 64 + 16 * h:80 + 16 * h], [[1, 2], [step, 2], [8, 4]], base)
+        whole(T.cw[:, 96 + 16 * h:112 + 16 * h], [[0, 4], [1, 2], [step, 2]], base)
+    whole(T.cw[:, 128:160], [[16, 2], [0, 16]], 0, 1)
+    whole(T.cw[:, 160:192], [[-16, 2], [0, 4], [16, 4]], 0, -1)
+    k_cw = whole(T.cw[:, 192:224], [[0, 32]], 0, -4)
+    c_b, c_k2, c_at, c_pb, c_g16, c_gap, c_base = [T.ck[:, 32 * i:32 * i + 1] for i in range(7)]
+    k_kp = diagonal([], blk(T.keep, 1), A.not_equal, -1.0)
+    k_jt = whole(T.jt[:, :], [[128, 4], [1, 16]], 0, 1)
+    whole(T.e0[:, 0:8], [[8, 2], [1, 2], [0, 2]], 16)
+    whole(T.e0[:, 8:16], [[1, 4], [0, 2]])
+    k_e0 = whole(T.e0[:, 16:20], [[32, 4]])
+    k_v0 = whole(T.val[:, 64:128], [[1, 4], [4, 16]], 2)
+    k_tb = sa([k_et, k_e], T.tb[:, :], T.et[:, :], 0.0, float(EMPTY))
 
-    def ones(b):
-        return "ones%d" % b, lambda: op("v", [k_e], lambda: V.quantize_mx(blk(T.eq, b), blk(T.es, b), T.et[:, 3 - b:515 - b]))
-    spare.extend([
-        ones(0), ones(1), ones(2),
-        ("own", lambda: vs([k_e0, k_ck], T.eo[:, 16:18], T.e0[:, 16:18], c_k, A.add)),
-        ("none", lambda: vm(T.lf[:, NONE:NONE + 8], 512.0)),
-        ones(3),
-        ("step16", lambda: vs([k_n0, k_fc], blk(T.stp, 0), blk(T.n0, 0), col["m"], A.not_equal, STEP - 1.0, A.add)),
-        ("step32", lambda: vs([k_n0, k_fc], blk(T.stp, 1), blk(T.n0, 1), col["r"], A.not_equal, STEP - 1.0, A.add)),
-        ("h0", lambda: vm(T.h[:, 256:512], 0.0)),
-        ("x0", lambda: vm(T.x[:, 0:8], 0.0)),
-        ("first", lambda: vs([k_fc], T.cc[:, 6:7], col["r"], 4.0, A.is_lt, float(NONE), A.mult)),
-        ("sel0", lambda: vs([k_fc], T.selo[:, 0:1], col["a32"], 0.25, A.mult, col["m"], A.add)),
-        ("sel1", lambda: vs([made["first"], k_later], T.selo[:, 1:2], c_later, float(NONE), A.min, T.cc[:, 6:7], A.max)),
-        ("before", lambda: vs([k_e0, k_ck], T.eo[:, 0:8], T.e0[:, 0:8], c_k, A.add)),
-        ("last", lambda: vs([k_e0, k_fc], T.eo[:, 8:16], T.e0[:, 8:16], col["k4"], A.add)),
-        ("pad", lambda: vm(T.run[:, 543:896:32], 0.0)),
-    ])
+    k_keep = vm(blk(T.keep, 2), 1.0)
+    k_w = vm(T.w[:, 0:96], 0.0)
+    k_none = vm(T.lf[:, NONE:NONE + 4], 512.0)
+    pad = 256 * (rank % 2)
+    chosen = T.h[:, 256 - pad:512 - pad]
+    k_h0 = vm(T.h[:, pad:pad + 256], 0.0)
+    k_x0 = vm(T.x[:, 0:8], 0.0)
+    vm(T.stp[:, 0:128:4], 4.0 * EMPTY)
+    vm(T.stp[:, 1:128:4], 0.0)
+    k_stp = vm(T.stp[:, 2:128:4], 0.0)
+    k_eq = [op("v", [k_e], lambda: V.quantize_mx(blk(T.eq, b), blk(T.es, b), T.et[:, 3 - b:515 - b])) for b in range(4)]
 
-    fill(3)
-    k_ut = [vc([lu, k_uoff], T.ut[:, 0:256], T.uc[:, 0:16].indirect(T.uoff[:, 0:16])),
-            sc([lu, k_uoff], T.ut[:, 256:512], T.uc[:, 0:16].indirect(T.uoff[:, 0:16]))]
+    def cc(i, n=1):
+        return T.cc[:, i:i + n]
+    small = {}
+
+    def scalar_constants():
+        k = [made["turned"], k_e0]
+        sa(k, cc(0), c_at, 1.0, 32.0)
+        j = sa(k, cc(4), c_g16, 4.0, c_base)
+        small["s"] = sa(k, cc(1), c_k2, 4.0, c_pb)
+        small["val"] = sa([j, k_v0], T.val[:, 0:64], T.val[:, 64:128], 1.0, cc(4))
+    spare.update({
+        "turned": lambda: turn([k_cw], T.ck[:, :], T.cw[:, :]),
+        "xo": lambda: vs([made["turned"]], T.so[:, 4:6], T.ck[:, 0:2], -8.0, A.mult, c_at, A.add),
+        "before": lambda: vs([k_e0, made["turned"]], T.eo[:, 0:8], T.e0[:, 0:8], c_k2, A.add),
+        "last": lambda: vs([k_e0, made["turned"]], T.eo[:, 8:16], T.e0[:, 8:16], c_k2, A.add, c_k2, A.add),
+        "nb": lambda: vs([small["s"]], T.so[:, 6:8], T.e0[:, 16:18], cc(1), A.add),
+        "early": lambda: vs([k_e0, made["turned"]], cc(2, 2), T.e0[:, 16:19:2], c_gap, A.add, 0.0, A.is_le),
+        "step": lambda: vs([made["turned"], k_stp], T.stp[:, 3:128:4], T.stp[:, 2:128:4], c_base, A.subtract),
+        "lown": lambda: vc([made["turned"]], T.so[:, 8:9], c_pb),
+        "group": lambda: vs([made["turned"]], T.so[:, 2:3], c_g16, 0.5, A.mult, c_pb, A.add),
+        "sel0": lambda: vs([made["early"]], T.so[:, 0:1], cc(2), float(NONE), A.mult, c_at, A.max),
+        "sel1": lambda: vs([made["early"], small["s"]], T.so[:, 1:2], cc(3), float(NONE), A.mult, cc(0), A.max),
+    })
+
+    k_ut = [vs([lu, k_ones], T.ut[:, b:512:4], blk(T.keep, 0), T.uc[:, b:b + 1], A.mult) for b in (0, 1)]
+    k_ut += [sa([lu, k_ones], T.ut[:, b:512:4], blk(T.keep, 0), 0.0, T.uc[:, b:b + 1]) for b in (2, 3)]
+    sc(lg[0:1], T.e32[:, 0:512], T.grt[:, 0:512])
 
     k_q, k_abs, k_scol, k_sc, k_row = {}, {}, {}, {}, {}
 
@@ -270,7 +263,7 @@ def rank_program(g, core, T, topo):
             blk(T.junk, 2 * q, 2), blk(T.cmp, 4 * q, 2), F.Identity, bias=T.sd[:, q:q + 1], scale=-512.0, accum_out=T.cnt[:, q:q + 1]))
 
     def running(q):
-        k_ts[q] = op("v", [k_b[q][2], k_b[q][3], k_kp], lambda: V.tensor_tensor_scan(blk(T.ts, 2 * q, 2), blk(T.keep, int(q == 2), 2), blk(T.cmp, 4 * q + 2, 2), -128.0 if q < 2 else 0.0, A.mult, A.add))
+        k_ts[q] = op("v", [k_b[q][2], k_b[q][3], k_kp, k_keep], lambda: V.tensor_tensor_scan(blk(T.ts, 2 * q, 2), blk(T.keep, int(q == 2), 2), blk(T.cmp, 4 * q + 2, 2), -128.0 if q < 2 else 0.0, A.mult, A.add))
 
     def place(q):
         k_ru.append(vs([k_ts[q], k_cnt[q]], T.ru[:, q:q + 1], T.cnt[:, q:q + 1], -1.0 / 512, A.mult, T.ts[:, 256 * q + 255:256 * q + 256], A.subtract))
@@ -281,20 +274,18 @@ def rank_program(g, core, T, topo):
         steps[step[0]](*step[1:])
     k_abs, k_scol = list(k_abs.values()), list(k_scol.values())
 
-    k_val = sa([k_v0, k_base], T.val[:, :], T.v0[:, :], UNIT, c_base)
-    k_c1 = sc(lg, T.e32[:, 0:1280], T.grt[:, 0:1280])
+    scalar_constants()
+    k_wide = sc(lg, T.e32[:, 512:2048], T.grt[:, 512:2048])
 
-    k = vc([k_w, k_jt] + k_ru, T.w[:, 0:512].indirect(T.ru[:, 0:4]), T.jt[:, 0:64])
-    fill()
-    k = vc([k], T.w[:, 64:128], T.w[:, 0:64])
-    fill()
-    k = [turn([k], T.t1[:, 32 * c:32 * c + 32], T.w[:, c:128:4]) for c in range(4)]
-    fill()
-    k = vt(k, T.y[:, 0:4], T.t1[:, 0:128:32], T.t1[:, 16:128:32], A.add)
-    fill(2)
-    k = [vt([k], T.y[a:a + 64, 4:8], T.y[a:a + 64, 0:4], T.y[64 - a:128 - a, 0:4], A.add) for a in (0, 64)]
-    fill()
-    k_lo = [vt(k, T.lo[a:a + 32, :], T.y[a:a + 32, 4:8], T.y[a ^ 32:(a ^ 32) + 32, 4:8], A.add) for a in (0, 32, 64, 96)]
+    k = vc([k_w, k_jt] + k_ru, T.w[:, 16:528].indirect(T.ru[:, 0:4]), T.jt[:, 0:64])
+    fill("xo")
+    k = [turn([k], T.t1[:, 0:96], T.w[:, 0:96]), turn([k], T.t1[:, 96:160], T.w[:, 16:80])]
+    fill("early")
+    k = vt(k, T.y[0:64, 0:10], T.t1[0:64, 0:160:16], T.t1[64:128, 0:160:16], A.add)
+    k = [vt([k], T.y[a:a + 32, 10:20], T.y[a:a + 32, 0:10], T.y[32 - a:64 - a, 0:10], A.add) for a in (0, 32)]
+    own = T.lf[:, 8 * rank:8 * rank + LW]
+    k_lo = [vt(k, T.lf[a:a + 64, 8 * rank:8 * rank + LW], T.y[0:64, 10:20:2], T.y[0:64, 11:20:2], A.add) for a in (0, 64)]
+    fill("sel0")
 
     far_e = topo.engines(core, T.cores[far[0]])
     near_e = [e for e in topo.engines(core, T.cores[near_others[0]]) if e not in far_e]
@@ -305,8 +296,9 @@ def rank_program(g, core, T, topo):
     def ids(ranks):
         return [DstId(rid=topo.addr(T.cores[r])[0], pnc=topo.addr(T.cores[r])[1]) for r in ranks]
 
-    def near_at(r):
-        return [q for q in near if q != r].index(rank)
+    def near_at(r, q=rank):
+        i, j = near.index(q), near.index(r)
+        return 64 * (i + (i > j or i == j and r % 2 == 0))
 
     def send(deps, src, near_dst, far_dst, near_sem, far_sem, far=far):
         need("p", deps)
@@ -315,127 +307,135 @@ def rank_program(g, core, T, topo):
             RemoteDMATransfer(dst_ids=ids(near_others), dma_engine_mask=near_mask, remote_sem=T.sem[near_sem], srcs=[src], dsts=[near_dst(r) for r in near_others]),
         ], local_sem=T.sem["loc"])
 
-    send(k_lo, T.lo[:, :], lambda r: T.lf[:, own:own + 4], lambda r: T.lf[:, own:own + 4], "ll", "lr")
-    ll = ("ll", len(near_others) * len(near_e))
-    lr = ("lr", len(far) * len(far_e))
+    def write(deps, src, ranks, dsts, mask, sem):
+        need("p", deps)
+        g.remote_dma_fused([RemoteDMATransfer(dst_ids=ids(ranks), dma_engine_mask=mask, remote_sem=T.sem[sem], srcs=[src], dsts=dsts)], local_sem=T.sem["loc"])
 
-    fill()
-    k = vc(k_lo + [made["own"]], T.xo[:, :], T.lo[:, :].indirect(T.eo[:, 16:18]))
-    k_lown = vc(k_lo, T.lown[:, :], T.lo[:, :])
+    send(k_lo, own, lambda r: own, lambda r: own, "ll", "lr")
+    lists = k_lo + [("ll", len(near_others) * len(near_e)), ("lr", len(far) * len(far_e)), k_none]
+
+    k = vc(k_lo + [made["xo"]], T.xo[:, :], own.indirect(T.so[:, 4:6]))
+    fill("sel1")
     k = turn([k], T.to[:, :], T.xo[:, :])
-    k_lf = vc(k_lo, T.lf[:, own:own + 4], T.lo[:, :])
-    k_ou = vs([k], T.ou[:, :], T.to[:, 0:16], 4.0, A.mult, col["b"], A.add)
-    fill(2)
-    k_h = [sc([k_ou] + lg, T.h[:, 128:256], T.grt[:, 0:2048].indirect(T.ou[:, 8:16])),
-           vc([k_ou] + lg, T.h[:, 0:128], T.grt[:, 0:2048].indirect(T.ou[:, 0:8]))]
-    fill()
-    k_hq = op("v", k_h + [made["h0"]], lambda: V.quantize_mx(T.hq[:, 0:128], T.hs[:, 0:128], T.h[:, 0:512]))
-    k_c0 = sc(lg, T.e32[:, 1280:2048], T.grt[:, 1280:2048])
+    fill("lown")
+    k_ou = vs([k], T.ou[:, :], T.to[:, 0:16], 4.0, A.mult, c_b, A.add)
+    k_oe = vs([k], T.oe[:, 0:32:2], T.to[:, 0:16], 4.0, A.mult, c_b, A.add)
+    k_h = [vc([k_ou] + lg, chosen, T.grt[:, 0:2048].indirect(T.ou[:, 0:16]))]
+    fill("last")
+    mine = near_at(rank)
+    tile = mine - 64 + pad // 4
+    k_hq = op("v", k_h + [k_h0], lambda: V.quantize_mx(T.ql[:, tile:tile + 128], T.pl[:, tile:tile + 128], T.h[:, 0:512]))
+    k_lown = vc(k_lo + [made["lown"]], T.lown[:, :], own.indirect(T.so[:, 8:9]))
+    fill("group", "before", "nb", "step")
 
     fa = 64 * near.index(rank)
-    partner = [far[near.index(rank)]]
-    send([k_hq], T.hq[:, 0:64].bitcast(dt.uint8),
-         lambda r: T.ql[:, 64 * near_at(r):64 * near_at(r) + 64].bitcast(dt.uint8),
-         lambda r: T.qr[:, fa:fa + 64].bitcast(dt.uint8), "cl", "cp", partner)
-    send([k_hq], T.hs[:, 0:64],
-         lambda r: T.pl[:, 64 * near_at(r):64 * near_at(r) + 64],
-         lambda r: T.pr[:, fa:fa + 64], "cl", "cq", partner)
+    partner = far[near.index(rank)]
+
+    def codes(t, a):
+        return t[:, a:a + 64].bitcast(dt.uint8)
+
+    def to_far():
+        write([k_hq], codes(T.ql, mine), [partner], [codes(T.qr, fa)], far_mask, "cp")
+        write([k_hq], T.pl[:, mine:mine + 64], [partner], [T.pr[:, fa:fa + 64]], far_mask, "cq")
+
+    def to_near():
+        write([k_hq], codes(T.ql, mine), near_others, [codes(T.ql, near_at(r)) for r in near_others], near_mask, "cl")
+        write([k_hq], T.pl[:, mine:mine + 64], near_others, [T.pl[:, near_at(r):near_at(r) + 64] for r in near_others], near_mask, "cl")
+    for call in (to_far, to_near) if fa < 128 else (to_near, to_far):
+        call()
     cl = ("cl", 2 * len(near_others) * len(near_e))
     cp = [("cp", len(far_e)), ("cq", len(far_e))]
-    for arrived, piece in zip(cp, (T.qr[:, fa:fa + 64].bitcast(dt.uint8), T.pr[:, fa:fa + 64])):
-        need("p", [arrived])
-        g.remote_dma_fused([RemoteDMATransfer(dst_ids=ids(near_others), dma_engine_mask=far_mask + near_mask, remote_sem=T.sem["cr"],
-                                              srcs=[piece], dsts=[piece] * len(near_others))], local_sem=T.sem["loc"])
-    cr = ("cr", 2 * len(near_others) * (len(far_e) + len(near_e)))
+    for arrived, piece in zip(cp, (codes(T.qr, fa), T.pr[:, fa:fa + 64])):
+        write([arrived], piece, near_others, [piece] * len(near_others), far_mask + near_mask, "cr%d" % (fa // 128))
+    g.sem_inc(T.sem["rel"], 1)
+    each = 2 * (len(far_e) + len(near_e))
+    cr = [cp + [("cr%d" % i, each)] if fa // 128 == i else [("cr%d" % i, 2 * each)] for i in range(2)]
 
     def unpack(b, to, q, s, a, n, deps):
-        return op("t", deps + [made["ones%d" % b]], lambda: g.tensor.matmul_mx(bank(to, n), blk(T.eq, b), blk(T.es, b), q[:, a:a + n], s[:, a:a + n], True, True))
+        return op("t", deps + [k_eq[b]], lambda: g.tensor.matmul_mx(bank(to, n), blk(T.eq, b), blk(T.es, b), q[:, a:a + n], s[:, a:a + n], True, True))
 
     def xs(r, b, n):
         return T.x[:, 8 + 256 * r + b:8 + 256 * (r + n):4]
-    k_own = [unpack(b, 4 + b, T.hq, T.hs, 0, 128, [k_hq] + k_scol + k_abs) for b in range(4)]
-    k_d = [vt([k_own[b]] + k_h, T.d[:, b:256:4], T.h[:, b:256:4], bank(4 + b, 64), A.subtract) for b in range(4)]
+    k_own = [unpack(b, 4 + b, T.ql, T.pl, tile, 128, [k_hq] + k_scol + k_abs) for b in range(4)]
+    at = 2048 + mine - tile
+    k_d = [vt([k_own[b]] + k_h, T.d[:, b:256:4], T.h[:, 256 - pad + b:512 - pad:4], T.ps[:, at + 512 * b:at + 512 * b + 64], A.subtract) for b in range(4)]
+    er_at = [0]
 
-    def put_er(a, b):
-        return vc(k_d + [k_c0, k_c1, k_ou, made["er"]], T.e32[:, 0:2048].indirect(T.ou[:, a:b]), T.d[:, 16 * a:16 * b])
+    def put_er(n=1):
+        a = er_at[0]
+        er_at[0] += n
+        at = T.ou[:, a:a + n] if n > 1 else T.oe[:, 2 * a:2 * a + 1]
+        made["er"] = vc(k_d + [k_wide, k_ou, k_oe, made["er"]], T.e32[:, 0:2048].indirect(at), T.d[:, 16 * a:16 * (a + n)])
+        if er_at[0] == 16:
+            store("y", [made["er"], ("rel", 1)], T.er[:, :], T.e32[:, :])
     made["er"] = k_ou
-    made["er"] = put_er(0, ER_FIRST)
-    spare.extend([("er", lambda a=a: put_er(a, a + 2)) for a in range(ER_FIRST, 16, 2)])
-    k_xo = [sc([k_d[b]], xs(rank, b, 1), bank(4 + b, 64)) for b in range(4)]
 
-    k = sc([k_lown] + k_abs, T.scg[:, :], T.sabs[:, 0:512].indirect(T.lown[:, 0:4]))
-    k = [sc([k], T.scp[0:1, c:64:4], T.scg[0:1, 16 * c:16 * c + 16]) for c in range(4)]
-    store("y", k, T.sc[:, :], T.scp[0:1, 0:64])
+    store("y", [sc([k_lown] + k_abs, T.scg[:, :], T.sabs[:, 0:512].indirect(T.lown[:, 0:4]))], T.sc[:, :], T.scg[0:1, :])
 
     table = T.tb[:, 0:520]
-    k_ls = vc([ll, lr, k_lf, made["none"], made["sel0"], made["sel1"]], T.ls[:, :], T.lf[:, 0:40].indirect(T.selo[:, 0:2]))
-    fill()
-    k = vc([k_ls, k_tb, k_val], table.indirect(T.ls[:, 0:4]), T.val[:, 0:64])
-    fill()
-    k_g1 = vc([k], T.got[:, 0:64], table.indirect(T.ls[:, 16:20]))
-    fill()
-    k_tab = vc([k_g1], table.indirect(T.ls[:, 4:8]), T.val[:, 64:128])
-    fill()
-    k_g2 = sc([k_tab], T.got[:, 64:256], table.indirect(T.ls[:, 20:32]))
+    k_ls = vc(lists + [made["group"], made["sel0"], made["sel1"]], T.ls[:, :], T.lf[:, :].indirect(T.so[:, 0:3]))
+    put_er(ER_FIRST)
+    k_tab = vc([k_ls, k_tb, small["val"]], table.indirect(T.ls[:, 32:36]), T.val[:, 0:64])
+    put_er(ER_TABLE)
+    n = 16 * TABLE_V
+    k_got = [sc([k_tab], T.got[:, n:512], table.indirect(T.ls[:, TABLE_V:32])),
+             vc([k_tab], T.got[:, 0:n], table.indirect(T.ls[:, 0:TABLE_V]))]
+    k = [turn([k_tab], blk(T.tt, c), T.tb[:, c:512:4]) for c in range(4)]
+    k += [turn(k_got[1:], T.tt[:, 512:512 + n], T.got[:, 0:n]), turn(k_got[:1], T.tt[:, 512 + n:1024], T.got[:, n:512])]
+    put_er()
+    k = op("v", k + [made["step"]], lambda: V.tensor_tensor_scan(T.run[:, :], T.stp[:, :], T.tt[:, 0:1024:8], 0.0, A.add, A.max))
+    put_er()
+    k = vt([k], T.zz[0:64, 32:64], T.run[0:64, 3:128:4], T.run[64:128, 3:128:4], A.max)
+    k_zz = [vt([k], T.zz[a:a + 32, 0:32], T.zz[0:32, 32:64], T.zz[32:64, 32:64], A.max) for a in (0, 32, 64, 96)]
 
-    k_near = [unpack(b, b, T.ql, T.pl, 0, 192, [cl] + k_abs + k_scol) for b in range(4)]
-    k_v = []
-    for b in range(4):
-        i = near.index(rank)
-        for at, first, n in ((0, near[0], i), (i, rank + 1, len(near) - 1 - i)):
-            if n:
-                k_v.append(sc([k_near[b]], xs(first, b, n), T.ps[:, 512 * b + 64 * at:512 * b + 64 * (at + n)]))
-    k_far = [[unpack(b, 4 + b, T.qr, T.pr, 0, 128, [cr] + cp + k_xo) for b in range(4)],
-             [unpack(b, b, T.qr, T.pr, 128, 128, [cr] + k_v) for b in range(4)]]
-
-    def copy_far(i):
-        return [sc([k_far[i][b]], xs(far[2 * i], b, 2), bank(4 * (1 - i) + b, 128)) for b in range(4)]
-
-    def pick(deps, out, step, in_):
-        return op("v", deps + [made["step16"], made["step32"]], lambda: V.tensor_tensor_scan(out, step, in_, 0.0, A.add, A.max))
-    k_last = [pick([k_tab], blk(T.run, c), blk(T.stp, 1), T.tb[:, c:512:4]) for c in range(4)]
-    k_run = [pick([k_g1, k_g2], T.run[:, 897 + 256 * i:1152 + 256 * i:2], blk(T.stp, 0), blk(T.got, i)) for i in range(2)]
-    k = [vt(k_last, T.zz[a:a + 64, 32:48], T.run[a:a + 64, 31:512:32], T.run[64 - a:128 - a, 31:512:32], A.max) for a in (0, 64)]
-
-    def later(a):
-        return T.run[32 * a:32 * a + 32, 927 - 128 * a:1408 - 128 * a:32]
-    k += [vt(k_run + [made["pad"]], T.zz[32 * a:32 * a + 32, 48:64], later(a), later(a ^ 2), A.max) for a in range(4)]
-    k_zz = [vt(k, T.zz[a:a + 32, 0:32], T.zz[a:a + 32, 32:64], T.zz[a ^ 32:(a ^ 32) + 32, 32:64], A.max) for a in (0, 32, 64, 96)]
     found = T.zz[:, 0:32]
-    k_ex = vs(k_zz + [made["before"], k_b16], T.ex[:, 0:64], found.indirect(T.eo[:, 0:4]), c_back16, A.add)
-    if far[0] == 0:
-        k_fv1 = copy_far(0)
-    k_ex2 = sa(k_zz + [made["before"], k_b16], T.ex[:, 64:128], found.indirect(T.eo[:, 4:8]), 1.0, c_back16)
-    if far[0] != 0:
-        k_fv1 = copy_far(0)
-    k_fv2 = copy_far(1)
-    k_ex3 = sa(k_zz + [made["last"], k_b32], T.ex[:, 128:256], found.indirect(T.eo[:, 8:16]), 1.0, c_back32)
+    k_ready = {}
+
+    def products(to, q, s, a, n, deps):
+        return [unpack(b, to + b, q, s, a, n, deps) for b in range(4)]
+
+    def copies(k, to, at, ranks, by=(sc, sc, sc, sc)):
+        done = [by[b]([k[b]], xs(ranks[0], b, len(ranks)), T.ps[:, 512 * (to + b) + at:512 * (to + b) + at + 64 * len(ranks)]) for b in range(4)]
+        k_ready.update({r: done for r in ranks})
+        return done
+
+    def pair(i, deps):
+        r = 2 * i
+        if r in near:
+            return products(4 * (i % 2), T.ql, T.pl, near_at(rank, r), 128, deps + [cl, k_hq])
+        return products(4 * (i % 2), T.qr, T.pr, 64 * far.index(r), 128, deps + cr[far.index(r) // 2])
 
     def offsets(deps, a, b):
-        return vs(deps, T.off[:, a:b], T.tx[:, a:b], 1.0 / UNIT, A.mult, col["b"], A.add)
-    fill()
+        return vs(deps, T.off[:, a:b], T.tx[:, a:b], 4.0, A.mult, c_b, A.add)
+    k_ex = vc(k_zz + [made["before"]], T.ex[:, 0:64], found.indirect(T.eo[:, 0:4]))
+    put_er()
     k = turn([k_ex], T.tx[:, 0:64], T.ex[:, 0:64])
-    fill()
+    put_er()
     k_off = offsets([k], 16, 64)
-    spare.extend([
-        ("t1", lambda: turn([k_ex2], T.tx[:, 64:128], T.ex[:, 64:128])),
-        ("o1", lambda: offsets([made["t1"]], 64, 128)),
-        ("t2", lambda: turn([k_ex3], T.tx[:, 128:256], T.ex[:, 128:256])),
-        ("o2", lambda: offsets([made["t2"]], 128, 256)),
-    ])
+    put_er()
+    k0, k1 = pair(0, k_abs + k_scol), pair(1, k_d)
+    k2 = pair(2, copies(k0, 0, 0, [0, 1]))
+    copies(k1, 4, 0, [2])
+    k_ex2 = k_ex3 = sc(k_zz + [made["before"], made["last"]], T.ex[:, 64:256], found.indirect(T.eo[:, 4:16]))
+    k3 = pair(3, copies(k1, 4, 64, [3]))
+    copies(k2, 0, 0, [4, 5])
+    copies(k3, 4, 0, [6, 7])
+    k_nb = sc(lists + [made["nb"]], T.nbg[:, :], T.lf[:, :].indirect(T.so[:, 6:8]))
 
-    store("y", [made["er"], left], T.er[:, :], T.e32[:, :])
-    for s in range(N):
-        store("y", [k_lf, ll, lr, left], T.nb[s:s + 1, 0:64], T.lf[0:16, 4 * s:4 * s + 4])
+    spare.update({
+        "ers": put_er,
+        "t1": lambda: turn([k_ex2], T.tx[:, 64:128], T.ex[:, 64:128]),
+        "o1": lambda: offsets([made["t1"]], 64, 128),
+        "t2": lambda: turn([k_ex3], T.tx[:, 128:256], T.ex[:, 128:256]),
+        "o2": lambda: offsets([made["t2"]], 128, 256),
+        "nbs": lambda: store("y", [turn([k_nb], T.nbt[:, :], T.nbg[:, :])], T.nb[:, :], T.nbt[0:32, 0:16]),
+    })
 
-    k_ready = {r: k_v + k_xo for r in near}
-    for r in far:
-        k_ready[r] = k_fv1 if r in far[:2] else k_fv2
-    k = made["x0"]
+    k = k_x0
     for s in range(1, N):
         a = 8 + 256 * s
         k = vt([k, k_off if s < 4 else made["o1"]] + k_ready[s] + k_ready[0], T.x[:, a:a + 256], T.x[:, 0:a].indirect(T.off[:, 16 * s:16 * s + 16]), T.x[:, a:a + 256], A.add)
-        fill()
+        fill(*list(spare)[:1])
     for e, y, a, b in STORES:
         out, src = T.ac[:, a:b], T.x[:, 0:2056].indirect(T.off[:, 128 + a // 16:128 + b // 16])
         store(y, [(vc if e == "v" else sc)([k, made["o2"]], out, src)], T.acc[:, a:b], out)

from concourse.bass import DstId, RemoteDMATransfer
from concourse.mybir import dt, AluOpType, AxisListType, ActivationFunctionType

A = AluOpType
F = ActivationFunctionType
LW = 5
NONE = 64
EMPTY = -1024

SCRATCH = {
    "grt": ("sbuf", [128, 2048], "bfloat16"),
    "uc": ("sbuf", [128, 16], "bfloat16"),
    "ut": ("sbuf", [128, 512], "bfloat16"),
    "uq": ("sbuf", [128, 128], "float8_e4m3fn_x4"),
    "us": ("sbuf", [128, 128], "uint8"),
    "gq": ("sbuf", [128, 512], "float8_e4m3fn_x4"),
    "gs": ("sbuf", [128, 512], "uint8"),
    "et": ("sbuf", [128, 520], "bfloat16"),
    "eq": ("sbuf", [128, 512], "float8_e4m3fn_x4"),
    "es": ("sbuf", [128, 512], "uint8"),
    "cw": ("sbuf", [128, 224], "float32"),
    "ck": ("sbuf", [128, 224], "float32"),
    "cc": ("sbuf", [128, 5], "float32"),
    "jt": ("sbuf", [128, 64], "float32"),
    "val": ("sbuf", [128, 128], "float32"),
    "e0": ("sbuf", [128, 20], "float32"),
    "eo": ("sbuf", [128, 16], "uint16"),
    "so": ("sbuf", [128, 10], "uint16"),
    "sabs": ("sbuf", [128, 512], "float32"),
    "scol": ("sbuf", [128, 4], "float32"),
    "sg": ("sbuf", [128, 1024], "bfloat16"),
    "keep": ("sbuf", [128, 384], "bfloat16"),
    "ts": ("sbuf", [128, 1024], "bfloat16"),
    "cmp": ("sbuf", [128, 2048], "bfloat16"),
    "junk": ("sbuf", [128, 1024], "float32"),
    "sd": ("sbuf", [128, 4], "float32"),
    "cnt": ("sbuf", [128, 4], "float32"),
    "ru": ("sbuf", [128, 4], "uint16"),
    "w": ("sbuf", [128, 528], "float32"),
    "t1": ("sbuf", [128, 160], "float32"),
    "y": ("sbuf", [128, 20], "float32"),
    "lf": ("sbuf", [128, NONE + 4], "float32"),
    "lown": ("sbuf", [128, 16], "uint16"),
    "xo": ("sbuf", [128, 32], "float32"),
    "to": ("sbuf", [128, 32], "float32"),
    "ou": ("sbuf", [128, 16], "uint16"),
    "oe": ("sbuf", [128, 32], "uint16"),
    "h": ("sbuf", [128, 512], "bfloat16"),
    "ql": ("sbuf", [128, 320], "float8_e4m3fn_x4"),
    "pl": ("sbuf", [128, 320], "uint8"),
    "qr": ("sbuf", [128, 256], "float8_e4m3fn_x4"),
    "pr": ("sbuf", [128, 256], "uint8"),
    "e32": ("sbuf", [128, 2048], "float32"),
    "d": ("sbuf", [128, 256], "float32"),
    "scg": ("sbuf", [128, 64], "float32"),
    "nbg": ("sbuf", [128, 32], "float32"),
    "nbt": ("sbuf", [128, 32], "float32"),
    "ls": ("sbuf", [128, 48], "uint16"),
    "tb": ("sbuf", [128, 520], "bfloat16"),
    "got": ("sbuf", [128, 512], "bfloat16"),
    "tt": ("sbuf", [128, 1024], "bfloat16"),
    "stp": ("sbuf", [128, 128], "float32"),
    "run": ("sbuf", [128, 128], "float32"),
    "zz": ("sbuf", [128, 64], "float32"),
    "ex": ("sbuf", [128, 256], "float32"),
    "tx": ("sbuf", [128, 256], "float32"),
    "x": ("sbuf", [128, 2056], "float32"),
    "off": ("sbuf", [128, 256], "uint16"),
    "ac": ("sbuf", [128, 2048], "float32"),
    "ps": ("psum", [128, 4096], "float32"),
}
ORDER = [("pack", 0), ("pack", "u"), ("scores", 0), ("pack", 1), ("scores", 1), ("pack", 2), ("scores", 2), ("pack", 3), ("scores", 3), ("fill", "turned"),
         ("sizes", 0), ("col", 0), ("sizes", 1), ("col", 1), ("beats", 0, 1), ("beats", 1, 0),
         ("sizes", 2), ("col", 2), ("signs", 0), ("beats", 0, 2), ("beats", 1, 2), ("beats", 2, 0, 2),
         ("sizes", 3), ("col", 3), ("signs", 1), ("beats", 3, 0, 2), ("signs", 2), ("signs", 3),
         ("total", 0), ("total", 1), ("total", 2), ("total", 3),
         ("equals", 0), ("beats", 0, 3), ("equals", 1), ("beats", 1, 3), ("running", 0), ("equals", 2), ("running", 1), ("equals", 3),
         ("place", 0), ("running", 2), ("place", 1), ("running", 3), ("place", 2), ("place", 3)]
ER_FIRST, ER_TABLE = 4, 6
TABLE_V = 10
STORES = (("v", "y", 0, 128), ("s", "y", 128, 352), ("v", "y", 352, 704), ("s", "y", 704, 1152), ("v", "y", 1152, 1600), ("s", "s", 1600, 2048))
SEMAPHORES = ["qv", "qs", "qt", "qp", "lu", "l0", "l1", "l2", "l3", "st", "ll", "lr", "cl", "cr0", "cr1", "cp", "cq", "loc", "rel"]


def rank_program(g, core, T, topo):
    rank = T.rank_of(core)
    if rank is None:
        return
    N = len(T.cores)
    near = [r for r in range(N) if topo.chip(T.cores[r]) == topo.chip(core)]
    far = [r for r in range(N) if r not in near]
    near_others = [r for r in near if r != rank]

    queue = {"v": g.vector, "s": g.scalar, "t": g.tensor, "p": g, "y": g.sync}
    count = {"v": 0, "s": 0, "t": 0, "p": 0, "st": 0}
    seen = {}

    def need(e, deps):
        top = {}
        for sem, val in deps:
            top[sem] = max(val, top.get(sem, 0))
        for sem in top:
            if seen.get((e, sem), 0) < top[sem]:
                queue[e].wait_ge(T.sem[sem], top[sem])
                seen[(e, sem)] = top[sem]

    def op(e, deps, call):
        need(e, deps)
        count[e] += 1
        call().then_inc(T.sem["q" + e], 1)
        return ("q" + e, count[e])

    def load(e, out, in_, sem):
        queue[e].dma_start(out, in_).then_inc(T.sem[sem], 16)
        return (sem, 16)

    def store(e, deps, out, in_):
        need(e, deps)
        queue[e].dma_start(out, in_).then_inc(T.sem["st"], 16)
        count["st"] += 16

    V, S = g.vector, g.scalar

    def bank(b, n):
        return T.ps[:, 512 * b:512 * b + n]

    def blk(t, j, n=1):
        return t[:, 128 * j:128 * (j + n)]

    def vs(deps, out, in0, s1, op0, s2=None, op1=None):
        if op1 is None:
            return op("v", deps, lambda: V.tensor_scalar(out=out, in0=in0, scalar1=s1, scalar2=None, op0=op0))
        return op("v", deps, lambda: V.tensor_scalar(out=out, in0=in0, scalar1=s1, scalar2=s2, op0=op0, op1=op1))

    def vt(deps, out, in0, in1, how):
        return op("v", deps, lambda: V.tensor_tensor(out, in0, in1, how))

    def vc(deps, out, in_):
        return op("v", deps, lambda: V.tensor_copy(out, in_))

    def vm(out, value):
        return op("v", [], lambda: V.memset(out, value))

    def turn(deps, out, in_):
        return op("v", deps, lambda: V.transpose(out, in_))

    def sa(deps, out, in_, scale=1.0, bias=0.0):
        return op("s", deps, lambda: S.activation(out, in_, F.Identity, bias=bias, scale=scale))

    def sc(deps, out, in_):
        return op("s", deps, lambda: S.activation(out, in_, F.Copy))

    spare, made = {}, {}

    def fill(*names):
        for name in names:
            made[name] = spare.pop(name)()

    lu = load("s", T.uc[:, 0:16], T.u[:, 0:16], "lu")
    lg = [load("y", blk(T.grt, 4 * q, 4), blk(T.gr, 4 * q, 4), "l%d" % q) for q in range(4)]

    def whole(out, pattern, base=0, step=0):
        return op("p", [], lambda: g.iota(out, pattern, base, step, allow_small_or_imprecise_dtypes=True))
    k_ones = vm(blk(T.keep, 0), 1.0)
    k_et = vm(T.et[:, :], 0.0)

    def diagonal(deps, out, how, other):
        return op("p", deps, lambda: g.affine_select(out, blk(T.keep, 0), [[-1, 128]], how, other, 0, 1))
    k_e = diagonal([k_ones, k_et], T.et[:, 3:515:4], A.is_equal, 0.0)
    whole(T.cw[:, 0:32], [[0, 8], [1, 4]])
    whole(T.cw[:, 32:64], [[0, 2], [2, 4], [0, 4]])
    for h, base, step in ((0, 3, -2), (1, 0, 3)):
        whole(T.cw[:, 64 + 16 * h:80 + 16 * h], [[1, 2], [step, 2], [8, 4]], base)
        whole(T.cw[:, 96 + 16 * h:112 + 16 * h], [[0, 4], [1, 2], [step, 2]], base)
    whole(T.cw[:, 128:160], [[16, 2], [0, 16]], 0, 1)
    whole(T.cw[:, 160:192], [[-16, 2], [0, 4], [16, 4]], 0, -1)
    k_cw = whole(T.cw[:, 192:224], [[0, 32]], 0, -4)
    c_b, c_k2, c_at, c_pb, c_g16, c_gap, c_base = [T.ck[:, 32 * i:32 * i + 1] for i in range(7)]
    k_kp = diagonal([], blk(T.keep, 1), A.not_equal, -1.0)
    k_jt = whole(T.jt[:, :], [[128, 4], [1, 16]], 0, 1)
    whole(T.e0[:, 0:8], [[8, 2], [1, 2], [0, 2]], 16)
    whole(T.e0[:, 8:16], [[1, 4], [0, 2]])
    k_e0 = whole(T.e0[:, 16:20], [[32, 4]])
    k_v0 = whole(T.val[:, 64:128], [[1, 4], [4, 16]], 2)
    k_tb = sa([k_et, k_e], T.tb[:, :], T.et[:, :], 0.0, float(EMPTY))

    k_keep = vm(blk(T.keep, 2), 1.0)
    k_w = vm(T.w[:, 0:96], 0.0)
    k_none = vm(T.lf[:, NONE:NONE + 4], 512.0)
    pad = 256 * (rank % 2)
    chosen = T.h[:, 256 - pad:512 - pad]
    k_h0 = vm(T.h[:, pad:pad + 256], 0.0)
    k_x0 = vm(T.x[:, 0:8], 0.0)
    vm(T.stp[:, 0:128:4], 4.0 * EMPTY)
    vm(T.stp[:, 1:128:4], 0.0)
    k_stp = vm(T.stp[:, 2:128:4], 0.0)
    k_eq = [op("v", [k_e], lambda: V.quantize_mx(blk(T.eq, b), blk(T.es, b), T.et[:, 3 - b:515 - b])) for b in range(4)]

    def cc(i, n=1):
        return T.cc[:, i:i + n]
    small = {}

    def scalar_constants():
        k = [made["turned"], k_e0]
        sa(k, cc(0), c_at, 1.0, 32.0)
        j = sa(k, cc(4), c_g16, 4.0, c_base)
        small["s"] = sa(k, cc(1), c_k2, 4.0, c_pb)
        small["val"] = sa([j, k_v0], T.val[:, 0:64], T.val[:, 64:128], 1.0, cc(4))
    spare.update({
        "turned": lambda: turn([k_cw], T.ck[:, :], T.cw[:, :]),
        "xo": lambda: vs([made["turned"]], T.so[:, 4:6], T.ck[:, 0:2], -8.0, A.mult, c_at, A.add),
        "before": lambda: vs([k_e0, made["turned"]], T.eo[:, 0:8], T.e0[:, 0:8], c_k2, A.add),
        "last": lambda: vs([k_e0, made["turned"]], T.eo[:, 8:16], T.e0[:, 8:16], c_k2, A.add, c_k2, A.add),
        "nb": lambda: vs([small["s"]], T.so[:, 6:8], T.e0[:, 16:18], cc(1), A.add),
        "early": lambda: vs([k_e0, made["turned"]], cc(2, 2), T.e0[:, 16:19:2], c_gap, A.add, 0.0, A.is_le),
        "step": lambda: vs([made["turned"], k_stp], T.stp[:, 3:128:4], T.stp[:, 2:128:4], c_base, A.subtract),
        "lown": lambda: vc([made["turned"]], T.so[:, 8:9], c_pb),
        "group": lambda: vs([made["turned"]], T.so[:, 2:3], c_g16, 0.5, A.mult, c_pb, A.add),
        "sel0": lambda: vs([made["early"]], T.so[:, 0:1], cc(2), float(NONE), A.mult, c_at, A.max),
        "sel1": lambda: vs([made["early"], small["s"]], T.so[:, 1:2], cc(3), float(NONE), A.mult, cc(0), A.max),
    })

    k_ut = [vs([lu, k_ones], T.ut[:, b:512:4], blk(T.keep, 0), T.uc[:, b:b + 1], A.mult) for b in (0, 1)]
    k_ut += [sa([lu, k_ones], T.ut[:, b:512:4], blk(T.keep, 0), 0.0, T.uc[:, b:b + 1]) for b in (2, 3)]
    sc(lg[0:1], T.e32[:, 0:512], T.grt[:, 0:512])

    k_q, k_abs, k_scol, k_sc, k_row = {}, {}, {}, {}, {}

    def pack(q):
        if q == "u":
            k_q[q] = op("v", k_ut, lambda: V.quantize_mx(T.uq[:, :], T.us[:, :], T.ut[:, :]))
        else:
            k_q[q] = op("v", [lg[q]], lambda: V.quantize_mx(blk(T.gq, q), blk(T.gs, q), blk(T.grt, 4 * q, 4)))

    def scores(q):
        k_row[q] = op("t", [k_q["u"], k_q[q]], lambda: g.tensor.matmul_mx(bank(4 + q, 128), T.uq[:, :], T.us[:, :], blk(T.gq, q), blk(T.gs, q), True, True))
        k_sc[q] = op("t", [k_q["u"], k_q[q]], lambda: g.tensor.matmul_mx(bank(q, 128), blk(T.gq, q), blk(T.gs, q), T.uq[:, :], T.us[:, :], True, True))

    def sizes(q):
        k_abs[q] = op("s", [k_row[q]], lambda: S.activation(blk(T.sabs, q), bank(4 + q, 128), F.Abs))

    def column_score(q):
        k_scol[q] = op("s", [k_sc[q]], lambda: S.activation(T.scol[:, q:q + 1], bank(q, 1), F.Abs))
    k_b, k_sg, k_cnt, k_ts, k_ru = {q: {} for q in range(4)}, {}, {}, {}, []

    def beats(q, j, n=1):
        at = 4 * q + j - (j > q)
        k = vs([k_abs[i] for i in range(j, j + n)] + [k_scol[q]], blk(T.cmp, at, n), blk(T.sabs, j, n), T.scol[:, q:q + 1], A.is_ge if j < q else A.is_gt, 0.5, A.add)
        for i in range(n):
            k_b[q][at + i - 4 * q] = k

    def signs(q):
        j, n = (q, 1) if q < 2 else (2, 2)
        k_sg[q] = op("s", [k_abs[j], k_abs[j + n - 1], k_scol[q]], lambda: S.activation(
            blk(T.sg, 2 * q, n), blk(T.sabs, j, n), F.Sign, bias=T.scol[:, q:q + 1], scale=-1.0, accum_out=T.sd[:, q:q + 1]))

    def equals(q):
        n = 1 if q < 2 else 2
        k_b[q][3] = k_b[q][4 - n] = vs([k_sg[q]], blk(T.cmp, 4 * q + 4 - n, n), blk(T.sg, 2 * q, n), 0.0, A.is_equal, 0.5, A.mult)

    def total(q):
        k_cnt[q] = op("s", [k_b[q][0], k_b[q][1], k_sg[q]], lambda: S.activation(
            blk(T.junk, 2 * q, 2), blk(T.cmp, 4 * q, 2), F.Identity, bias=T.sd[:, q:q + 1], scale=-512.0, accum_out=T.cnt[:, q:q + 1]))

    def running(q):
        k_ts[q] = op("v", [k_b[q][2], k_b[q][3], k_kp, k_keep], lambda: V.tensor_tensor_scan(blk(T.ts, 2 * q, 2), blk(T.keep, int(q == 2), 2), blk(T.cmp, 4 * q + 2, 2), -128.0 if q < 2 else 0.0, A.mult, A.add))

    def place(q):
        k_ru.append(vs([k_ts[q], k_cnt[q]], T.ru[:, q:q + 1], T.cnt[:, q:q + 1], -1.0 / 512, A.mult, T.ts[:, 256 * q + 255:256 * q + 256], A.subtract))

    steps = {"pack": pack, "scores": scores, "sizes": sizes, "col": column_score, "beats": beats, "signs": signs, "equals": equals, "total": total,
             "running": running, "place": place, "fill": fill}
    for step in ORDER:
        steps[step[0]](*step[1:])
    k_abs, k_scol = list(k_abs.values()), list(k_scol.values())

    scalar_constants()
    k_wide = sc(lg, T.e32[:, 512:2048], T.grt[:, 512:2048])

    k = vc([k_w, k_jt] + k_ru, T.w[:, 16:528].indirect(T.ru[:, 0:4]), T.jt[:, 0:64])
    fill("xo")
    k = [turn([k], T.t1[:, 0:96], T.w[:, 0:96]), turn([k], T.t1[:, 96:160], T.w[:, 16:80])]
    fill("early")
    k = vt(k, T.y[0:64, 0:10], T.t1[0:64, 0:160:16], T.t1[64:128, 0:160:16], A.add)
    k = [vt([k], T.y[a:a + 32, 10:20], T.y[a:a + 32, 0:10], T.y[32 - a:64 - a, 0:10], A.add) for a in (0, 32)]
    own = T.lf[:, 8 * rank:8 * rank + LW]
    k_lo = [vt(k, T.lf[a:a + 64, 8 * rank:8 * rank + LW], T.y[0:64, 10:20:2], T.y[0:64, 11:20:2], A.add) for a in (0, 64)]
    fill("sel0")

    far_e = topo.engines(core, T.cores[far[0]])
    near_e = [e for e in topo.engines(core, T.cores[near_others[0]]) if e not in far_e]
    far_mask = sum(1 << e for e in far_e)
    near_mask = sum(1 << e for e in near_e)
    left = ("loc", 5 * (len(far_e) + len(near_e)))

    def ids(ranks):
        return [DstId(rid=topo.addr(T.cores[r])[0], pnc=topo.addr(T.cores[r])[1]) for r in ranks]

    def near_at(r, q=rank):
        i, j = near.index(q), near.index(r)
        return 64 * (i + (i > j or i == j and r % 2 == 0))

    def send(deps, src, near_dst, far_dst, near_sem, far_sem, far=far):
        need("p", deps)
        g.remote_dma_fused([
            RemoteDMATransfer(dst_ids=ids(far), dma_engine_mask=far_mask, remote_sem=T.sem[far_sem], srcs=[src], dsts=[far_dst(r) for r in far]),
            RemoteDMATransfer(dst_ids=ids(near_others), dma_engine_mask=near_mask, remote_sem=T.sem[near_sem], srcs=[src], dsts=[near_dst(r) for r in near_others]),
        ], local_sem=T.sem["loc"])

    def write(deps, src, ranks, dsts, mask, sem):
        need("p", deps)
        g.remote_dma_fused([RemoteDMATransfer(dst_ids=ids(ranks), dma_engine_mask=mask, remote_sem=T.sem[sem], srcs=[src], dsts=dsts)], local_sem=T.sem["loc"])

    send(k_lo, own, lambda r: own, lambda r: own, "ll", "lr")
    lists = k_lo + [("ll", len(near_others) * len(near_e)), ("lr", len(far) * len(far_e)), k_none]

    k = vc(k_lo + [made["xo"]], T.xo[:, :], own.indirect(T.so[:, 4:6]))
    fill("sel1")
    k = turn([k], T.to[:, :], T.xo[:, :])
    fill("lown")
    k_ou = vs([k], T.ou[:, :], T.to[:, 0:16], 4.0, A.mult, c_b, A.add)
    k_oe = vs([k], T.oe[:, 0:32:2], T.to[:, 0:16], 4.0, A.mult, c_b, A.add)
    k_h = [vc([k_ou] + lg, chosen, T.grt[:, 0:2048].indirect(T.ou[:, 0:16]))]
    fill("last")
    mine = near_at(rank)
    tile = mine - 64 + pad // 4
    k_hq = op("v", k_h + [k_h0], lambda: V.quantize_mx(T.ql[:, tile:tile + 128], T.pl[:, tile:tile + 128], T.h[:, 0:512]))
    k_lown = vc(k_lo + [made["lown"]], T.lown[:, :], own.indirect(T.so[:, 8:9]))
    fill("group", "before", "nb", "step")

    fa = 64 * near.index(rank)
    partner = far[near.index(rank)]

    def codes(t, a):
        return t[:, a:a + 64].bitcast(dt.uint8)

    def to_far():
        write([k_hq], codes(T.ql, mine), [partner], [codes(T.qr, fa)], far_mask, "cp")
        write([k_hq], T.pl[:, mine:mine + 64], [partner], [T.pr[:, fa:fa + 64]], far_mask, "cq")

    def to_near():
        write([k_hq], codes(T.ql, mine), near_others, [codes(T.ql, near_at(r)) for r in near_others], near_mask, "cl")
        write([k_hq], T.pl[:, mine:mine + 64], near_others, [T.pl[:, near_at(r):near_at(r) + 64] for r in near_others], near_mask, "cl")
    for call in (to_far, to_near) if fa < 128 else (to_near, to_far):
        call()
    cl = ("cl", 2 * len(near_others) * len(near_e))
    cp = [("cp", len(far_e)), ("cq", len(far_e))]
    for arrived, piece in zip(cp, (codes(T.qr, fa), T.pr[:, fa:fa + 64])):
        write([arrived], piece, near_others, [piece] * len(near_others), far_mask + near_mask, "cr%d" % (fa // 128))
    g.sem_inc(T.sem["rel"], 1)
    each = 2 * (len(far_e) + len(near_e))
    cr = [cp + [("cr%d" % i, each)] if fa // 128 == i else [("cr%d" % i, 2 * each)] for i in range(2)]

    def unpack(b, to, q, s, a, n, deps):
        return op("t", deps + [k_eq[b]], lambda: g.tensor.matmul_mx(bank(to, n), blk(T.eq, b), blk(T.es, b), q[:, a:a + n], s[:, a:a + n], True, True))

    def xs(r, b, n):
        return T.x[:, 8 + 256 * r + b:8 + 256 * (r + n):4]
    k_own = [unpack(b, 4 + b, T.ql, T.pl, tile, 128, [k_hq] + k_scol + k_abs) for b in range(4)]
    at = 2048 + mine - tile
    k_d = [vt([k_own[b]] + k_h, T.d[:, b:256:4], T.h[:, 256 - pad + b:512 - pad:4], T.ps[:, at + 512 * b:at + 512 * b + 64], A.subtract) for b in range(4)]
    er_at = [0]

    def put_er(n=1):
        a = er_at[0]
        er_at[0] += n
        at = T.ou[:, a:a + n] if n > 1 else T.oe[:, 2 * a:2 * a + 1]
        made["er"] = vc(k_d + [k_wide, k_ou, k_oe, made["er"]], T.e32[:, 0:2048].indirect(at), T.d[:, 16 * a:16 * (a + n)])
        if er_at[0] == 16:
            store("y", [made["er"], ("rel", 1)], T.er[:, :], T.e32[:, :])
    made["er"] = k_ou

    store("y", [sc([k_lown] + k_abs, T.scg[:, :], T.sabs[:, 0:512].indirect(T.lown[:, 0:4]))], T.sc[:, :], T.scg[0:1, :])

    table = T.tb[:, 0:520]
    k_ls = vc(lists + [made["group"], made["sel0"], made["sel1"]], T.ls[:, :], T.lf[:, :].indirect(T.so[:, 0:3]))
    put_er(ER_FIRST)
    k_tab = vc([k_ls, k_tb, small["val"]], table.indirect(T.ls[:, 32:36]), T.val[:, 0:64])
    put_er(ER_TABLE)
    n = 16 * TABLE_V
    k_got = [sc([k_tab], T.got[:, n:512], table.indirect(T.ls[:, TABLE_V:32])),
             vc([k_tab], T.got[:, 0:n], table.indirect(T.ls[:, 0:TABLE_V]))]
    k = [turn([k_tab], blk(T.tt, c), T.tb[:, c:512:4]) for c in range(4)]
    k += [turn(k_got[1:], T.tt[:, 512:512 + n], T.got[:, 0:n]), turn(k_got[:1], T.tt[:, 512 + n:1024], T.got[:, n:512])]
    put_er()
    k = op("v", k + [made["step"]], lambda: V.tensor_tensor_scan(T.run[:, :], T.stp[:, :], T.tt[:, 0:1024:8], 0.0, A.add, A.max))
    put_er()
    k = vt([k], T.zz[0:64, 32:64], T.run[0:64, 3:128:4], T.run[64:128, 3:128:4], A.max)
    k_zz = [vt([k], T.zz[a:a + 32, 0:32], T.zz[0:32, 32:64], T.zz[32:64, 32:64], A.max) for a in (0, 32, 64, 96)]

    found = T.zz[:, 0:32]
    k_ready = {}

    def products(to, q, s, a, n, deps):
        return [unpack(b, to + b, q, s, a, n, deps) for b in range(4)]

    def copies(k, to, at, ranks, by=(sc, sc, sc, sc)):
        done = [by[b]([k[b]], xs(ranks[0], b, len(ranks)), T.ps[:, 512 * (to + b) + at:512 * (to + b) + at + 64 * len(ranks)]) for b in range(4)]
        k_ready.update({r: done for r in ranks})
        return done

    def pair(i, deps):
        r = 2 * i
        if r in near:
            return products(4 * (i % 2), T.ql, T.pl, near_at(rank, r), 128, deps + [cl, k_hq])
        return products(4 * (i % 2), T.qr, T.pr, 64 * far.index(r), 128, deps + cr[far.index(r) // 2])

    def offsets(deps, a, b):
        return vs(deps, T.off[:, a:b], T.tx[:, a:b], 4.0, A.mult, c_b, A.add)
    k_ex = vc(k_zz + [made["before"]], T.ex[:, 0:64], found.indirect(T.eo[:, 0:4]))
    put_er()
    k = turn([k_ex], T.tx[:, 0:64], T.ex[:, 0:64])
    put_er()
    k_off = offsets([k], 16, 64)
    put_er()
    k0, k1 = pair(0, k_abs + k_scol), pair(1, k_d)
    k2 = pair(2, copies(k0, 0, 0, [0, 1]))
    copies(k1, 4, 0, [2])
    k_ex2 = k_ex3 = sc(k_zz + [made["before"], made["last"]], T.ex[:, 64:256], found.indirect(T.eo[:, 4:16]))
    k3 = pair(3, copies(k1, 4, 64, [3]))
    copies(k2, 0, 0, [4, 5])
    copies(k3, 4, 0, [6, 7])
    k_nb = sc(lists + [made["nb"]], T.nbg[:, :], T.lf[:, :].indirect(T.so[:, 6:8]))

    spare.update({
        "ers": put_er,
        "t1": lambda: turn([k_ex2], T.tx[:, 64:128], T.ex[:, 64:128]),
        "o1": lambda: offsets([made["t1"]], 64, 128),
        "t2": lambda: turn([k_ex3], T.tx[:, 128:256], T.ex[:, 128:256]),
        "o2": lambda: offsets([made["t2"]], 128, 256),
        "nbs": lambda: store("y", [turn([k_nb], T.nbt[:, :], T.nbg[:, :])], T.nb[:, :], T.nbt[0:32, 0:16]),
    })

    k = k_x0
    for s in range(1, N):
        a = 8 + 256 * s
        k = vt([k, k_off if s < 4 else made["o1"]] + k_ready[s] + k_ready[0], T.x[:, a:a + 256], T.x[:, 0:a].indirect(T.off[:, 16 * s:16 * s + 16]), T.x[:, a:a + 256], A.add)
        fill(*list(spare)[:1])
    for e, y, a, b in STORES:
        out, src = T.ac[:, a:b], T.x[:, 0:2056].indirect(T.off[:, 128 + a // 16:128 + b // 16])
        store(y, [(vc if e == "v" else sc)([k, made["o2"]], out, src)], T.acc[:, a:b], out)

    need("p", [("q" + e, count[e]) for e in "vstp"] + [("st", count["st"]), left])
